import numpy as np
import ml_dtypes


def mxq(x, axis, fmt="e4m3"):
    dtype, down = {"e4m3": (ml_dtypes.float8_e4m3fn, 7), "e5m2": (ml_dtypes.float8_e5m2, 14)}[fmt]
    v = np.moveaxis(np.asarray(x, np.float32).astype(ml_dtypes.bfloat16).astype(np.float64), axis, -1)
    blocks = v.reshape(v.shape[:-1] + (-1, 32))
    amax = np.abs(blocks).max(-1, keepdims=True)
    byte = np.maximum(np.where(amax > 0, np.frexp(amax)[1] - 1 + 127, 0) - down, 1)
    scale = np.exp2(byte - 127.0)
    codes = (blocks / scale).astype(np.float32).astype(dtype).astype(np.float64)
    return np.moveaxis((codes * scale).reshape(v.shape), -1, axis)


WIDE = False


def mx_kscale(k):
    if not WIDE:
        return np.ones(k)
    levels = np.array([10, -10, 5, -5, 0])
    if k % 512:
        return np.exp2(np.random.permutation(np.resize(levels, k // 32))).repeat(32)
    a = np.empty((k // 512, 16))
    for p in range(k // 512):
        a[p, :8] = np.random.permutation(np.resize(levels, 8))
        for g in range(8):
            far = levels[np.abs(levels - a[p, g]) >= 10]
            a[p, g + 8] = far[np.random.randint(len(far))]
    return np.exp2(a.ravel()).repeat(32)


def f64(x):
    return np.asarray(x).astype(np.float64)


def striped(idx):
    return np.tile(idx.reshape(-1, 16).T, (8, 1)).astype(np.uint16)


def unstriped(offs):
    return offs[:16].T.reshape(-1).astype(np.int64)


E2M1 = np.array([0.0, 0.5, 1.0, 1.5, 2.0, 3.0, 4.0, 6.0, -0.0, -0.5, -1.0, -1.5, -2.0, -3.0, -4.0, -6.0])


def pack_fp4(w):
    k, n = w.shape
    w = f64(np.asarray(w, np.float32).astype(ml_dtypes.bfloat16)).reshape(k // 32, 32, n)
    amax = np.abs(w).max(1)
    mant, ex = np.frexp(amax / 6.0)
    byte = np.clip(np.where(amax > 0, np.where(mant > 0.5, ex, ex - 1) + 127, 1), 1, 254)
    scaled = (w * np.exp2(127.0 - byte)[:, None, :]).reshape(k, n).astype(np.float32)
    c = np.ascontiguousarray(scaled.reshape(k // 512, 128, 4, n).transpose(0, 1, 3, 2)).astype(ml_dtypes.float4_e2m1fn).view(np.uint8) & 0xF
    words = (c[..., 0::2] | (c[..., 1::2] << 4)).reshape(k // 512, 128, 2 * n)
    return np.ascontiguousarray(words), np.ascontiguousarray(byte.astype(np.uint8).reshape(k // 512, 16, n))


def unpack_fp4(words, scales):
    g, _, n = scales.shape
    words = np.ascontiguousarray(words).reshape(g, 128, n, 2)
    nib = np.empty((g, 128, n, 4), np.uint8)
    nib[..., 0::2] = words & 0xF
    nib[..., 1::2] = words >> 4
    vals = E2M1[nib] * np.repeat(np.exp2(scales.astype(np.float64) - 127.0), 8, axis=1)[..., None]
    return vals.transpose(0, 1, 3, 2).reshape(g * 512, n)


def relu(v):
    return np.maximum(v, 0.0)


K, T, S, H, N, U, V = 1024, 2048, 1024, 512, 128, 1024, 512


def setup_inputs():
    n = np.random.standard_normal
    s = mx_kscale(K)[:, None]
    u = mx_kscale(H)
    packed_xT = pack_fp4(n((K, T)) * s)
    return {
        "x_words": packed_xT[0],
        "x_scales": packed_xT[1],
        "w1": (n((K, H)) / np.sqrt(K) / s * u).astype(np.float32),
        "w2": (n((K, H)) / np.sqrt(K) / s * u).astype(np.float32),
        "w3": (n((H, N)) / np.sqrt(H) / u[:, None]).astype(np.float32),
        "offs": striped(np.random.permutation(T)[:S]),
        "near": striped(np.random.permutation(U)[:V]),
        "far": striped(np.random.permutation(U)[:V]),
    }


def reference(x_words, x_scales, w1, w2, w3, offs, near, far):
    xq = unpack_fp4(x_words, x_scales)[:, unstriped(offs)]
    a = np.zeros((H, S))
    a[:, unstriped(near)] = relu(mxq(f64(w1), 0, "e4m3").T @ xq[:, :V])
    e = np.zeros((H, S))
    e[:, unstriped(far)] = relu(mxq(f64(w2), 0, "e4m3").T @ xq[:, V:2 * V])
    z = np.maximum(a, e)
    return mxq(f64(w3), 0, "e4m3").T @ mxq(z, 0, "e4m3")

@@ -1,0 +1,199 @@
+from contextlib import ExitStack
+
+import concourse.mybir as mybir
+
+K, T, S, H, N, V = 1024, 2048, 1024, 512, 128, 512
+FLOPS = 2 * K * H * V * 2 + 2 * H * N * S
+
+F32 = mybir.dt.float32
+BF16 = mybir.dt.bfloat16
+I32 = mybir.dt.int32
+U32 = mybir.dt.uint32
+U16 = mybir.dt.uint16
+U8 = mybir.dt.uint8
+FP8X4 = mybir.dt.float8_e4m3fn_x4
+FP4X4 = mybir.dt.float4_e2m1fn_x4
+RELU = mybir.ActivationFunctionType.Relu
+MAX = mybir.AluOpType.max
+
+P = 128
+PACK = 4
+PASSES = K // (P * PACK)
+CHUNK = 256
+
+
+def tile_picked_bev_max_p_kernel(
+    tc, x_words, x_scales, w1, w2, w3, offs, near, far, out
+):
+    nc = tc.nc
+    with ExitStack() as ctx:
+        keep = ctx.enter_context(tc.tile_pool(name="keep", bufs=1))
+        head = ctx.enter_context(tc.tile_pool(name="head", bufs=1))
+        psum = ctx.enter_context(tc.psum_pool(name="psum", bufs=4))
+
+        offs_sb = keep.tile([P, S // 16], U16, name="offs_sb")
+        near_sb = keep.tile([P, V // 16], U16, name="near_sb")
+        far_sb = keep.tile([P, V // 16], U16, name="far_sb")
+        store_scales = head.tile([P, T], U8, name="store_scales", align_bytes=64, offset=1024)
+        picked_scales = keep.tile([P, S], U8, name="picked_scales", align_bytes=64)
+        moved_scales = keep.tile([P, S], U8, name="moved_scales", align_bytes=64)
+        store_words = [keep.tile([P, T], U16, name=f"store_words{z}", align_bytes=64) for z in range(PASSES)]
+        raw = [[keep.tile([P, PACK, H], F32, name=f"raw0{z}") for z in range(PASSES)]]
+        near_maps = [keep.tile([P, 2 * S], F32, name=f"near_map{b}", align_bytes=64) for b in range(3)]
+        far_map = keep.tile([P, 2 * S], F32, name="far_map", align_bytes=64)
+        joined = keep.tile([P, PACK, S], BF16, name="joined")
+
+        nc.vector.memset(store_scales[:].bitcast(I32), 0)
+        nc.sync.dma_start(offs_sb[:], offs)
+        nc.sync.dma_start(store_words[0][:].bitcast(I32), x_words[0].bitcast(I32))
+        for q in range(4):
+            nc.sync.dma_start(
+                store_scales[32 * q : 32 * q + 8, :].bitcast(I32), x_scales[:, 4 * q : 4 * q + 4, :].bitcast(I32)
+            )
+        nc.sync.dma_start(store_words[1][:].bitcast(I32), x_words[1].bitcast(I32))
+        for z in range(PASSES):
+            nc.sync.dma_start(raw[0][z][:], w1[512 * z : 512 * (z + 1), :].rearrange("(p j) c -> p j c", j=PACK))
+        nc.sync.dma_start(near_sb[:], near)
+        nc.sync.dma_start(far_sb[:], far)
+
+        nc.vector.memset(moved_scales[:].bitcast(I32), 0)
+        nc.vector.memset(near_maps[0][:, :S].bitcast(I32), 0)
+        for cell_map in near_maps[1:] + [far_map]:
+            nc.scalar.copy(cell_map[:, :S], near_maps[0][:, :S])
+
+        nc.vector.tensor_copy(picked_scales[:], store_scales[:].indirect(offs_sb[:]))
+        nc.sync.dma_start(moved_scales[0:100, :].bitcast(I32), picked_scales[4:104, :].bitcast(I32))
+        raw_w2 = head.tile([P, PASSES, PACK, H], F32, name="raw_w2", align_bytes=64, offset=2048)
+        raw.append([raw_w2[:, z] for z in range(PASSES)])
+        for z in range(PASSES):
+            nc.sync.dma_start(raw[1][z], w2[512 * z : 512 * (z + 1), :].rearrange("(p j) c -> p j c", j=PACK))
+        x_planes = [picked_scales, moved_scales]
+        picked_words = {}
+        staged = {}
+        weights = {}
+        sums = {}
+        results = {}
+
+        def pick(s, z, home):
+            picked_words[s, z] = home
+            nc.vector.tensor_copy(home, store_words[z][:].indirect(offs_sb[:, 32 * s : 32 * (s + 1)]))
+
+        def spare(cell_map, place):
+            return cell_map[:, S + 256 * place : S + 256 * (place + 1)].bitcast(BF16)
+
+        def cast(key, source, home):
+            if home is None:
+                own = keep.tile([P, P * PACK], BF16, name=f"staged{key}", align_bytes=64)
+                home = own[:]
+            staged[key] = home
+            nc.scalar.copy(home.rearrange("p (g q j) -> p g q j", q=8, j=PACK), source)
+
+        def cast_w(s, z, t, home=None):
+            cast(f"{s}{z}{t}", raw[s][z][:].rearrange("p j (g t q) -> p t g q j", t=PACK, q=8)[:, t], home)
+
+        def quantize(key):
+            codes = keep.tile([P, P], U32, name=f"codes{key}", align_bytes=64)
+            plane = keep.tile([P, P], U8, name=f"plane{key}", align_bytes=64)
+            nc.vector.quantize_mx(out=codes[:].bitcast(FP8X4), scales=plane[:], in_=staged[key])
+            weights[key] = (codes, plane)
+
+        def multiply(s, t):
+            acc = psum.tile([P, V], F32, name="acc")
+            sums[s, t] = acc
+            for z in range(PASSES):
+                codes, plane = weights[f"{s}{z}{t}"]
+                nc.tensor.matmul_mx(
+                    out=acc[:],
+                    lhsT=codes[:].bitcast(FP8X4),
+                    lhsT_scale=plane[:],
+                    rhs=picked_words[s, z].bitcast(FP4X4),
+                    rhs_scale=x_planes[z][:, V * s : V * (s + 1)],
+                    start=(z == 0),
+                    stop=(z == PASSES - 1),
+                )
+
+        def prepare(s, t, homes=(None, None)):
+            for z in range(PASSES):
+                if f"{s}{z}{t}" not in staged:
+                    cast_w(s, z, t, homes[z])
+                    quantize(f"{s}{z}{t}")
+            multiply(s, t)
+
+        def rectify(s, t):
+            results[s, t] = keep.tile([P, V], F32, name=f"result{s}{t}")
+            nc.scalar.activation(results[s, t][:], sums[s, t][:], RELU)
+
+        def put_near(t):
+            nc.vector.tensor_copy(near_maps[t % 3][:].indirect(near_sb[:]), results[0, t][:])
+
+        def put_far(t):
+            nc.vector.tensor_copy(far_map[:].indirect(far_sb[:]), results[1, t][:])
+            nc.vector.tensor_tensor(joined[:, t, :], near_maps[t % 3][:, :S], far_map[:, :S], MAX)
+
+        first_words = keep.tile([P, V], U16, name="first_words", align_bytes=64)
+        middle_words = head.tile([P, 2, V], U16, name="middle_words", align_bytes=64, offset=0)
+        pick(0, 0, first_words[:])
+        pick(0, 1, middle_words[:, 0, :])
+        pick(1, 0, middle_words[:, 1, :])
+        for t in range(3):
+            cast_w(0, 0, t)
+            quantize(f"00{t}")
+        prepare(0, 0)
+        last_words = keep.tile([P, V], U16, name="last_words", tag="staged010", align_bytes=64)
+        pick(1, 1, last_words[:])
+        prepare(0, 1, (None, spare(near_maps[0], 0)))
+        rectify(0, 0)
+        put_near(0)
+        prepare(0, 2, (None, spare(near_maps[1], 0)))
+        rectify(0, 1)
+        prepare(0, 3, (spare(near_maps[1], 1), spare(near_maps[1], 2)))
+        put_near(1)
+        prepare(1, 0, (spare(near_maps[2], 0), spare(near_maps[2], 1)))
+        rectify(0, 2)
+        prepare(1, 1, (spare(near_maps[2], 2), spare(near_maps[2], 3)))
+        rectify(0, 3)
+        put_near(2)
+        prepare(1, 2, (spare(far_map, 0), spare(far_map, 1)))
+        rectify(1, 0)
+        prepare(1, 3, (spare(far_map, 2), spare(far_map, 3)))
+        rectify(1, 1)
+        put_far(0)
+        put_near(3)
+        rectify(1, 2)
+        rectify(1, 3)
+        for t in range(1, PACK):
+            put_far(t)
+
+        raw3 = keep.tile([P, PACK, N], F32, name="raw3", tag="raw00")
+        w3_slots = w3.rearrange("(g t q) n -> t g q n", t=PACK, q=8)
+        for t in range(PACK):
+            nc.sync.dma_start(raw3[:, t, :], w3_slots[t])
+        cast("w3", raw3[:].rearrange("p t (g q) -> p g q t", q=8), None)
+        quantize("w3")
+        codes3, plane3 = weights["w3"]
+
+        for c in range(S // CHUNK):
+            cols = slice(c * CHUNK, (c + 1) * CHUNK)
+            woven = keep.tile([P, CHUNK * PACK], BF16, name=f"woven{c}", align_bytes=64)
+            dst = woven[:].rearrange("p (c i t) -> p c t i", i=4, t=PACK)
+            src = joined[:, :, cols].rearrange("p t (c i) -> p c t i", i=4)
+            if c in (0, 3):
+                nc.scalar.copy(dst, src)
+            else:
+                nc.vector.tensor_copy(dst, src)
+            z_codes = keep.tile([P, CHUNK], U32, name=f"z_codes{c}", align_bytes=64)
+            z_plane = keep.tile([P, CHUNK], U8, name=f"z_plane{c}", align_bytes=64)
+            nc.vector.quantize_mx(out=z_codes[:].bitcast(FP8X4), scales=z_plane[:], in_=woven[:])
+            total = psum.tile([P, CHUNK], F32, name="total")
+            nc.tensor.matmul_mx(
+                out=total[:],
+                lhsT=codes3[:].bitcast(FP8X4),
+                lhsT_scale=plane3[:],
+                rhs=z_codes[:].bitcast(FP8X4),
+                rhs_scale=z_plane[:],
+                start=True,
+                stop=True,
+            )
+            leaving = keep.tile([P, CHUNK], F32, name=f"leaving{c}")
+            nc.scalar.copy(leaving[:], total[:])
+            nc.sync.dma_start(out[:, cols], leaving[:])

@@ -15,11 +15,15 @@ FP8X4 = mybir.dt.float8_e4m3fn_x4
 FP4X4 = mybir.dt.float4_e2m1fn_x4
 RELU = mybir.ActivationFunctionType.Relu
 MAX = mybir.AluOpType.max
+ADD = mybir.AluOpType.add
+SUBTRACT = mybir.AluOpType.subtract
 
 P = 128
 PACK = 4
 PASSES = K // (P * PACK)
+BLOCK = P * PACK
 CHUNK = 256
+NEAR, FAR = 0, 1
 
 
 def tile_picked_bev_max_p_kernel(
@@ -29,171 +33,193 @@ def tile_picked_bev_max_p_kernel(
     with ExitStack() as ctx:
         keep = ctx.enter_context(tc.tile_pool(name="keep", bufs=1))
         head = ctx.enter_context(tc.tile_pool(name="head", bufs=1))
+        mid = ctx.enter_context(tc.tile_pool(name="mid", bufs=1))
         psum = ctx.enter_context(tc.psum_pool(name="psum", bufs=4))
 
         offs_sb = keep.tile([P, S // 16], U16, name="offs_sb")
         near_sb = keep.tile([P, V // 16], U16, name="near_sb")
         far_sb = keep.tile([P, V // 16], U16, name="far_sb")
-        store_scales = head.tile([P, T], U8, name="store_scales", align_bytes=64, offset=1024)
+        store_scales = head.tile([P, T], U8, name="store_scales", align_bytes=64, offset=2048)
         picked_scales = keep.tile([P, S], U8, name="picked_scales", align_bytes=64)
         moved_scales = keep.tile([P, S], U8, name="moved_scales", align_bytes=64)
         store_words = [keep.tile([P, T], U16, name=f"store_words{z}", align_bytes=64) for z in range(PASSES)]
-        raw = [[keep.tile([P, PACK, H], F32, name=f"raw0{z}") for z in range(PASSES)]]
-        near_maps = [keep.tile([P, 2 * S], F32, name=f"near_map{b}", align_bytes=64) for b in range(3)]
-        far_map = keep.tile([P, 2 * S], F32, name="far_map", align_bytes=64)
+        raw_w1 = [keep.tile([P, PACK, H], F32, name=f"raw_w1_{z}") for z in range(PASSES)]
+        near_maps = [keep.tile([P, 2 * S], F32, name=f"near_map{b}", align_bytes=64) for b in range(2)]
+        far_maps = [keep.tile([P, 2 * S], F32, name=f"far_map{b}", align_bytes=64) for b in range(3)]
         joined = keep.tile([P, PACK, S], BF16, name="joined")
 
         nc.vector.memset(store_scales[:].bitcast(I32), 0)
         nc.sync.dma_start(offs_sb[:], offs)
         nc.sync.dma_start(store_words[0][:].bitcast(I32), x_words[0].bitcast(I32))
-        for q in range(4):
-            nc.sync.dma_start(
-                store_scales[32 * q : 32 * q + 8, :].bitcast(I32), x_scales[:, 4 * q : 4 * q + 4, :].bitcast(I32)
-            )
+        scale_rows = x_scales.bitcast(I32).rearrange("z (q j) c -> j q z c", j=4)
+        for j in range(4):
+            nc.sync.dma_start(store_scales[j:P:16, :].bitcast(I32), scale_rows[j])
         nc.sync.dma_start(store_words[1][:].bitcast(I32), x_words[1].bitcast(I32))
         for z in range(PASSES):
-            nc.sync.dma_start(raw[0][z][:], w1[512 * z : 512 * (z + 1), :].rearrange("(p j) c -> p j c", j=PACK))
+            nc.sync.dma_start(raw_w1[z][:], w1[BLOCK * z : BLOCK * (z + 1), :].rearrange("(p j) c -> p j c", j=PACK))
         nc.sync.dma_start(near_sb[:], near)
         nc.sync.dma_start(far_sb[:], far)
 
         nc.vector.memset(moved_scales[:].bitcast(I32), 0)
-        nc.vector.memset(near_maps[0][:, :S].bitcast(I32), 0)
-        for cell_map in near_maps[1:] + [far_map]:
+        for cell_map in (near_maps[0], near_maps[1]):
+            nc.vector.memset(cell_map[:, :S].bitcast(I32), 0)
+        for cell_map in far_maps:
             nc.scalar.copy(cell_map[:, :S], near_maps[0][:, :S])
 
         nc.vector.tensor_copy(picked_scales[:], store_scales[:].indirect(offs_sb[:]))
-        nc.sync.dma_start(moved_scales[0:100, :].bitcast(I32), picked_scales[4:104, :].bitcast(I32))
-        raw_w2 = head.tile([P, PASSES, PACK, H], F32, name="raw_w2", align_bytes=64, offset=2048)
-        raw.append([raw_w2[:, z] for z in range(PASSES)])
+        nc.sync.dma_start(moved_scales[0:112, :].bitcast(I32), picked_scales[16:128, :].bitcast(I32))
+        raw_w2 = head.tile([P, PASSES, PACK, H], F32, name="raw_w2", align_bytes=64, offset=3584)
         for z in range(PASSES):
-            nc.sync.dma_start(raw[1][z], w2[512 * z : 512 * (z + 1), :].rearrange("(p j) c -> p j c", j=PACK))
+            nc.sync.dma_start(raw_w2[:, z], w2[BLOCK * z : BLOCK * (z + 1), :].rearrange("(p j) c -> p j c", j=PACK))
+        raw_w3 = head.tile([P, PACK, N], F32, name="raw_w3", align_bytes=64, offset=512)
+        w3_slots = w3.rearrange("(g t q) n -> t g q n", t=PACK, q=8)
+        for t in range(PACK):
+            nc.sync.dma_start(raw_w3[:, t, :], w3_slots[t])
+
+        raw = [[raw_w1[z][:] for z in range(PASSES)], [raw_w2[:, z] for z in range(PASSES)]]
         x_planes = [picked_scales, moved_scales]
         picked_words = {}
-        staged = {}
         weights = {}
         sums = {}
         results = {}
 
         def pick(s, z, home):
             picked_words[s, z] = home
-            nc.vector.tensor_copy(home, store_words[z][:].indirect(offs_sb[:, 32 * s : 32 * (s + 1)]))
+            nc.vector.tensor_copy(home[:], store_words[z][:].indirect(offs_sb[:, 32 * s : 32 * (s + 1)]))
 
-        def spare(cell_map, place):
-            return cell_map[:, S + 256 * place : S + 256 * (place + 1)].bitcast(BF16)
+        def source(key):
+            s, z, t = key
+            return raw[s][z].rearrange("p j (g t q) -> p t g q j", t=PACK, q=8)[:, t]
 
-        def cast(key, source, home):
-            if home is None:
-                own = keep.tile([P, P * PACK], BF16, name=f"staged{key}", align_bytes=64)
-                home = own[:]
-            staged[key] = home
-            nc.scalar.copy(home.rearrange("p (g q j) -> p g q j", q=8, j=PACK), source)
+        def quantize(label, sources, staging, codes_tag=None):
+            count = len(sources)
+            for i, (key, values) in enumerate(sources):
+                block = staging[:, BLOCK * i : BLOCK * (i + 1)]
+                nc.scalar.copy(block.rearrange("p (g q j) -> p g q j", q=8, j=PACK), values)
+            codes = keep.tile([P, P * count], U32, name=f"codes_{label}", tag=codes_tag or f"codes_{label}", align_bytes=64)
+            plane = keep.tile([P, P * count], U8, name=f"plane_{label}", align_bytes=64)
+            nc.vector.quantize_mx(out=codes[:].bitcast(FP8X4), scales=plane[:], in_=staging[:, : BLOCK * count])
+            for i, (key, values) in enumerate(sources):
+                weights[key] = (codes[:, P * i : P * (i + 1)], plane[:, P * i : P * (i + 1)])
 
-        def cast_w(s, z, t, home=None):
-            cast(f"{s}{z}{t}", raw[s][z][:].rearrange("p j (g t q) -> p t g q j", t=PACK, q=8)[:, t], home)
+        def quantize_alone(key, tag):
+            staging = keep.tile([P, BLOCK], BF16, name=f"staging_{tag}", tag=tag, align_bytes=64)
+            quantize("%d%d%d" % key, [(key, source(key))], staging[:])
 
-        def quantize(key):
-            codes = keep.tile([P, P], U32, name=f"codes{key}", align_bytes=64)
-            plane = keep.tile([P, P], U8, name=f"plane{key}", align_bytes=64)
-            nc.vector.quantize_mx(out=codes[:].bitcast(FP8X4), scales=plane[:], in_=staged[key])
-            weights[key] = (codes, plane)
+        def quantize_in(cell_map, keys, codes_tag=None):
+            quantize("%d%d%d" % keys[0], [(key, source(key)) for key in keys], cell_map[:, S:].bitcast(BF16), codes_tag)
 
         def multiply(s, t):
             acc = psum.tile([P, V], F32, name="acc")
             sums[s, t] = acc
-            for z in range(PASSES):
-                codes, plane = weights[f"{s}{z}{t}"]
+            order = (0, 1) if t < 2 else (1, 0)
+            for z in order:
+                codes, plane = weights[s, z, t]
                 nc.tensor.matmul_mx(
                     out=acc[:],
-                    lhsT=codes[:].bitcast(FP8X4),
-                    lhsT_scale=plane[:],
-                    rhs=picked_words[s, z].bitcast(FP4X4),
+                    lhsT=codes.bitcast(FP8X4),
+                    lhsT_scale=plane,
+                    rhs=picked_words[s, z][:].bitcast(FP4X4),
                     rhs_scale=x_planes[z][:, V * s : V * (s + 1)],
-                    start=(z == 0),
-                    stop=(z == PASSES - 1),
+                    start=(z == order[0]),
+                    stop=(z == order[1]),
                 )
 
-        def prepare(s, t, homes=(None, None)):
-            for z in range(PASSES):
-                if f"{s}{z}{t}" not in staged:
-                    cast_w(s, z, t, homes[z])
-                    quantize(f"{s}{z}{t}")
-            multiply(s, t)
-
         def rectify(s, t):
-            results[s, t] = keep.tile([P, V], F32, name=f"result{s}{t}")
+            results[s, t] = keep.tile([P, V], F32, name=f"result{s}{t}", align_bytes=64)
             nc.scalar.activation(results[s, t][:], sums[s, t][:], RELU)
 
         def put_near(t):
-            nc.vector.tensor_copy(near_maps[t % 3][:].indirect(near_sb[:]), results[0, t][:])
+            nc.vector.tensor_copy(near_maps[t % 2][:].indirect(near_sb[:]), results[NEAR, t][:])
 
         def put_far(t):
-            nc.vector.tensor_copy(far_map[:].indirect(far_sb[:]), results[1, t][:])
-            nc.vector.tensor_tensor(joined[:, t, :], near_maps[t % 3][:, :S], far_map[:, :S], MAX)
+            nc.vector.tensor_copy(far_maps[t % 3][:].indirect(far_sb[:]), results[FAR, t][:])
 
-        first_words = keep.tile([P, V], U16, name="first_words", align_bytes=64)
-        middle_words = head.tile([P, 2, V], U16, name="middle_words", align_bytes=64, offset=0)
-        pick(0, 0, first_words[:])
-        pick(0, 1, middle_words[:, 0, :])
-        pick(1, 0, middle_words[:, 1, :])
-        for t in range(3):
-            cast_w(0, 0, t)
-            quantize(f"00{t}")
-        prepare(0, 0)
-        last_words = keep.tile([P, V], U16, name="last_words", tag="staged010", align_bytes=64)
-        pick(1, 1, last_words[:])
-        prepare(0, 1, (None, spare(near_maps[0], 0)))
-        rectify(0, 0)
+        def join(t, between=None):
+            excess = keep.tile([P, S], F32, name=f"excess{t}", tag=f"join{t % 2}")
+            lifted = keep.tile([P, S], F32, name=f"lifted{t}", tag=f"join{(t + 1) % 2}")
+            halves = [slice(h * V, (h + 1) * V) for h in range(2)]
+            for cols in halves:
+                nc.gpsimd.tensor_tensor(excess[:, cols], near_maps[t % 2][:, cols], far_maps[t][:, cols], SUBTRACT)
+                nc.scalar.activation(lifted[:, cols], excess[:, cols], RELU)
+                if between and cols.start == 0:
+                    multiply(*between)
+                    rectify(*between)
+            for cols in halves:
+                nc.gpsimd.tensor_tensor(joined[:, t, cols], lifted[:, cols], far_maps[t][:, cols], ADD)
+
+        pick(NEAR, 0, keep.tile([P, V], U16, name="words_near0", align_bytes=64))
+        pick(NEAR, 1, head.tile([P, V], U16, name="words_near1", align_bytes=64, offset=2560))
+        quantize_alone((NEAR, 0, 0), "stage_a")
+        quantize_alone((NEAR, 0, 1), "stage_b")
+        pick(FAR, 0, keep.tile([P, V], U16, name="words_far0", tag="stage_b", align_bytes=64))
+        staging_first = mid.tile([P, BLOCK], BF16, name="staging_first", align_bytes=64, offset=512)
+        quantize("010", [((NEAR, 1, 0), source((NEAR, 1, 0)))], staging_first[:])
+        multiply(NEAR, 0)
+        pick(FAR, 1, mid.tile([P, V], U16, name="words_far1", align_bytes=64, offset=0))
+        quantize_alone((NEAR, 1, 1), "stage_d")
+        multiply(NEAR, 1)
+        rectify(NEAR, 0)
         put_near(0)
-        prepare(0, 2, (None, spare(near_maps[1], 0)))
-        rectify(0, 1)
-        prepare(0, 3, (spare(near_maps[1], 1), spare(near_maps[1], 2)))
+        rectify(NEAR, 1)
+        quantize_alone((NEAR, 0, 2), "stage_e")
+        quantize_in(near_maps[1], [(FAR, 0, 0), (FAR, 1, 0)])
         put_near(1)
-        prepare(1, 0, (spare(near_maps[2], 0), spare(near_maps[2], 1)))
-        rectify(0, 2)
-        prepare(1, 1, (spare(near_maps[2], 2), spare(near_maps[2], 3)))
-        rectify(0, 3)
-        put_near(2)
-        prepare(1, 2, (spare(far_map, 0), spare(far_map, 1)))
-        rectify(1, 0)
-        prepare(1, 3, (spare(far_map, 2), spare(far_map, 3)))
-        rectify(1, 1)
-        put_far(0)
-        put_near(3)
-        rectify(1, 2)
-        rectify(1, 3)
-        for t in range(1, PACK):
-            put_far(t)
-
-        raw3 = keep.tile([P, PACK, N], F32, name="raw3", tag="raw00")
-        w3_slots = w3.rearrange("(g t q) n -> t g q n", t=PACK, q=8)
-        for t in range(PACK):
-            nc.sync.dma_start(raw3[:, t, :], w3_slots[t])
-        cast("w3", raw3[:].rearrange("p t (g q) -> p g q t", q=8), None)
-        quantize("w3")
+        multiply(FAR, 0)
+        staging_late = mid.tile([P, 4 * BLOCK], BF16, name="staging_late", align_bytes=64, offset=1024)
+        late = [(key, source(key)) for key in ((NEAR, 1, 2), (NEAR, 0, 3), (NEAR, 1, 3))]
+        quantize("late", late + [("w3", raw_w3[:].rearrange("p t (g q) -> p g q t", q=8))], staging_late[:])
         codes3, plane3 = weights["w3"]
+        staging_far1 = keep.tile([P, 2 * BLOCK], BF16, name="staging_far1", align_bytes=64)
+        quantize("far1", [((FAR, z, 1), source((FAR, z, 1))) for z in range(PASSES)], staging_far1[:])
+        rectify(FAR, 0)
+        put_far(0)
+        multiply(FAR, 1)
+        rectify(FAR, 1)
+        quantize_in(far_maps[1], [(FAR, z, t) for t in (2, 3) for z in range(PASSES)])
+        put_far(1)
+        join(0, (NEAR, 2))
+        put_near(2)
+        for s, t in ((FAR, 2), (FAR, 3), (NEAR, 3)):
+            multiply(s, t)
+            rectify(s, t)
+        put_far(2)
+        join(1)
+        join(2)
+        chunks = [slice(c * CHUNK, (c + 1) * CHUNK) for c in range(S // CHUNK)]
+        woven = [keep.tile([P, CHUNK, PACK], BF16, name=f"woven{c}", align_bytes=64) for c in range(S // CHUNK)]
+        for c, cols in enumerate(chunks):
+            nc.scalar.copy(woven[c][:, :, 0:2], joined[:, 0:2, cols].rearrange("p t r -> p r t"))
+        put_near(3)
+        put_far(3)
 
-        for c in range(S // CHUNK):
-            cols = slice(c * CHUNK, (c + 1) * CHUNK)
-            woven = keep.tile([P, CHUNK * PACK], BF16, name=f"woven{c}", align_bytes=64)
-            dst = woven[:].rearrange("p (c i t) -> p c t i", i=4, t=PACK)
-            src = joined[:, :, cols].rearrange("p t (c i) -> p c t i", i=4)
-            if c in (0, 3):
-                nc.scalar.copy(dst, src)
+        for cols in chunks:
+            nc.vector.tensor_tensor(joined[:, 3, cols], near_maps[1][:, cols], far_maps[0][:, cols], MAX)
+        for c, cols in enumerate(chunks):
+            upper = joined[:, 2:4, cols].rearrange("p t r -> p r t")
+            if c < 3:
+                nc.scalar.copy(woven[c][:, :, 2:4], upper)
             else:
-                nc.vector.tensor_copy(dst, src)
+                nc.vector.tensor_copy(woven[c][:, :, 2:4], upper)
+        for c in (0, 3, 1, 2):
             z_codes = keep.tile([P, CHUNK], U32, name=f"z_codes{c}", align_bytes=64)
             z_plane = keep.tile([P, CHUNK], U8, name=f"z_plane{c}", align_bytes=64)
-            nc.vector.quantize_mx(out=z_codes[:].bitcast(FP8X4), scales=z_plane[:], in_=woven[:])
+            nc.vector.quantize_mx(
+                out=z_codes[:].bitcast(FP8X4), scales=z_plane[:], in_=woven[c][:].rearrange("p r t -> p (r t)")
+            )
             total = psum.tile([P, CHUNK], F32, name="total")
             nc.tensor.matmul_mx(
                 out=total[:],
-                lhsT=codes3[:].bitcast(FP8X4),
-                lhsT_scale=plane3[:],
+                lhsT=codes3.bitcast(FP8X4),
+                lhsT_scale=plane3,
                 rhs=z_codes[:].bitcast(FP8X4),
                 rhs_scale=z_plane[:],
                 start=True,
                 stop=True,
             )
             leaving = keep.tile([P, CHUNK], F32, name=f"leaving{c}")
-            nc.scalar.copy(leaving[:], total[:])
-            nc.sync.dma_start(out[:, cols], leaving[:])
+            if c == 2:
+                nc.vector.tensor_copy(leaving[:], total[:])
+            else:
+                nc.scalar.copy(leaving[:], total[:])
+            nc.sync.dma_start(out[:, chunks[c]], leaving[:])

@@ -3,7 +3,7 @@ from contextlib import ExitStack
 import concourse.mybir as mybir
 
 K, T, S, H, N, V = 1024, 2048, 1024, 512, 128, 512
-FLOPS = 2 * K * H * V * 2 + 2 * H * N * S
+FLOPS = 2 * (2 * K * H * V) + 2 * H * N * S
 
 F32 = mybir.dt.float32
 BF16 = mybir.dt.bfloat16
@@ -20,10 +20,18 @@ SUBTRACT = mybir.AluOpType.subtract
 
 P = 128
 PACK = 4
-PASSES = K // (P * PACK)
-BLOCK = P * PACK
-CHUNK = 256
+PASS_ROWS = P * PACK
+PASSES = K // PASS_ROWS
+GROUP = 8
+SECOND_PASS_ROW = 16
+LIST_COLUMNS = V // 16
 NEAR, FAR = 0, 1
+PSUM_BUFS = 4
+MAX_WIDTH = 256
+CHUNK_EDGES = (0, 256, 512, 768, 896, 1024)
+VECTOR_WEAVES = 2
+FINISH_ORDER = (0, 2, 1, 3, 4)
+VECTOR_EMPTIES = (3, 4)
 
 
 def tile_picked_bev_max_p_kernel(
@@ -32,14 +40,14 @@ def tile_picked_bev_max_p_kernel(
     nc = tc.nc
     with ExitStack() as ctx:
         keep = ctx.enter_context(tc.tile_pool(name="keep", bufs=1))
-        head = ctx.enter_context(tc.tile_pool(name="head", bufs=1))
-        mid = ctx.enter_context(tc.tile_pool(name="mid", bufs=1))
-        psum = ctx.enter_context(tc.psum_pool(name="psum", bufs=4))
+        after_scales = ctx.enter_context(tc.tile_pool(name="after_scales", bufs=1))
+        after_first = ctx.enter_context(tc.tile_pool(name="after_first", bufs=1))
+        psum = ctx.enter_context(tc.psum_pool(name="psum", bufs=PSUM_BUFS))
 
         offs_sb = keep.tile([P, S // 16], U16, name="offs_sb")
-        near_sb = keep.tile([P, V // 16], U16, name="near_sb")
-        far_sb = keep.tile([P, V // 16], U16, name="far_sb")
-        store_scales = head.tile([P, T], U8, name="store_scales", align_bytes=64, offset=2048)
+        near_sb = keep.tile([P, LIST_COLUMNS], U16, name="near_sb")
+        far_sb = keep.tile([P, LIST_COLUMNS], U16, name="far_sb")
+        store_scales = after_scales.tile([P, T], U8, name="store_scales", align_bytes=64, offset=2048)
         picked_scales = keep.tile([P, S], U8, name="picked_scales", align_bytes=64)
         moved_scales = keep.tile([P, S], U8, name="moved_scales", align_bytes=64)
         store_words = [keep.tile([P, T], U16, name=f"store_words{z}", align_bytes=64) for z in range(PASSES)]
@@ -53,172 +61,202 @@ def tile_picked_bev_max_p_kernel(
         nc.sync.dma_start(store_words[0][:].bitcast(I32), x_words[0].bitcast(I32))
         scale_rows = x_scales.bitcast(I32).rearrange("z (q j) c -> j q z c", j=4)
         for j in range(4):
-            nc.sync.dma_start(store_scales[j:P:16, :].bitcast(I32), scale_rows[j])
+            nc.sync.dma_start(store_scales[j:P:SECOND_PASS_ROW, :].bitcast(I32), scale_rows[j])
         nc.sync.dma_start(store_words[1][:].bitcast(I32), x_words[1].bitcast(I32))
         for z in range(PASSES):
-            nc.sync.dma_start(raw_w1[z][:], w1[BLOCK * z : BLOCK * (z + 1), :].rearrange("(p j) c -> p j c", j=PACK))
+            rows = w1[PASS_ROWS * z : PASS_ROWS * (z + 1), :]
+            nc.sync.dma_start(raw_w1[z][:], rows.rearrange("(p j) c -> p j c", j=PACK))
         nc.sync.dma_start(near_sb[:], near)
         nc.sync.dma_start(far_sb[:], far)
 
         nc.vector.memset(moved_scales[:].bitcast(I32), 0)
-        for cell_map in (near_maps[0], near_maps[1]):
+        for cell_map in near_maps:
             nc.vector.memset(cell_map[:, :S].bitcast(I32), 0)
         for cell_map in far_maps:
             nc.scalar.copy(cell_map[:, :S], near_maps[0][:, :S])
 
         nc.vector.tensor_copy(picked_scales[:], store_scales[:].indirect(offs_sb[:]))
-        nc.sync.dma_start(moved_scales[0:112, :].bitcast(I32), picked_scales[16:128, :].bitcast(I32))
-        raw_w2 = head.tile([P, PASSES, PACK, H], F32, name="raw_w2", align_bytes=64, offset=3584)
+        nc.sync.dma_start(
+            moved_scales[0 : P - SECOND_PASS_ROW, :].bitcast(I32), picked_scales[SECOND_PASS_ROW:P, :].bitcast(I32)
+        )
+        raw_w2 = after_scales.tile([P, PASSES, PACK, H], F32, name="raw_w2", align_bytes=64, offset=3584)
         for z in range(PASSES):
-            nc.sync.dma_start(raw_w2[:, z], w2[BLOCK * z : BLOCK * (z + 1), :].rearrange("(p j) c -> p j c", j=PACK))
-        raw_w3 = head.tile([P, PACK, N], F32, name="raw_w3", align_bytes=64, offset=512)
-        w3_slots = w3.rearrange("(g t q) n -> t g q n", t=PACK, q=8)
+            rows = w2[PASS_ROWS * z : PASS_ROWS * (z + 1), :]
+            nc.sync.dma_start(raw_w2[:, z], rows.rearrange("(p j) c -> p j c", j=PACK))
+        raw_w3 = after_scales.tile([P, PACK, N], F32, name="raw_w3", align_bytes=64, offset=512)
+        w3_slabs = w3.rearrange("(g t q) n -> t g q n", t=PACK, q=GROUP)
         for t in range(PACK):
-            nc.sync.dma_start(raw_w3[:, t, :], w3_slots[t])
+            nc.sync.dma_start(raw_w3[:, t, :], w3_slabs[t])
 
         raw = [[raw_w1[z][:] for z in range(PASSES)], [raw_w2[:, z] for z in range(PASSES)]]
-        x_planes = [picked_scales, moved_scales]
+        x_scale_tiles = [picked_scales, moved_scales]
         picked_words = {}
         weights = {}
         sums = {}
         results = {}
 
-        def pick(s, z, home):
-            picked_words[s, z] = home
-            nc.vector.tensor_copy(home[:], store_words[z][:].indirect(offs_sb[:, 32 * s : 32 * (s + 1)]))
+        def pick(sensor, z, words):
+            picked_words[sensor, z] = words
+            entries = offs_sb[:, LIST_COLUMNS * sensor : LIST_COLUMNS * (sensor + 1)]
+            nc.vector.tensor_copy(words[:], store_words[z][:].indirect(entries))
 
-        def source(key):
-            s, z, t = key
-            return raw[s][z].rearrange("p j (g t q) -> p t g q j", t=PACK, q=8)[:, t]
+        def layer_operand(key):
+            sensor, z, t = key
+            return key, raw[sensor][z].rearrange("p j (g t q) -> p t g q j", t=PACK, q=GROUP)[:, t]
 
-        def quantize(label, sources, staging, codes_tag=None):
-            count = len(sources)
-            for i, (key, values) in enumerate(sources):
-                block = staging[:, BLOCK * i : BLOCK * (i + 1)]
-                nc.scalar.copy(block.rearrange("p (g q j) -> p g q j", q=8, j=PACK), values)
-            codes = keep.tile([P, P * count], U32, name=f"codes_{label}", tag=codes_tag or f"codes_{label}", align_bytes=64)
-            plane = keep.tile([P, P * count], U8, name=f"plane_{label}", align_bytes=64)
-            nc.vector.quantize_mx(out=codes[:].bitcast(FP8X4), scales=plane[:], in_=staging[:, : BLOCK * count])
-            for i, (key, values) in enumerate(sources):
-                weights[key] = (codes[:, P * i : P * (i + 1)], plane[:, P * i : P * (i + 1)])
+        def quantize(label, operands, staging):
+            count = len(operands)
+            for n, (key, values) in enumerate(operands):
+                rounded = staging[:, PASS_ROWS * n : PASS_ROWS * (n + 1)]
+                nc.scalar.copy(rounded.rearrange("p (g q j) -> p g q j", q=GROUP, j=PACK), values)
+            codes = keep.tile([P, P * count], U32, name=f"codes_{label}", align_bytes=64)
+            scales = keep.tile([P, P * count], U8, name=f"scales_{label}", align_bytes=64)
+            nc.vector.quantize_mx(out=codes[:].bitcast(FP8X4), scales=scales[:], in_=staging[:, : PASS_ROWS * count])
+            for n, (key, values) in enumerate(operands):
+                weights[key] = (codes[:, P * n : P * (n + 1)], scales[:, P * n : P * (n + 1)])
 
         def quantize_alone(key, tag):
-            staging = keep.tile([P, BLOCK], BF16, name=f"staging_{tag}", tag=tag, align_bytes=64)
-            quantize("%d%d%d" % key, [(key, source(key))], staging[:])
+            staging = keep.tile([P, PASS_ROWS], BF16, name=tag, tag=tag, align_bytes=64)
+            quantize("%d%d%d" % key, [layer_operand(key)], staging[:])
 
-        def quantize_in(cell_map, keys, codes_tag=None):
-            quantize("%d%d%d" % keys[0], [(key, source(key)) for key in keys], cell_map[:, S:].bitcast(BF16), codes_tag)
+        def quantize_before_scatter(cell_map, keys):
+            quantize("%d%d%d" % keys[0], [layer_operand(key) for key in keys], cell_map[:, S:].bitcast(BF16))
 
-        def multiply(s, t):
+        def multiply(sensor, t):
             acc = psum.tile([P, V], F32, name="acc")
-            sums[s, t] = acc
+            sums[sensor, t] = acc
             order = (0, 1) if t < 2 else (1, 0)
             for z in order:
-                codes, plane = weights[s, z, t]
+                codes, scales = weights[sensor, z, t]
                 nc.tensor.matmul_mx(
                     out=acc[:],
                     lhsT=codes.bitcast(FP8X4),
-                    lhsT_scale=plane,
-                    rhs=picked_words[s, z][:].bitcast(FP4X4),
-                    rhs_scale=x_planes[z][:, V * s : V * (s + 1)],
+                    lhsT_scale=scales,
+                    rhs=picked_words[sensor, z][:].bitcast(FP4X4),
+                    rhs_scale=x_scale_tiles[z][:, V * sensor : V * (sensor + 1)],
                     start=(z == order[0]),
                     stop=(z == order[1]),
                 )
 
-        def rectify(s, t):
-            results[s, t] = keep.tile([P, V], F32, name=f"result{s}{t}", align_bytes=64)
-            nc.scalar.activation(results[s, t][:], sums[s, t][:], RELU)
+        def rectify(sensor, t):
+            results[sensor, t] = keep.tile([P, V], F32, name=f"result{sensor}{t}", align_bytes=64)
+            nc.scalar.activation(results[sensor, t][:], sums[sensor, t][:], RELU)
 
-        def put_near(t):
-            nc.vector.tensor_copy(near_maps[t % 2][:].indirect(near_sb[:]), results[NEAR, t][:])
+        def near_map(t):
+            return near_maps[t % len(near_maps)]
 
-        def put_far(t):
-            nc.vector.tensor_copy(far_maps[t % 3][:].indirect(far_sb[:]), results[FAR, t][:])
+        def far_map(t):
+            return far_maps[t % len(far_maps)]
 
-        def join(t, between=None):
+        def scatter_near(t):
+            nc.vector.tensor_copy(near_map(t)[:].indirect(near_sb[:]), results[NEAR, t][:])
+
+        def scatter_far(t):
+            nc.vector.tensor_copy(far_map(t)[:].indirect(far_sb[:]), results[FAR, t][:])
+
+        halves = [slice(0, S // 2), slice(S // 2, S)]
+
+        def join_tiles(t):
             excess = keep.tile([P, S], F32, name=f"excess{t}", tag=f"join{t % 2}")
             lifted = keep.tile([P, S], F32, name=f"lifted{t}", tag=f"join{(t + 1) % 2}")
-            halves = [slice(h * V, (h + 1) * V) for h in range(2)]
+            return excess, lifted
+
+        def lift(t, excess, lifted, cols):
+            nc.gpsimd.tensor_tensor(excess[:, cols], near_map(t)[:, cols], far_map(t)[:, cols], SUBTRACT)
+            nc.scalar.activation(lifted[:, cols], excess[:, cols], RELU)
+
+        def settle(t, lifted):
             for cols in halves:
-                nc.gpsimd.tensor_tensor(excess[:, cols], near_maps[t % 2][:, cols], far_maps[t][:, cols], SUBTRACT)
-                nc.scalar.activation(lifted[:, cols], excess[:, cols], RELU)
-                if between and cols.start == 0:
-                    multiply(*between)
-                    rectify(*between)
-            for cols in halves:
-                nc.gpsimd.tensor_tensor(joined[:, t, cols], lifted[:, cols], far_maps[t][:, cols], ADD)
+                nc.gpsimd.tensor_tensor(joined[:, t, cols], lifted[:, cols], far_map(t)[:, cols], ADD)
 
         pick(NEAR, 0, keep.tile([P, V], U16, name="words_near0", align_bytes=64))
-        pick(NEAR, 1, head.tile([P, V], U16, name="words_near1", align_bytes=64, offset=2560))
-        quantize_alone((NEAR, 0, 0), "stage_a")
-        quantize_alone((NEAR, 0, 1), "stage_b")
-        pick(FAR, 0, keep.tile([P, V], U16, name="words_far0", tag="stage_b", align_bytes=64))
-        staging_first = mid.tile([P, BLOCK], BF16, name="staging_first", align_bytes=64, offset=512)
-        quantize("010", [((NEAR, 1, 0), source((NEAR, 1, 0)))], staging_first[:])
+        pick(NEAR, 1, after_scales.tile([P, V], U16, name="words_near1", align_bytes=64, offset=2560))
+        quantize_alone((NEAR, 0, 0), "staging_000")
+        quantize_alone((NEAR, 0, 1), "staging_001")
+        pick(FAR, 0, keep.tile([P, V], U16, name="words_far0", tag="staging_001", align_bytes=64))
+        staging_first = after_first.tile([P, PASS_ROWS], BF16, name="staging_first", align_bytes=64, offset=512)
+        quantize("010", [layer_operand((NEAR, 1, 0))], staging_first[:])
         multiply(NEAR, 0)
-        pick(FAR, 1, mid.tile([P, V], U16, name="words_far1", align_bytes=64, offset=0))
-        quantize_alone((NEAR, 1, 1), "stage_d")
+        pick(FAR, 1, after_first.tile([P, V], U16, name="words_far1", align_bytes=64, offset=0))
+        quantize_alone((NEAR, 1, 1), "staging_011")
         multiply(NEAR, 1)
         rectify(NEAR, 0)
-        put_near(0)
+        scatter_near(0)
+
         rectify(NEAR, 1)
-        quantize_alone((NEAR, 0, 2), "stage_e")
-        quantize_in(near_maps[1], [(FAR, 0, 0), (FAR, 1, 0)])
-        put_near(1)
+        quantize_alone((NEAR, 0, 2), "staging_002")
+        quantize_before_scatter(near_map(1), [(FAR, 0, 0), (FAR, 1, 0)])
+        scatter_near(1)
         multiply(FAR, 0)
-        staging_late = mid.tile([P, 4 * BLOCK], BF16, name="staging_late", align_bytes=64, offset=1024)
-        late = [(key, source(key)) for key in ((NEAR, 1, 2), (NEAR, 0, 3), (NEAR, 1, 3))]
-        quantize("late", late + [("w3", raw_w3[:].rearrange("p t (g q) -> p g q t", q=8))], staging_late[:])
-        codes3, plane3 = weights["w3"]
-        staging_far1 = keep.tile([P, 2 * BLOCK], BF16, name="staging_far1", align_bytes=64)
-        quantize("far1", [((FAR, z, 1), source((FAR, z, 1))) for z in range(PASSES)], staging_far1[:])
+        staging_late = after_first.tile([P, 4 * PASS_ROWS], BF16, name="staging_late", align_bytes=64, offset=1024)
+        late = [layer_operand(key) for key in ((NEAR, 1, 2), (NEAR, 0, 3), (NEAR, 1, 3))]
+        late.append(("w3", raw_w3[:].rearrange("p t (g q) -> p g q t", q=GROUP)))
+        quantize("late", late, staging_late[:])
+        w3_codes, w3_scales = weights["w3"]
+        staging_far1 = keep.tile([P, PASSES * PASS_ROWS], BF16, name="staging_far1", align_bytes=64)
+        quantize("far1", [layer_operand((FAR, z, 1)) for z in range(PASSES)], staging_far1[:])
         rectify(FAR, 0)
-        put_far(0)
+        scatter_far(0)
         multiply(FAR, 1)
         rectify(FAR, 1)
-        quantize_in(far_maps[1], [(FAR, z, t) for t in (2, 3) for z in range(PASSES)])
-        put_far(1)
-        join(0, (NEAR, 2))
-        put_near(2)
-        for s, t in ((FAR, 2), (FAR, 3), (NEAR, 3)):
-            multiply(s, t)
-            rectify(s, t)
-        put_far(2)
-        join(1)
-        join(2)
-        chunks = [slice(c * CHUNK, (c + 1) * CHUNK) for c in range(S // CHUNK)]
-        woven = [keep.tile([P, CHUNK, PACK], BF16, name=f"woven{c}", align_bytes=64) for c in range(S // CHUNK)]
+        quantize_before_scatter(far_map(1), [(FAR, z, t) for t in (2, 3) for z in range(PASSES)])
+        scatter_far(1)
+
+        excess, lifted = join_tiles(0)
+        lift(0, excess, lifted, halves[0])
+        multiply(NEAR, 2)
+        rectify(NEAR, 2)
+        lift(0, excess, lifted, halves[1])
+        settle(0, lifted)
+        scatter_near(2)
+        for sensor, t in ((FAR, 2), (FAR, 3), (NEAR, 3)):
+            multiply(sensor, t)
+            rectify(sensor, t)
+        scatter_far(2)
+        for t in (1, 2):
+            excess, lifted = join_tiles(t)
+            for cols in halves:
+                lift(t, excess, lifted, cols)
+            settle(t, lifted)
+
+        chunks = [slice(lo, hi) for lo, hi in zip(CHUNK_EDGES, CHUNK_EDGES[1:])]
+        woven = [
+            keep.tile([P, cols.stop - cols.start, PACK], BF16, name=f"woven{c}", align_bytes=64)
+            for c, cols in enumerate(chunks)
+        ]
         for c, cols in enumerate(chunks):
             nc.scalar.copy(woven[c][:, :, 0:2], joined[:, 0:2, cols].rearrange("p t r -> p r t"))
-        put_near(3)
-        put_far(3)
+        scatter_near(3)
+        scatter_far(3)
 
-        for cols in chunks:
-            nc.vector.tensor_tensor(joined[:, 3, cols], near_maps[1][:, cols], far_maps[0][:, cols], MAX)
+        for lo in range(0, S, MAX_WIDTH):
+            cols = slice(lo, lo + MAX_WIDTH)
+            nc.vector.tensor_tensor(joined[:, 3, cols], near_map(3)[:, cols], far_map(3)[:, cols], MAX)
         for c, cols in enumerate(chunks):
             upper = joined[:, 2:4, cols].rearrange("p t r -> p r t")
-            if c < 3:
-                nc.scalar.copy(woven[c][:, :, 2:4], upper)
-            else:
+            if c == VECTOR_WEAVES:
                 nc.vector.tensor_copy(woven[c][:, :, 2:4], upper)
-        for c in (0, 3, 1, 2):
-            z_codes = keep.tile([P, CHUNK], U32, name=f"z_codes{c}", align_bytes=64)
-            z_plane = keep.tile([P, CHUNK], U8, name=f"z_plane{c}", align_bytes=64)
+            else:
+                nc.scalar.copy(woven[c][:, :, 2:4], upper)
+        for c in FINISH_ORDER:
+            width = chunks[c].stop - chunks[c].start
+            z_codes = keep.tile([P, width], U32, name=f"z_codes{c}", align_bytes=64)
+            z_scales = keep.tile([P, width], U8, name=f"z_scales{c}", align_bytes=64)
             nc.vector.quantize_mx(
-                out=z_codes[:].bitcast(FP8X4), scales=z_plane[:], in_=woven[c][:].rearrange("p r t -> p (r t)")
+                out=z_codes[:].bitcast(FP8X4), scales=z_scales[:], in_=woven[c][:].rearrange("p r t -> p (r t)")
             )
-            total = psum.tile([P, CHUNK], F32, name="total")
+            total = psum.tile([P, width], F32, name="total")
             nc.tensor.matmul_mx(
                 out=total[:],
-                lhsT=codes3.bitcast(FP8X4),
-                lhsT_scale=plane3,
+                lhsT=w3_codes.bitcast(FP8X4),
+                lhsT_scale=w3_scales,
                 rhs=z_codes[:].bitcast(FP8X4),
-                rhs_scale=z_plane[:],
+                rhs_scale=z_scales[:],
                 start=True,
                 stop=True,
             )
-            leaving = keep.tile([P, CHUNK], F32, name=f"leaving{c}")
-            if c == 2:
+            leaving = keep.tile([P, width], F32, name=f"leaving{c}")
+            if c in VECTOR_EMPTIES:
                 nc.vector.tensor_copy(leaving[:], total[:])
             else:
                 nc.scalar.copy(leaving[:], total[:])

@@ -27,9 +27,9 @@ SECOND_PASS_ROW = 16
 LIST_COLUMNS = V // 16
 NEAR, FAR = 0, 1
 PSUM_BUFS = 4
-MAX_WIDTH = 256
+MAX_RUNS = ((0, 0), (2, 3), (1, 1), (4, 4))
 CHUNK_EDGES = (0, 256, 512, 768, 896, 1024)
-VECTOR_WEAVES = 2
+VECTOR_WEAVES = (2, 3)
 FINISH_ORDER = (0, 2, 1, 3, 4)
 VECTOR_EMPTIES = (3, 4)
 
@@ -58,11 +58,11 @@ def tile_picked_bev_max_p_kernel(
 
         nc.vector.memset(store_scales[:].bitcast(I32), 0)
         nc.sync.dma_start(offs_sb[:], offs)
-        nc.sync.dma_start(store_words[0][:].bitcast(I32), x_words[0].bitcast(I32))
         scale_rows = x_scales.bitcast(I32).rearrange("z (q j) c -> j q z c", j=4)
         for j in range(4):
             nc.sync.dma_start(store_scales[j:P:SECOND_PASS_ROW, :].bitcast(I32), scale_rows[j])
-        nc.sync.dma_start(store_words[1][:].bitcast(I32), x_words[1].bitcast(I32))
+        for z in range(PASSES):
+            nc.sync.dma_start(store_words[z][:].bitcast(I32), x_words[z].bitcast(I32))
         for z in range(PASSES):
             rows = w1[PASS_ROWS * z : PASS_ROWS * (z + 1), :]
             nc.sync.dma_start(raw_w1[z][:], rows.rearrange("(p j) c -> p j c", j=PACK))
@@ -102,13 +102,13 @@ def tile_picked_bev_max_p_kernel(
 
         def layer_operand(key):
             sensor, z, t = key
-            return key, raw[sensor][z].rearrange("p j (g t q) -> p t g q j", t=PACK, q=GROUP)[:, t]
+            return key, raw[sensor][z].rearrange("p j (g t h i) -> p t g h j i", t=PACK, h=2, i=PACK)[:, t]
 
         def quantize(label, operands, staging):
             count = len(operands)
             for n, (key, values) in enumerate(operands):
                 rounded = staging[:, PASS_ROWS * n : PASS_ROWS * (n + 1)]
-                nc.scalar.copy(rounded.rearrange("p (g q j) -> p g q j", q=GROUP, j=PACK), values)
+                nc.scalar.copy(rounded.rearrange("p (g h i j) -> p g h j i", h=2, i=PACK, j=PACK), values)
             codes = keep.tile([P, P * count], U32, name=f"codes_{label}", align_bytes=64)
             scales = keep.tile([P, P * count], U8, name=f"scales_{label}", align_bytes=64)
             nc.vector.quantize_mx(out=codes[:].bitcast(FP8X4), scales=scales[:], in_=staging[:, : PASS_ROWS * count])
@@ -190,7 +190,7 @@ def tile_picked_bev_max_p_kernel(
         multiply(FAR, 0)
         staging_late = after_first.tile([P, 4 * PASS_ROWS], BF16, name="staging_late", align_bytes=64, offset=1024)
         late = [layer_operand(key) for key in ((NEAR, 1, 2), (NEAR, 0, 3), (NEAR, 1, 3))]
-        late.append(("w3", raw_w3[:].rearrange("p t (g q) -> p g q t", q=GROUP)))
+        late.append(("w3", raw_w3[:].rearrange("p t (g h i) -> p g h t i", h=2, i=PACK)))
         quantize("late", late, staging_late[:])
         w3_codes, w3_scales = weights["w3"]
         staging_far1 = keep.tile([P, PASSES * PASS_ROWS], BF16, name="staging_far1", align_bytes=64)
@@ -229,12 +229,12 @@ def tile_picked_bev_max_p_kernel(
         scatter_near(3)
         scatter_far(3)
 
-        for lo in range(0, S, MAX_WIDTH):
-            cols = slice(lo, lo + MAX_WIDTH)
+        for first, last in MAX_RUNS:
+            cols = slice(chunks[first].start, chunks[last].stop)
             nc.vector.tensor_tensor(joined[:, 3, cols], near_map(3)[:, cols], far_map(3)[:, cols], MAX)
         for c, cols in enumerate(chunks):
             upper = joined[:, 2:4, cols].rearrange("p t r -> p r t")
-            if c == VECTOR_WEAVES:
+            if c in VECTOR_WEAVES:
                 nc.vector.tensor_copy(woven[c][:, :, 2:4], upper)
             else:
                 nc.scalar.copy(woven[c][:, :, 2:4], upper)

@@ -52,8 +52,8 @@ def tile_picked_bev_max_p_kernel(
         moved_scales = keep.tile([P, S], U8, name="moved_scales", align_bytes=64)
         store_words = [keep.tile([P, T], U16, name=f"store_words{z}", align_bytes=64) for z in range(PASSES)]
         raw_w1 = [keep.tile([P, PACK, H], F32, name=f"raw_w1_{z}") for z in range(PASSES)]
-        near_maps = [keep.tile([P, 2 * S], F32, name=f"near_map{b}", align_bytes=64) for b in range(2)]
-        far_maps = [keep.tile([P, 2 * S], F32, name=f"far_map{b}", align_bytes=64) for b in range(3)]
+        near_maps = [keep.tile([P, S], F32, name=f"near_map{b}", align_bytes=64) for b in range(2)]
+        far_maps = [keep.tile([P, S], F32, name=f"far_map{b}", align_bytes=64) for b in range(3)]
         joined = keep.tile([P, PACK, S], BF16, name="joined")
 
         nc.vector.memset(store_scales[:].bitcast(I32), 0)
@@ -80,13 +80,13 @@ def tile_picked_bev_max_p_kernel(
             moved_scales[0 : P - SECOND_PASS_ROW, :].bitcast(I32), picked_scales[SECOND_PASS_ROW:P, :].bitcast(I32)
         )
         raw_w2 = after_scales.tile([P, PASSES, PACK, H], F32, name="raw_w2", align_bytes=64, offset=3584)
-        for z in range(PASSES):
-            rows = w2[PASS_ROWS * z : PASS_ROWS * (z + 1), :]
-            nc.sync.dma_start(raw_w2[:, z], rows.rearrange("(p j) c -> p j c", j=PACK))
+        w2_passes = w2.rearrange("(z p j) c -> z p j c", z=PASSES, j=PACK)
+        nc.sync.dma_start(raw_w2[:, 0], w2_passes[0])
         raw_w3 = after_scales.tile([P, PACK, N], F32, name="raw_w3", align_bytes=64, offset=512)
         w3_slabs = w3.rearrange("(g t q) n -> t g q n", t=PACK, q=GROUP)
         for t in range(PACK):
             nc.sync.dma_start(raw_w3[:, t, :], w3_slabs[t])
+        nc.sync.dma_start(raw_w2[:, 1], w2_passes[1])
 
         raw = [[raw_w1[z][:] for z in range(PASSES)], [raw_w2[:, z] for z in range(PASSES)]]
         x_scale_tiles = [picked_scales, moved_scales]
@@ -118,9 +118,6 @@ def tile_picked_bev_max_p_kernel(
         def quantize_alone(key, tag):
             staging = keep.tile([P, PASS_ROWS], BF16, name=tag, tag=tag, align_bytes=64)
             quantize("%d%d%d" % key, [layer_operand(key)], staging[:])
-
-        def quantize_before_scatter(cell_map, keys):
-            quantize("%d%d%d" % keys[0], [layer_operand(key) for key in keys], cell_map[:, S:].bitcast(BF16))
 
         def multiply(sensor, t):
             acc = psum.tile([P, V], F32, name="acc")
@@ -176,30 +173,48 @@ def tile_picked_bev_max_p_kernel(
         pick(FAR, 0, keep.tile([P, V], U16, name="words_far0", tag="staging_001", align_bytes=64))
         staging_first = after_first.tile([P, PASS_ROWS], BF16, name="staging_first", align_bytes=64, offset=512)
         quantize("010", [layer_operand((NEAR, 1, 0))], staging_first[:])
-        multiply(NEAR, 0)
         pick(FAR, 1, after_first.tile([P, V], U16, name="words_far1", align_bytes=64, offset=0))
+        first_sums = [psum.tile([P, P], F32, name=f"first_sums{n}", tag="total") for n in range(V // P)]
+        for z in range(PASSES):
+            codes, scales = weights[NEAR, z, 0]
+            for n, acc in enumerate(first_sums):
+                nc.tensor.matmul_mx(
+                    out=acc[:],
+                    lhsT=codes.bitcast(FP8X4),
+                    lhsT_scale=scales,
+                    rhs=picked_words[NEAR, z][:, P * n : P * (n + 1)].bitcast(FP4X4),
+                    rhs_scale=x_scale_tiles[z][:, P * n : P * (n + 1)],
+                    start=(z == 0),
+                    stop=(z == PASSES - 1),
+                )
+        first_head = keep.tile([P, P], F32, name="first_head", align_bytes=64)
+        first_rest = keep.tile([P, V - P], F32, name="first_rest", align_bytes=64)
+        nc.scalar.activation(first_head[:], first_sums[0][:], RELU)
+        for n in range(1, V // P):
+            nc.scalar.activation(first_rest[:, P * (n - 1) : P * n], first_sums[n][:], RELU)
+        nc.vector.tensor_copy(near_map(0)[:].indirect(near_sb[:, : P // 16]), first_head[:])
         quantize_alone((NEAR, 1, 1), "staging_011")
+        nc.vector.tensor_copy(near_map(0)[:].indirect(near_sb[:, P // 16 :]), first_rest[:])
         multiply(NEAR, 1)
-        rectify(NEAR, 0)
-        scatter_near(0)
 
         rectify(NEAR, 1)
-        quantize_alone((NEAR, 0, 2), "staging_002")
-        quantize_before_scatter(near_map(1), [(FAR, 0, 0), (FAR, 1, 0)])
         scatter_near(1)
+        quantize_alone((NEAR, 0, 2), "staging_002")
+        quantize_alone((FAR, 0, 0), "staging_100")
+        quantize_alone((FAR, 1, 0), "staging_110")
         multiply(FAR, 0)
-        staging_late = after_first.tile([P, 4 * PASS_ROWS], BF16, name="staging_late", align_bytes=64, offset=1024)
-        late = [layer_operand(key) for key in ((NEAR, 1, 2), (NEAR, 0, 3), (NEAR, 1, 3))]
-        late.append(("w3", raw_w3[:].rearrange("p t (g h i) -> p g h t i", h=2, i=PACK)))
-        quantize("late", late, staging_late[:])
+        staging_late = after_first.tile([P, 8 * PASS_ROWS], BF16, name="staging_late", align_bytes=64, offset=1024)
+        staging_next = keep.tile([P, 2 * PASS_ROWS], BF16, name="staging_next", align_bytes=64)
+        w3_values = raw_w3[:].rearrange("p t (g h i) -> p g h t i", h=2, i=PACK)
+        quantize("next", [layer_operand((FAR, 1, 1)), ("w3", w3_values)], staging_next[:])
         w3_codes, w3_scales = weights["w3"]
-        staging_far1 = keep.tile([P, PASSES * PASS_ROWS], BF16, name="staging_far1", align_bytes=64)
-        quantize("far1", [layer_operand((FAR, z, 1)) for z in range(PASSES)], staging_far1[:])
+        late = [layer_operand((FAR, 1, t)) for t in (2, 3)] + [layer_operand((FAR, 0, t)) for t in (1, 2, 3)]
+        late += [layer_operand(key) for key in ((NEAR, 0, 3), (NEAR, 1, 2), (NEAR, 1, 3))]
+        quantize("late", late, staging_late[:])
         rectify(FAR, 0)
         scatter_far(0)
         multiply(FAR, 1)
         rectify(FAR, 1)
-        quantize_before_scatter(far_map(1), [(FAR, z, t) for t in (2, 3) for z in range(PASSES)])
         scatter_far(1)
 
         excess, lifted = join_tiles(0)
@@ -245,7 +260,7 @@ def tile_picked_bev_max_p_kernel(
             nc.vector.quantize_mx(
                 out=z_codes[:].bitcast(FP8X4), scales=z_scales[:], in_=woven[c][:].rearrange("p r t -> p (r t)")
             )
-            total = psum.tile([P, width], F32, name="total")
+            total = psum.tile([P, width], F32, name="total", tag="total")
             nc.tensor.matmul_mx(
                 out=total[:],
                 lhsT=w3_codes.bitcast(FP8X4),

@@ -56,23 +56,23 @@ def tile_picked_bev_max_p_kernel(
         far_maps = [keep.tile([P, S], F32, name=f"far_map{b}", align_bytes=64) for b in range(3)]
         joined = keep.tile([P, PACK, S], BF16, name="joined")
 
-        nc.vector.memset(store_scales[:].bitcast(I32), 0)
+        nc.vector.memset(store_scales[:, : T // 2].bitcast(I32), 0)
+        nc.gpsimd.memset(store_scales[:, T // 2 :].bitcast(I32), 0)
+        nc.sync.dma_start(store_words[0][:].bitcast(I32), x_words[0].bitcast(I32))
         nc.sync.dma_start(offs_sb[:], offs)
+        nc.sync.dma_start(near_sb[:], near)
         scale_rows = x_scales.bitcast(I32).rearrange("z (q j) c -> j q z c", j=4)
         for j in range(4):
             nc.sync.dma_start(store_scales[j:P:SECOND_PASS_ROW, :].bitcast(I32), scale_rows[j])
-        for z in range(PASSES):
-            nc.sync.dma_start(store_words[z][:].bitcast(I32), x_words[z].bitcast(I32))
+        nc.sync.dma_start(store_words[1][:].bitcast(I32), x_words[1].bitcast(I32))
         for z in range(PASSES):
             rows = w1[PASS_ROWS * z : PASS_ROWS * (z + 1), :]
             nc.sync.dma_start(raw_w1[z][:], rows.rearrange("(p j) c -> p j c", j=PACK))
-        nc.sync.dma_start(near_sb[:], near)
         nc.sync.dma_start(far_sb[:], far)
 
         nc.vector.memset(moved_scales[:].bitcast(I32), 0)
-        for cell_map in near_maps:
-            nc.vector.memset(cell_map[:, :S].bitcast(I32), 0)
-        for cell_map in far_maps:
+        nc.vector.memset(near_maps[0][:].bitcast(I32), 0)
+        for cell_map in near_maps[1:] + far_maps:
             nc.scalar.copy(cell_map[:, :S], near_maps[0][:, :S])
 
         nc.vector.tensor_copy(picked_scales[:], store_scales[:].indirect(offs_sb[:]))
@@ -167,10 +167,10 @@ def tile_picked_bev_max_p_kernel(
                 nc.gpsimd.tensor_tensor(joined[:, t, cols], lifted[:, cols], far_map(t)[:, cols], ADD)
 
         pick(NEAR, 0, keep.tile([P, V], U16, name="words_near0", align_bytes=64))
-        pick(NEAR, 1, after_scales.tile([P, V], U16, name="words_near1", align_bytes=64, offset=2560))
+        pick(NEAR, 1, keep.tile([P, V], U16, name="words_near1", align_bytes=64))
         quantize_alone((NEAR, 0, 0), "staging_000")
         quantize_alone((NEAR, 0, 1), "staging_001")
-        pick(FAR, 0, keep.tile([P, V], U16, name="words_far0", tag="staging_001", align_bytes=64))
+        pick(FAR, 0, after_scales.tile([P, V], U16, name="words_far0", align_bytes=64, offset=2560))
         staging_first = after_first.tile([P, PASS_ROWS], BF16, name="staging_first", align_bytes=64, offset=512)
         quantize("010", [layer_operand((NEAR, 1, 0))], staging_first[:])
         pick(FAR, 1, after_first.tile([P, V], U16, name="words_far1", align_bytes=64, offset=0))

@@ -26,6 +26,7 @@ GROUP = 8
 SECOND_PASS_ROW = 16
 LIST_COLUMNS = V // 16
 NEAR, FAR = 0, 1
+HALF = H // 2
 PSUM_BUFS = 4
 MAX_RUNS = ((0, 0), (2, 3), (1, 1), (4, 4))
 CHUNK_EDGES = (0, 256, 512, 768, 896, 1024)
@@ -42,19 +43,25 @@ def tile_picked_bev_max_p_kernel(
         keep = ctx.enter_context(tc.tile_pool(name="keep", bufs=1))
         after_scales = ctx.enter_context(tc.tile_pool(name="after_scales", bufs=1))
         after_first = ctx.enter_context(tc.tile_pool(name="after_first", bufs=1))
+        after_moves = ctx.enter_context(tc.tile_pool(name="after_moves", bufs=1))
         psum = ctx.enter_context(tc.psum_pool(name="psum", bufs=PSUM_BUFS))
 
         offs_sb = keep.tile([P, S // 16], U16, name="offs_sb")
         near_sb = keep.tile([P, LIST_COLUMNS], U16, name="near_sb")
         far_sb = keep.tile([P, LIST_COLUMNS], U16, name="far_sb")
-        store_scales = after_scales.tile([P, T], U8, name="store_scales", align_bytes=64, offset=2048)
+        scales_tile = after_scales.tile([P, 3 * T], U8, name="scales_tile", align_bytes=64, offset=8192 - 512)
+        store_scales = scales_tile[:, :T]
         picked_scales = keep.tile([P, S], U8, name="picked_scales", align_bytes=64)
         moved_scales = keep.tile([P, S], U8, name="moved_scales", align_bytes=64)
         store_words = [keep.tile([P, T], U16, name=f"store_words{z}", align_bytes=64) for z in range(PASSES)]
-        raw_w1 = [keep.tile([P, PACK, H], F32, name=f"raw_w1_{z}") for z in range(PASSES)]
+        raw_left = [
+            after_first.tile([P, PACK, HALF], F32, name=f"raw_left{z}", align_bytes=64, offset=4096 * z)
+            for z in range(PASSES)
+        ]
         near_maps = [keep.tile([P, S], F32, name=f"near_map{b}", align_bytes=64) for b in range(2)]
         far_maps = [keep.tile([P, S], F32, name=f"far_map{b}", align_bytes=64) for b in range(3)]
-        joined = keep.tile([P, PACK, S], BF16, name="joined")
+        lower = [keep.tile([P, 2, S // 2], BF16, name=f"lower{h}") for h in range(2)]
+        second = [after_moves.tile([P, S // 2], BF16, name=f"second{h}", offset=S * h) for h in range(2)]
 
         nc.vector.memset(store_scales[:, : T // 2].bitcast(I32), 0)
         nc.gpsimd.memset(store_scales[:, T // 2 :].bitcast(I32), 0)
@@ -65,30 +72,47 @@ def tile_picked_bev_max_p_kernel(
         for j in range(4):
             nc.sync.dma_start(store_scales[j:P:SECOND_PASS_ROW, :].bitcast(I32), scale_rows[j])
         nc.sync.dma_start(store_words[1][:].bitcast(I32), x_words[1].bitcast(I32))
+        w1_passes = w1.rearrange("(z p j) c -> z p j c", z=PASSES, j=PACK)
         for z in range(PASSES):
-            rows = w1[PASS_ROWS * z : PASS_ROWS * (z + 1), :]
-            nc.sync.dma_start(raw_w1[z][:], rows.rearrange("(p j) c -> p j c", j=PACK))
+            nc.sync.dma_start(raw_left[z][:], w1_passes[z][:, :, :HALF])
+        raw_right0 = keep.tile([P, PACK, HALF], F32, name="raw_right0", align_bytes=64)
+        nc.sync.dma_start(raw_right0[:], w1_passes[0][:, :, HALF:])
         nc.sync.dma_start(far_sb[:], far)
 
         nc.vector.memset(moved_scales[:].bitcast(I32), 0)
-        nc.vector.memset(near_maps[0][:].bitcast(I32), 0)
-        for cell_map in near_maps[1:] + far_maps:
+        for cell_map in near_maps:
+            nc.vector.memset(cell_map[:].bitcast(I32), 0)
+        for cell_map in far_maps:
             nc.scalar.copy(cell_map[:, :S], near_maps[0][:, :S])
 
-        nc.vector.tensor_copy(picked_scales[:], store_scales[:].indirect(offs_sb[:]))
-        nc.sync.dma_start(
-            moved_scales[0 : P - SECOND_PASS_ROW, :].bitcast(I32), picked_scales[SECOND_PASS_ROW:P, :].bitcast(I32)
-        )
-        raw_w2 = after_scales.tile([P, PASSES, PACK, H], F32, name="raw_w2", align_bytes=64, offset=3584)
+        nc.vector.tensor_copy(picked_scales[:], store_scales.indirect(offs_sb[:]))
+        for q in range(4):
+            nc.sync.dma_start(
+                moved_scales[32 * q : 32 * q + 4, :].bitcast(I32),
+                picked_scales[32 * q + SECOND_PASS_ROW : 32 * q + SECOND_PASS_ROW + 4, :].bitcast(I32),
+            )
+        raw_right1 = after_scales.tile([P, PACK, HALF], F32, name="raw_right1", align_bytes=64, offset=4096)
+        nc.sync.dma_start(raw_right1[:], w1_passes[1][:, :, HALF:])
         w2_passes = w2.rearrange("(z p j) c -> z p j c", z=PASSES, j=PACK)
-        nc.sync.dma_start(raw_w2[:, 0], w2_passes[0])
-        raw_w3 = after_scales.tile([P, PACK, N], F32, name="raw_w3", align_bytes=64, offset=512)
+        raw_far0 = after_scales.tile([P, PACK, HALF], F32, name="raw_far0", align_bytes=64, offset=8192)
+        nc.sync.dma_start(raw_far0[:], w2_passes[0][:, :, :HALF])
+        raw_late = after_scales.tile([P, PACK * (3 * HALF + N)], F32, name="raw_late", align_bytes=64, offset=12288)
+        late_halves = raw_late[:, : 3 * PACK * HALF].rearrange("p (n j c) -> p n j c", n=3, j=PACK)
+        raw_w3 = raw_late[:, 3 * PACK * HALF :].rearrange("p (t n) -> p t n", t=PACK)
+        nc.sync.dma_start(late_halves[:, 0], w2_passes[1][:, :, :HALF])
         w3_slabs = w3.rearrange("(g t q) n -> t g q n", t=PACK, q=GROUP)
         for t in range(PACK):
             nc.sync.dma_start(raw_w3[:, t, :], w3_slabs[t])
-        nc.sync.dma_start(raw_w2[:, 1], w2_passes[1])
+        for z in range(PASSES):
+            nc.sync.dma_start(late_halves[:, 1 + z], w2_passes[z][:, :, HALF:])
 
-        raw = [[raw_w1[z][:] for z in range(PASSES)], [raw_w2[:, z] for z in range(PASSES)]]
+        raw = {(NEAR, z, 0): raw_left[z][:] for z in range(PASSES)}
+        raw[NEAR, 0, 1] = raw_right0[:]
+        raw[NEAR, 1, 1] = raw_right1[:]
+        raw[FAR, 0, 0] = raw_far0[:]
+        raw[FAR, 1, 0] = late_halves[:, 0]
+        raw[FAR, 0, 1] = late_halves[:, 1]
+        raw[FAR, 1, 1] = late_halves[:, 2]
         x_scale_tiles = [picked_scales, moved_scales]
         picked_words = {}
         weights = {}
@@ -100,29 +124,39 @@ def tile_picked_bev_max_p_kernel(
             entries = offs_sb[:, LIST_COLUMNS * sensor : LIST_COLUMNS * (sensor + 1)]
             nc.vector.tensor_copy(words[:], store_words[z][:].indirect(entries))
 
-        def layer_operand(key):
-            sensor, z, t = key
-            return key, raw[sensor][z].rearrange("p j (g t h i) -> p t g h j i", t=PACK, h=2, i=PACK)[:, t]
+        def round_pair(sensor, z, c, pair, rounded):
+            values = raw[sensor, z, c].rearrange("p j (g t q) -> p t g j q", t=PACK, q=GROUP)
+            nc.scalar.copy(rounded, values[:, 2 * pair : 2 * pair + 2])
 
-        def quantize(label, operands, staging):
-            count = len(operands)
-            for n, (key, values) in enumerate(operands):
-                rounded = staging[:, PASS_ROWS * n : PASS_ROWS * (n + 1)]
-                nc.scalar.copy(rounded.rearrange("p (g h i j) -> p g h j i", h=2, i=PACK, j=PACK), values)
+        def round_low(sensor, c, staging):
+            for z in range(PASSES):
+                rounded = staging[:, PASS_ROWS * z : PASS_ROWS * (z + 1)]
+                round_pair(sensor, z, c, 0, rounded.rearrange("p (u g q j) -> p u g j q", u=2, q=GROUP, j=PACK))
+
+        def round_high(sensor, z, c, staging):
+            rounded = staging[:].rearrange("p (z u c g q j) -> p z c u g j q", z=PASSES, u=2, c=2, q=GROUP, j=PACK)
+            round_pair(sensor, z, c, 1, rounded[:, z, c])
+
+        def quantize(label, keys, staging):
+            count = len(keys)
             codes = keep.tile([P, P * count], U32, name=f"codes_{label}", align_bytes=64)
             scales = keep.tile([P, P * count], U8, name=f"scales_{label}", align_bytes=64)
-            nc.vector.quantize_mx(out=codes[:].bitcast(FP8X4), scales=scales[:], in_=staging[:, : PASS_ROWS * count])
-            for n, (key, values) in enumerate(operands):
+            nc.vector.quantize_mx(out=codes[:].bitcast(FP8X4), scales=scales[:], in_=staging)
+            for n, key in enumerate(keys):
                 weights[key] = (codes[:, P * n : P * (n + 1)], scales[:, P * n : P * (n + 1)])
 
-        def quantize_alone(key, tag):
-            staging = keep.tile([P, PASS_ROWS], BF16, name=tag, tag=tag, align_bytes=64)
-            quantize("%d%d%d" % key, [layer_operand(key)], staging[:])
+        def quantize_low(sensor, c):
+            staging = keep.tile([P, PASSES * PASS_ROWS], BF16, name=f"staging_low{sensor}{c}", align_bytes=64)
+            round_low(sensor, c, staging)
+            quantize(f"low{sensor}{c}", [(sensor, z, c) for z in range(PASSES)], staging[:])
+
+        def quantize_high(sensor, staging):
+            quantize(f"high{sensor}", [(sensor, z, t) for z in range(PASSES) for t in (2, 3)], staging[:])
 
         def multiply(sensor, t):
             acc = psum.tile([P, V], F32, name="acc")
             sums[sensor, t] = acc
-            order = (0, 1) if t < 2 else (1, 0)
+            order = (0, 1)
             for z in order:
                 codes, scales = weights[sensor, z, t]
                 nc.tensor.matmul_mx(
@@ -136,7 +170,12 @@ def tile_picked_bev_max_p_kernel(
                 )
 
         def rectify(sensor, t):
-            results[sensor, t] = keep.tile([P, V], F32, name=f"result{sensor}{t}", align_bytes=64)
+            if (sensor, t) == (NEAR, 1):
+                results[sensor, t] = after_scales.tile([P, V], F32, name="result01", align_bytes=64, offset=8192)
+            elif (sensor, t) == (FAR, 0):
+                results[sensor, t] = after_scales.tile([P, V], F32, name="result10", align_bytes=64, offset=16384)
+            else:
+                results[sensor, t] = keep.tile([P, V], F32, name=f"result{sensor}{t}", align_bytes=64)
             nc.scalar.activation(results[sensor, t][:], sums[sensor, t][:], RELU)
 
         def near_map(t):
@@ -163,54 +202,54 @@ def tile_picked_bev_max_p_kernel(
             nc.scalar.activation(lifted[:, cols], excess[:, cols], RELU)
 
         def settle(t, lifted):
-            for cols in halves:
-                nc.gpsimd.tensor_tensor(joined[:, t, cols], lifted[:, cols], far_map(t)[:, cols], ADD)
+            for h, cols in enumerate(halves):
+                target = upper[:, 0, cols] if t == 2 else (lower[h][:, 0, :], second[h][:])[t]
+                nc.gpsimd.tensor_tensor(target, lifted[:, cols], far_map(t)[:, cols], ADD)
+                if t == 1:
+                    nc.sync.dma_start(lower[h][P // 2 :, 0, :], second[h][: P // 2, :])
+                    nc.sync.dma_start(lower[h][P // 2 :, 1, :], second[h][P // 2 :, :])
+                if t == 0:
+                    nc.sync.dma_start(lower[h][: P // 2, 1, :], lower[h][P // 2 :, 0, :])
 
+        staging_high = [
+            keep.tile([P, 2 * PASSES * PASS_ROWS], BF16, name=f"staging_high{sensor}", align_bytes=64)
+            for sensor in (NEAR, FAR)
+        ]
         pick(NEAR, 0, keep.tile([P, V], U16, name="words_near0", align_bytes=64))
         pick(NEAR, 1, keep.tile([P, V], U16, name="words_near1", align_bytes=64))
-        quantize_alone((NEAR, 0, 0), "staging_000")
-        quantize_alone((NEAR, 0, 1), "staging_001")
-        pick(FAR, 0, after_scales.tile([P, V], U16, name="words_far0", align_bytes=64, offset=2560))
-        staging_first = after_first.tile([P, PASS_ROWS], BF16, name="staging_first", align_bytes=64, offset=512)
-        quantize("010", [layer_operand((NEAR, 1, 0))], staging_first[:])
-        pick(FAR, 1, after_first.tile([P, V], U16, name="words_far1", align_bytes=64, offset=0))
-        first_sums = [psum.tile([P, P], F32, name=f"first_sums{n}", tag="total") for n in range(V // P)]
+        quantize_low(NEAR, 0)
         for z in range(PASSES):
-            codes, scales = weights[NEAR, z, 0]
-            for n, acc in enumerate(first_sums):
-                nc.tensor.matmul_mx(
-                    out=acc[:],
-                    lhsT=codes.bitcast(FP8X4),
-                    lhsT_scale=scales,
-                    rhs=picked_words[NEAR, z][:, P * n : P * (n + 1)].bitcast(FP4X4),
-                    rhs_scale=x_scale_tiles[z][:, P * n : P * (n + 1)],
-                    start=(z == 0),
-                    stop=(z == PASSES - 1),
-                )
-        first_head = keep.tile([P, P], F32, name="first_head", align_bytes=64)
-        first_rest = keep.tile([P, V - P], F32, name="first_rest", align_bytes=64)
-        nc.scalar.activation(first_head[:], first_sums[0][:], RELU)
-        for n in range(1, V // P):
-            nc.scalar.activation(first_rest[:, P * (n - 1) : P * n], first_sums[n][:], RELU)
-        nc.vector.tensor_copy(near_map(0)[:].indirect(near_sb[:, : P // 16]), first_head[:])
-        quantize_alone((NEAR, 1, 1), "staging_011")
-        nc.vector.tensor_copy(near_map(0)[:].indirect(near_sb[:, P // 16 :]), first_rest[:])
+            round_high(NEAR, z, 0, staging_high[NEAR])
+        pick(FAR, 0, after_first.tile([P, V], U16, name="words_far0", align_bytes=64, offset=4096))
+        pick(FAR, 1, after_first.tile([P, V], U16, name="words_far1", align_bytes=64, offset=5120))
+        multiply(NEAR, 0)
+        first_head = keep.tile([P, V // 2], F32, name="first_head", align_bytes=64)
+        nc.scalar.activation(first_head[:], sums[NEAR, 0][:, : V // 2], RELU)
+        nc.vector.tensor_copy(near_map(0)[:].indirect(near_sb[:, : LIST_COLUMNS // 2]), first_head[:])
+        quantize_low(NEAR, 1)
+        for z in range(PASSES):
+            round_high(NEAR, z, 1, staging_high[NEAR])
+        quantize_high(NEAR, staging_high[NEAR])
         multiply(NEAR, 1)
-
+        first_rest = after_scales.tile([P, V // 2], F32, name="first_rest", align_bytes=64, offset=4096)
+        nc.scalar.activation(first_rest[:], sums[NEAR, 0][:, V // 2 :], RELU)
+        nc.vector.tensor_copy(near_map(0)[:].indirect(near_sb[:, LIST_COLUMNS // 2 :]), first_rest[:])
+        quantize_low(FAR, 0)
+        round_high(FAR, 0, 0, staging_high[FAR])
         rectify(NEAR, 1)
         scatter_near(1)
-        quantize_alone((NEAR, 0, 2), "staging_002")
-        quantize_alone((FAR, 0, 0), "staging_100")
-        quantize_alone((FAR, 1, 0), "staging_110")
         multiply(FAR, 0)
-        staging_late = after_first.tile([P, 8 * PASS_ROWS], BF16, name="staging_late", align_bytes=64, offset=1024)
-        staging_next = keep.tile([P, 2 * PASS_ROWS], BF16, name="staging_next", align_bytes=64)
-        w3_values = raw_w3[:].rearrange("p t (g h i) -> p g h t i", h=2, i=PACK)
-        quantize("next", [layer_operand((FAR, 1, 1)), ("w3", w3_values)], staging_next[:])
+        quantize_low(FAR, 1)
+        staging_w3 = keep.tile([P, PASS_ROWS], BF16, name="staging_w3", align_bytes=64)
+        nc.scalar.copy(
+            staging_w3[:].rearrange("p (g h i t) -> p g h t i", h=2, i=PACK, t=PACK),
+            raw_w3.rearrange("p t (g h i) -> p g h t i", h=2, i=PACK),
+        )
+        quantize("w3", ["w3"], staging_w3[:])
         w3_codes, w3_scales = weights["w3"]
-        late = [layer_operand((FAR, 1, t)) for t in (2, 3)] + [layer_operand((FAR, 0, t)) for t in (1, 2, 3)]
-        late += [layer_operand(key) for key in ((NEAR, 0, 3), (NEAR, 1, 2), (NEAR, 1, 3))]
-        quantize("late", late, staging_late[:])
+        for z, c in ((1, 0), (0, 1), (1, 1)):
+            round_high(FAR, z, c, staging_high[FAR])
+        quantize_high(FAR, staging_high[FAR])
         rectify(FAR, 0)
         scatter_far(0)
         multiply(FAR, 1)
@@ -228,6 +267,7 @@ def tile_picked_bev_max_p_kernel(
             multiply(sensor, t)
             rectify(sensor, t)
         scatter_far(2)
+        upper = after_moves.tile([P, 2, S], BF16, name="upper", offset=S)
         for t in (1, 2):
             excess, lifted = join_tiles(t)
             for cols in halves:
@@ -240,19 +280,21 @@ def tile_picked_bev_max_p_kernel(
             for c, cols in enumerate(chunks)
         ]
         for c, cols in enumerate(chunks):
-            nc.scalar.copy(woven[c][:, :, 0:2], joined[:, 0:2, cols].rearrange("p t r -> p r t"))
+            h, start = divmod(cols.start, S // 2)
+            inside = slice(start, start + cols.stop - cols.start)
+            nc.scalar.copy(woven[c][:, :, 0:2], lower[h][:, :, inside].rearrange("p t r -> p r t"))
         scatter_near(3)
         scatter_far(3)
 
         for first, last in MAX_RUNS:
             cols = slice(chunks[first].start, chunks[last].stop)
-            nc.vector.tensor_tensor(joined[:, 3, cols], near_map(3)[:, cols], far_map(3)[:, cols], MAX)
+            nc.vector.tensor_tensor(upper[:, 1, cols], near_map(3)[:, cols], far_map(3)[:, cols], MAX)
         for c, cols in enumerate(chunks):
-            upper = joined[:, 2:4, cols].rearrange("p t r -> p r t")
+            pairs = upper[:, :, cols].rearrange("p t r -> p r t")
             if c in VECTOR_WEAVES:
-                nc.vector.tensor_copy(woven[c][:, :, 2:4], upper)
+                nc.vector.tensor_copy(woven[c][:, :, 2:4], pairs)
             else:
-                nc.scalar.copy(woven[c][:, :, 2:4], upper)
+                nc.scalar.copy(woven[c][:, :, 2:4], pairs)
         for c in FINISH_ORDER:
             width = chunks[c].stop - chunks[c].start
             z_codes = keep.tile([P, width], U32, name=f"z_codes{c}", align_bytes=64)

@@ -217,14 +217,30 @@ def tile_picked_bev_max_p_kernel(
         ]
         pick(NEAR, 0, keep.tile([P, V], U16, name="words_near0", align_bytes=64))
         pick(NEAR, 1, keep.tile([P, V], U16, name="words_near1", align_bytes=64))
-        quantize_low(NEAR, 0)
+        staging_first = keep.tile([P, PASSES * PASS_ROWS], BF16, name="staging_first", align_bytes=64)
+        round_low(NEAR, 0, staging_first)
         for z in range(PASSES):
-            round_high(NEAR, z, 0, staging_high[NEAR])
-        pick(FAR, 0, after_first.tile([P, V], U16, name="words_far0", align_bytes=64, offset=4096))
+            quantize(f"first{z}", [(NEAR, z, 0)], staging_first[:, PASS_ROWS * z : PASS_ROWS * (z + 1)])
+        round_high(NEAR, 0, 0, staging_high[NEAR])
+        pick(FAR, 0, after_first.tile([P, V], U16, name="words_far0", align_bytes=64, offset=0))
+        round_high(NEAR, 1, 0, staging_high[NEAR])
         pick(FAR, 1, after_first.tile([P, V], U16, name="words_far1", align_bytes=64, offset=5120))
-        multiply(NEAR, 0)
+        first_sums = [psum.tile([P, P], F32, name=f"first_sums{n}", tag="total") for n in range(V // P)]
+        for z in range(PASSES):
+            codes, scales = weights[NEAR, z, 0]
+            for n, acc in enumerate(first_sums):
+                nc.tensor.matmul_mx(
+                    out=acc[:],
+                    lhsT=codes.bitcast(FP8X4),
+                    lhsT_scale=scales,
+                    rhs=picked_words[NEAR, z][:, P * n : P * (n + 1)].bitcast(FP4X4),
+                    rhs_scale=x_scale_tiles[z][:, P * n : P * (n + 1)],
+                    start=(z == 0),
+                    stop=(z == PASSES - 1),
+                )
         first_head = keep.tile([P, V // 2], F32, name="first_head", align_bytes=64)
-        nc.scalar.activation(first_head[:], sums[NEAR, 0][:, : V // 2], RELU)
+        for n in range(2):
+            nc.scalar.activation(first_head[:, P * n : P * (n + 1)], first_sums[n][:], RELU)
         nc.vector.tensor_copy(near_map(0)[:].indirect(near_sb[:, : LIST_COLUMNS // 2]), first_head[:])
         quantize_low(NEAR, 1)
         for z in range(PASSES):
@@ -232,7 +248,8 @@ def tile_picked_bev_max_p_kernel(
         quantize_high(NEAR, staging_high[NEAR])
         multiply(NEAR, 1)
         first_rest = after_scales.tile([P, V // 2], F32, name="first_rest", align_bytes=64, offset=4096)
-        nc.scalar.activation(first_rest[:], sums[NEAR, 0][:, V // 2 :], RELU)
+        for n in range(2):
+            nc.scalar.activation(first_rest[:, P * n : P * (n + 1)], first_sums[2 + n][:], RELU)
         nc.vector.tensor_copy(near_map(0)[:].indirect(near_sb[:, LIST_COLUMNS // 2 :]), first_rest[:])
         quantize_low(FAR, 0)
         round_high(FAR, 0, 0, staging_high[FAR])

@@ -43,7 +43,7 @@ def tile_picked_bev_max_p_kernel(
         keep = ctx.enter_context(tc.tile_pool(name="keep", bufs=1))
         after_scales = ctx.enter_context(tc.tile_pool(name="after_scales", bufs=1))
         after_first = ctx.enter_context(tc.tile_pool(name="after_first", bufs=1))
-        after_moves = ctx.enter_context(tc.tile_pool(name="after_moves", bufs=1))
+        after_joins = ctx.enter_context(tc.tile_pool(name="after_joins", bufs=1))
         psum = ctx.enter_context(tc.psum_pool(name="psum", bufs=PSUM_BUFS))
 
         offs_sb = keep.tile([P, S // 16], U16, name="offs_sb")
@@ -59,9 +59,11 @@ def tile_picked_bev_max_p_kernel(
             for z in range(PASSES)
         ]
         near_maps = [keep.tile([P, S], F32, name=f"near_map{b}", align_bytes=64) for b in range(2)]
-        far_maps = [keep.tile([P, S], F32, name=f"far_map{b}", align_bytes=64) for b in range(3)]
+        far_maps = [after_joins.tile([P, S], F32, name=f"far_map{b}", align_bytes=64, offset=4 * S * b) for b in range(3)]
         lower = [keep.tile([P, 2, S // 2], BF16, name=f"lower{h}") for h in range(2)]
-        second = [after_moves.tile([P, S // 2], BF16, name=f"second{h}", offset=S * h) for h in range(2)]
+        upper_tile = keep.tile([P, 3 * S], BF16, name="upper_tile")
+        upper = upper_tile[:, : 2 * S].rearrange("p (t r) -> p t r", t=2)
+        second = [upper_tile[:, S // 2 * (1 - h) : S // 2 * (2 - h)] for h in range(2)]
 
         nc.vector.memset(store_scales[:, : T // 2].bitcast(I32), 0)
         nc.gpsimd.memset(store_scales[:, T // 2 :].bitcast(I32), 0)
@@ -96,15 +98,15 @@ def tile_picked_bev_max_p_kernel(
         w2_passes = w2.rearrange("(z p j) c -> z p j c", z=PASSES, j=PACK)
         raw_far0 = after_scales.tile([P, PACK, HALF], F32, name="raw_far0", align_bytes=64, offset=8192)
         nc.sync.dma_start(raw_far0[:], w2_passes[0][:, :, :HALF])
-        raw_late = after_scales.tile([P, PACK * (3 * HALF + N)], F32, name="raw_late", align_bytes=64, offset=12288)
-        late_halves = raw_late[:, : 3 * PACK * HALF].rearrange("p (n j c) -> p n j c", n=3, j=PACK)
-        raw_w3 = raw_late[:, 3 * PACK * HALF :].rearrange("p (t n) -> p t n", t=PACK)
+        raw_late = after_scales.tile([P, PACK * 3 * HALF], F32, name="raw_late", align_bytes=64, offset=12288)
+        late_halves = raw_late[:].rearrange("p (n j c) -> p n j c", n=3, j=PACK)
         nc.sync.dma_start(late_halves[:, 0], w2_passes[1][:, :, :HALF])
+        for z in range(PASSES):
+            nc.sync.dma_start(late_halves[:, 1 + z], w2_passes[z][:, :, HALF:])
+        raw_w3 = after_first.tile([P, PACK, N], F32, name="raw_w3", align_bytes=64, offset=6144)
         w3_slabs = w3.rearrange("(g t q) n -> t g q n", t=PACK, q=GROUP)
         for t in range(PACK):
             nc.sync.dma_start(raw_w3[:, t, :], w3_slabs[t])
-        for z in range(PASSES):
-            nc.sync.dma_start(late_halves[:, 1 + z], w2_passes[z][:, :, HALF:])
 
         raw = {(NEAR, z, 0): raw_left[z][:] for z in range(PASSES)}
         raw[NEAR, 0, 1] = raw_right0[:]
@@ -194,6 +196,8 @@ def tile_picked_bev_max_p_kernel(
 
         def join_tiles(t):
             excess = keep.tile([P, S], F32, name=f"excess{t}", tag=f"join{t % 2}")
+            if t == 2:
+                return excess, upper_tile[:, S:].bitcast(F32)
             lifted = keep.tile([P, S], F32, name=f"lifted{t}", tag=f"join{(t + 1) % 2}")
             return excess, lifted
 
@@ -202,8 +206,9 @@ def tile_picked_bev_max_p_kernel(
             nc.scalar.activation(lifted[:, cols], excess[:, cols], RELU)
 
         def settle(t, lifted):
-            for h, cols in enumerate(halves):
-                target = upper[:, 0, cols] if t == 2 else (lower[h][:, 0, :], second[h][:])[t]
+            for h in (1, 0) if t == 2 else (0, 1):
+                cols = halves[h]
+                target = upper[:, 0, cols] if t == 2 else (lower[h][:, 0, :], second[h])[t]
                 nc.gpsimd.tensor_tensor(target, lifted[:, cols], far_map(t)[:, cols], ADD)
                 if t == 1:
                     nc.sync.dma_start(lower[h][P // 2 :, 0, :], second[h][: P // 2, :])
@@ -257,13 +262,6 @@ def tile_picked_bev_max_p_kernel(
         scatter_near(1)
         multiply(FAR, 0)
         quantize_low(FAR, 1)
-        staging_w3 = keep.tile([P, PASS_ROWS], BF16, name="staging_w3", align_bytes=64)
-        nc.scalar.copy(
-            staging_w3[:].rearrange("p (g h i t) -> p g h t i", h=2, i=PACK, t=PACK),
-            raw_w3.rearrange("p t (g h i) -> p g h t i", h=2, i=PACK),
-        )
-        quantize("w3", ["w3"], staging_w3[:])
-        w3_codes, w3_scales = weights["w3"]
         for z, c in ((1, 0), (0, 1), (1, 1)):
             round_high(FAR, z, c, staging_high[FAR])
         quantize_high(FAR, staging_high[FAR])
@@ -272,6 +270,11 @@ def tile_picked_bev_max_p_kernel(
         multiply(FAR, 1)
         rectify(FAR, 1)
         scatter_far(1)
+        staging_w3 = keep.tile([P, PASS_ROWS], BF16, name="staging_w3", align_bytes=64)
+        nc.scalar.copy(
+            staging_w3[:].rearrange("p (g h i t) -> p g h t i", h=2, i=PACK, t=PACK),
+            raw_w3[:].rearrange("p t (g h i) -> p g h t i", h=2, i=PACK),
+        )
 
         excess, lifted = join_tiles(0)
         lift(0, excess, lifted, halves[0])
@@ -284,10 +287,9 @@ def tile_picked_bev_max_p_kernel(
             multiply(sensor, t)
             rectify(sensor, t)
         scatter_far(2)
-        upper = after_moves.tile([P, 2, S], BF16, name="upper", offset=S)
         for t in (1, 2):
             excess, lifted = join_tiles(t)
-            for cols in halves:
+            for cols in halves[::-1] if t == 2 else halves:
                 lift(t, excess, lifted, cols)
             settle(t, lifted)
 
@@ -302,6 +304,9 @@ def tile_picked_bev_max_p_kernel(
             nc.scalar.copy(woven[c][:, :, 0:2], lower[h][:, :, inside].rearrange("p t r -> p r t"))
         scatter_near(3)
         scatter_far(3)
+        w3_codes = after_joins.tile([P, P], U32, name="w3_codes", align_bytes=64, offset=8 * S)
+        w3_scales = after_joins.tile([P, P], U8, name="w3_scales", align_bytes=64, offset=8 * S + 512)
+        nc.vector.quantize_mx(out=w3_codes[:].bitcast(FP8X4), scales=w3_scales[:], in_=staging_w3[:])
 
         for first, last in MAX_RUNS:
             cols = slice(chunks[first].start, chunks[last].stop)
@@ -322,8 +327,8 @@ def tile_picked_bev_max_p_kernel(
             total = psum.tile([P, width], F32, name="total", tag="total")
             nc.tensor.matmul_mx(
                 out=total[:],
-                lhsT=w3_codes.bitcast(FP8X4),
-                lhsT_scale=w3_scales,
+                lhsT=w3_codes[:].bitcast(FP8X4),
+                lhsT_scale=w3_scales[:],
                 rhs=z_codes[:].bitcast(FP8X4),
                 rhs_scale=z_scales[:],
                 start=True,

@@ -14,23 +14,23 @@ U8 = mybir.dt.uint8
 FP8X4 = mybir.dt.float8_e4m3fn_x4
 FP4X4 = mybir.dt.float4_e2m1fn_x4
 RELU = mybir.ActivationFunctionType.Relu
+COPY = mybir.ActivationFunctionType.Copy
 MAX = mybir.AluOpType.max
-ADD = mybir.AluOpType.add
-SUBTRACT = mybir.AluOpType.subtract
 
 P = 128
 PACK = 4
 PASS_ROWS = P * PACK
 PASSES = K // PASS_ROWS
-GROUP = 8
+RUN = 4
 SECOND_PASS_ROW = 16
 LIST_COLUMNS = V // 16
 NEAR, FAR = 0, 1
 HALF = H // 2
-PSUM_BUFS = 4
-MAX_RUNS = ((0, 0), (2, 3), (1, 1), (4, 4))
+PIECE = PACK * HALF
+SHARED_ENTRIES = 128
 CHUNK_EDGES = (0, 256, 512, 768, 896, 1024)
-VECTOR_WEAVES = (2, 3)
+MAX_RUNS = ((0, 0), (1, 1), (2, 4))
+VECTOR_WEAVES = (2, 3, 4)
 FINISH_ORDER = (0, 2, 1, 3, 4)
 VECTOR_EMPTIES = (3, 4)
 
@@ -41,103 +41,97 @@ def tile_picked_bev_max_p_kernel(
     nc = tc.nc
     with ExitStack() as ctx:
         keep = ctx.enter_context(tc.tile_pool(name="keep", bufs=1))
-        after_scales = ctx.enter_context(tc.tile_pool(name="after_scales", bufs=1))
         after_first = ctx.enter_context(tc.tile_pool(name="after_first", bufs=1))
-        after_joins = ctx.enter_context(tc.tile_pool(name="after_joins", bufs=1))
-        psum = ctx.enter_context(tc.psum_pool(name="psum", bufs=PSUM_BUFS))
+        after_left = ctx.enter_context(tc.tile_pool(name="after_left", bufs=1))
+        after_staging = ctx.enter_context(tc.tile_pool(name="after_staging", bufs=1))
+        psum = ctx.enter_context(tc.psum_pool(name="psum", bufs=1))
 
         offs_sb = keep.tile([P, S // 16], U16, name="offs_sb")
         near_sb = keep.tile([P, LIST_COLUMNS], U16, name="near_sb")
         far_sb = keep.tile([P, LIST_COLUMNS], U16, name="far_sb")
-        scales_tile = after_scales.tile([P, 3 * T], U8, name="scales_tile", align_bytes=64, offset=8192 - 512)
-        store_scales = scales_tile[:, :T]
+        lists = [near_sb, far_sb]
+        store_scales = after_first.tile([P, T], U8, name="store_scales", align_bytes=64, offset=0)
         picked_scales = keep.tile([P, S], U8, name="picked_scales", align_bytes=64)
+        raw_right = keep.tile([P, PACK, HALF], F32, name="raw_right", align_bytes=64)
         moved_scales = keep.tile([P, S], U8, name="moved_scales", align_bytes=64)
         store_words = [keep.tile([P, T], U16, name=f"store_words{z}", align_bytes=64) for z in range(PASSES)]
         raw_left = [
-            after_first.tile([P, PACK, HALF], F32, name=f"raw_left{z}", align_bytes=64, offset=4096 * z)
+            after_left.tile([P, PACK, HALF], F32, name=f"raw_left{z}", align_bytes=64, offset=4 * PIECE * z)
             for z in range(PASSES)
         ]
-        near_maps = [keep.tile([P, S], F32, name=f"near_map{b}", align_bytes=64) for b in range(2)]
-        far_maps = [after_joins.tile([P, S], F32, name=f"far_map{b}", align_bytes=64, offset=4 * S * b) for b in range(3)]
-        lower = [keep.tile([P, 2, S // 2], BF16, name=f"lower{h}") for h in range(2)]
-        upper_tile = keep.tile([P, 3 * S], BF16, name="upper_tile")
-        upper = upper_tile[:, : 2 * S].rearrange("p (t r) -> p t r", t=2)
-        second = [upper_tile[:, S // 2 * (1 - h) : S // 2 * (2 - h)] for h in range(2)]
+        maps = {}
+        for key in ((NEAR, 0), (NEAR, 1), (FAR, 3), (FAR, 0), (FAR, 1), (NEAR, 2)):
+            maps[key] = keep.tile([P, S], F32, name=f"map{key[0]}{key[1]}", align_bytes=64)
 
         nc.vector.memset(store_scales[:, : T // 2].bitcast(I32), 0)
         nc.gpsimd.memset(store_scales[:, T // 2 :].bitcast(I32), 0)
-        nc.sync.dma_start(store_words[0][:].bitcast(I32), x_words[0].bitcast(I32))
+        w1_passes = w1.rearrange("(z p j) c -> z p j c", z=PASSES, j=PACK)
+        w2_passes = w2.rearrange("(z p j) c -> z p j c", z=PASSES, j=PACK)
         nc.sync.dma_start(offs_sb[:], offs)
         nc.sync.dma_start(near_sb[:], near)
+        nc.sync.dma_start(raw_left[0][:], w1_passes[0][:, :, :HALF])
         scale_rows = x_scales.bitcast(I32).rearrange("z (q j) c -> j q z c", j=4)
         for j in range(4):
             nc.sync.dma_start(store_scales[j:P:SECOND_PASS_ROW, :].bitcast(I32), scale_rows[j])
-        nc.sync.dma_start(store_words[1][:].bitcast(I32), x_words[1].bitcast(I32))
-        w1_passes = w1.rearrange("(z p j) c -> z p j c", z=PASSES, j=PACK)
         for z in range(PASSES):
-            nc.sync.dma_start(raw_left[z][:], w1_passes[z][:, :, :HALF])
-        raw_right0 = keep.tile([P, PACK, HALF], F32, name="raw_right0", align_bytes=64)
-        nc.sync.dma_start(raw_right0[:], w1_passes[0][:, :, HALF:])
+            nc.sync.dma_start(store_words[z][:].bitcast(I32), x_words[z].bitcast(I32))
+        nc.sync.dma_start(raw_left[1][:], w1_passes[1][:, :, :HALF])
+        nc.sync.dma_start(raw_right[:], w1_passes[0][:, :, HALF:])
         nc.sync.dma_start(far_sb[:], far)
 
-        nc.vector.memset(moved_scales[:].bitcast(I32), 0)
-        for cell_map in near_maps:
-            nc.vector.memset(cell_map[:].bitcast(I32), 0)
-        for cell_map in far_maps:
-            nc.scalar.copy(cell_map[:, :S], near_maps[0][:, :S])
+        nc.vector.memset(maps[FAR, 3][:].bitcast(I32), 0)
+        nc.gpsimd.memset(moved_scales[:].bitcast(I32), 0)
+        for key in ((NEAR, 0), (NEAR, 1), (NEAR, 2)):
+            nc.vector.tensor_copy(maps[key][:], maps[FAR, 3][:])
+        for key in ((FAR, 0), (FAR, 1)):
+            nc.scalar.activation(maps[key][:], maps[FAR, 3][:], RELU)
 
-        nc.vector.tensor_copy(picked_scales[:], store_scales.indirect(offs_sb[:]))
+        nc.vector.tensor_copy(picked_scales[:], store_scales[:].indirect(offs_sb[:]))
         for q in range(4):
             nc.sync.dma_start(
                 moved_scales[32 * q : 32 * q + 4, :].bitcast(I32),
                 picked_scales[32 * q + SECOND_PASS_ROW : 32 * q + SECOND_PASS_ROW + 4, :].bitcast(I32),
             )
-        raw_right1 = after_scales.tile([P, PACK, HALF], F32, name="raw_right1", align_bytes=64, offset=4096)
-        nc.sync.dma_start(raw_right1[:], w1_passes[1][:, :, HALF:])
-        w2_passes = w2.rearrange("(z p j) c -> z p j c", z=PASSES, j=PACK)
-        raw_far0 = after_scales.tile([P, PACK, HALF], F32, name="raw_far0", align_bytes=64, offset=8192)
-        nc.sync.dma_start(raw_far0[:], w2_passes[0][:, :, :HALF])
-        raw_late = after_scales.tile([P, PACK * 3 * HALF], F32, name="raw_late", align_bytes=64, offset=12288)
-        late_halves = raw_late[:].rearrange("p (n j c) -> p n j c", n=3, j=PACK)
-        nc.sync.dma_start(late_halves[:, 0], w2_passes[1][:, :, :HALF])
-        for z in range(PASSES):
-            nc.sync.dma_start(late_halves[:, 1 + z], w2_passes[z][:, :, HALF:])
-        raw_w3 = after_first.tile([P, PACK, N], F32, name="raw_w3", align_bytes=64, offset=6144)
-        w3_slabs = w3.rearrange("(g t q) n -> t g q n", t=PACK, q=GROUP)
+        raw_late = after_first.tile([P, 5 * PIECE + PACK * N], F32, name="raw_late", align_bytes=64, offset=0)
+        raw = {(NEAR, z, 0): raw_left[z][:] for z in range(PASSES)}
+        raw[NEAR, 0, 1] = raw_right[:]
+        late_keys = [(NEAR, 1, 1)] + [(FAR, z, c) for c in range(2) for z in range(PASSES)]
+        for n, (sensor, z, c) in enumerate(late_keys):
+            raw[sensor, z, c] = raw_late[:, PIECE * n : PIECE * (n + 1)].rearrange("p (j c) -> p j c", j=PACK)
+            source = (w1_passes, w2_passes)[sensor][z]
+            nc.sync.dma_start(raw[sensor, z, c], source[:, :, HALF * c : HALF * (c + 1)])
+        raw_w3 = raw_late[:, 5 * PIECE :].rearrange("p (t n) -> p t n", t=PACK)
+        w3_slabs = w3.rearrange("(g t i) n -> t g i n", t=PACK, i=RUN)
         for t in range(PACK):
             nc.sync.dma_start(raw_w3[:, t, :], w3_slabs[t])
 
-        raw = {(NEAR, z, 0): raw_left[z][:] for z in range(PASSES)}
-        raw[NEAR, 0, 1] = raw_right0[:]
-        raw[NEAR, 1, 1] = raw_right1[:]
-        raw[FAR, 0, 0] = raw_far0[:]
-        raw[FAR, 1, 0] = late_halves[:, 0]
-        raw[FAR, 0, 1] = late_halves[:, 1]
-        raw[FAR, 1, 1] = late_halves[:, 2]
-        x_scale_tiles = [picked_scales, moved_scales]
         picked_words = {}
         weights = {}
         sums = {}
         results = {}
+
+        def copy_on(engine, target, source):
+            if engine is nc.scalar:
+                nc.scalar.copy(target, source)
+            else:
+                engine.tensor_copy(target, source)
 
         def pick(sensor, z, words):
             picked_words[sensor, z] = words
             entries = offs_sb[:, LIST_COLUMNS * sensor : LIST_COLUMNS * (sensor + 1)]
             nc.vector.tensor_copy(words[:], store_words[z][:].indirect(entries))
 
-        def round_pair(sensor, z, c, pair, rounded):
-            values = raw[sensor, z, c].rearrange("p j (g t q) -> p t g j q", t=PACK, q=GROUP)
-            nc.scalar.copy(rounded, values[:, 2 * pair : 2 * pair + 2])
+        def round_pair(engine, sensor, z, c, pair, rounded):
+            values = raw[sensor, z, c].rearrange("p j (g t i) -> p t g j i", t=PACK, i=RUN)
+            copy_on(engine, rounded, values[:, 2 * pair : 2 * pair + 2])
 
-        def round_low(sensor, c, staging):
-            for z in range(PASSES):
-                rounded = staging[:, PASS_ROWS * z : PASS_ROWS * (z + 1)]
-                round_pair(sensor, z, c, 0, rounded.rearrange("p (u g q j) -> p u g j q", u=2, q=GROUP, j=PACK))
+        def round_low(engine, sensor, z, c, staging):
+            rounded = staging[:, PASS_ROWS * z : PASS_ROWS * (z + 1)]
+            round_pair(engine, sensor, z, c, 0, rounded.rearrange("p (u g i j) -> p u g j i", u=2, i=RUN, j=PACK))
 
-        def round_high(sensor, z, c, staging):
-            rounded = staging[:].rearrange("p (z u c g q j) -> p z c u g j q", z=PASSES, u=2, c=2, q=GROUP, j=PACK)
-            round_pair(sensor, z, c, 1, rounded[:, z, c])
+        def round_high(engine, sensor, z, c, staging):
+            rounded = staging[:].rearrange("p (z u c g i j) -> p z c u g j i", z=PASSES, u=2, c=2, i=RUN, j=PACK)
+            round_pair(engine, sensor, z, c, 1, rounded[:, z, c])
 
         def quantize(label, keys, staging):
             count = len(keys)
@@ -147,184 +141,159 @@ def tile_picked_bev_max_p_kernel(
             for n, key in enumerate(keys):
                 weights[key] = (codes[:, P * n : P * (n + 1)], scales[:, P * n : P * (n + 1)])
 
-        def quantize_low(sensor, c):
-            staging = keep.tile([P, PASSES * PASS_ROWS], BF16, name=f"staging_low{sensor}{c}", align_bytes=64)
-            round_low(sensor, c, staging)
+        def quantize_low(sensor, c, staging):
             quantize(f"low{sensor}{c}", [(sensor, z, c) for z in range(PASSES)], staging[:])
 
         def quantize_high(sensor, staging):
             quantize(f"high{sensor}", [(sensor, z, t) for z in range(PASSES) for t in (2, 3)], staging[:])
 
         def multiply(sensor, t):
-            acc = psum.tile([P, V], F32, name="acc")
-            sums[sensor, t] = acc
-            order = (0, 1)
-            for z in order:
+            sums[sensor, t] = psum.tile([P, V], F32, name="acc", tag=f"bank{PACK * sensor + t}")
+            accumulate(sums[sensor, t], sensor, t, slice(0, V))
+
+        def accumulate(acc, sensor, t, entries):
+            x_scale_planes = [plane[:, V * sensor : V * (sensor + 1)] for plane in (picked_scales, moved_scales)]
+            for z in range(PASSES):
                 codes, scales = weights[sensor, z, t]
                 nc.tensor.matmul_mx(
                     out=acc[:],
                     lhsT=codes.bitcast(FP8X4),
                     lhsT_scale=scales,
-                    rhs=picked_words[sensor, z][:].bitcast(FP4X4),
-                    rhs_scale=x_scale_tiles[z][:, V * sensor : V * (sensor + 1)],
-                    start=(z == order[0]),
-                    stop=(z == order[1]),
-                )
-
-        def rectify(sensor, t):
-            if (sensor, t) == (NEAR, 1):
-                results[sensor, t] = after_scales.tile([P, V], F32, name="result01", align_bytes=64, offset=8192)
-            elif (sensor, t) == (FAR, 0):
-                results[sensor, t] = after_scales.tile([P, V], F32, name="result10", align_bytes=64, offset=16384)
-            else:
-                results[sensor, t] = keep.tile([P, V], F32, name=f"result{sensor}{t}", align_bytes=64)
-            nc.scalar.activation(results[sensor, t][:], sums[sensor, t][:], RELU)
-
-        def near_map(t):
-            return near_maps[t % len(near_maps)]
-
-        def far_map(t):
-            return far_maps[t % len(far_maps)]
-
-        def scatter_near(t):
-            nc.vector.tensor_copy(near_map(t)[:].indirect(near_sb[:]), results[NEAR, t][:])
-
-        def scatter_far(t):
-            nc.vector.tensor_copy(far_map(t)[:].indirect(far_sb[:]), results[FAR, t][:])
-
-        halves = [slice(0, S // 2), slice(S // 2, S)]
-
-        def join_tiles(t):
-            excess = keep.tile([P, S], F32, name=f"excess{t}", tag=f"join{t % 2}")
-            if t == 2:
-                return excess, upper_tile[:, S:].bitcast(F32)
-            lifted = keep.tile([P, S], F32, name=f"lifted{t}", tag=f"join{(t + 1) % 2}")
-            return excess, lifted
-
-        def lift(t, excess, lifted, cols):
-            nc.gpsimd.tensor_tensor(excess[:, cols], near_map(t)[:, cols], far_map(t)[:, cols], SUBTRACT)
-            nc.scalar.activation(lifted[:, cols], excess[:, cols], RELU)
-
-        def settle(t, lifted):
-            for h in (1, 0) if t == 2 else (0, 1):
-                cols = halves[h]
-                target = upper[:, 0, cols] if t == 2 else (lower[h][:, 0, :], second[h])[t]
-                nc.gpsimd.tensor_tensor(target, lifted[:, cols], far_map(t)[:, cols], ADD)
-                if t == 1:
-                    nc.sync.dma_start(lower[h][P // 2 :, 0, :], second[h][: P // 2, :])
-                    nc.sync.dma_start(lower[h][P // 2 :, 1, :], second[h][P // 2 :, :])
-                if t == 0:
-                    nc.sync.dma_start(lower[h][: P // 2, 1, :], lower[h][P // 2 :, 0, :])
-
-        staging_high = [
-            keep.tile([P, 2 * PASSES * PASS_ROWS], BF16, name=f"staging_high{sensor}", align_bytes=64)
-            for sensor in (NEAR, FAR)
-        ]
-        pick(NEAR, 0, keep.tile([P, V], U16, name="words_near0", align_bytes=64))
-        pick(NEAR, 1, keep.tile([P, V], U16, name="words_near1", align_bytes=64))
-        staging_first = keep.tile([P, PASSES * PASS_ROWS], BF16, name="staging_first", align_bytes=64)
-        round_low(NEAR, 0, staging_first)
-        for z in range(PASSES):
-            quantize(f"first{z}", [(NEAR, z, 0)], staging_first[:, PASS_ROWS * z : PASS_ROWS * (z + 1)])
-        round_high(NEAR, 0, 0, staging_high[NEAR])
-        pick(FAR, 0, after_first.tile([P, V], U16, name="words_far0", align_bytes=64, offset=0))
-        round_high(NEAR, 1, 0, staging_high[NEAR])
-        pick(FAR, 1, after_first.tile([P, V], U16, name="words_far1", align_bytes=64, offset=5120))
-        first_sums = [psum.tile([P, P], F32, name=f"first_sums{n}", tag="total") for n in range(V // P)]
-        for z in range(PASSES):
-            codes, scales = weights[NEAR, z, 0]
-            for n, acc in enumerate(first_sums):
-                nc.tensor.matmul_mx(
-                    out=acc[:],
-                    lhsT=codes.bitcast(FP8X4),
-                    lhsT_scale=scales,
-                    rhs=picked_words[NEAR, z][:, P * n : P * (n + 1)].bitcast(FP4X4),
-                    rhs_scale=x_scale_tiles[z][:, P * n : P * (n + 1)],
+                    rhs=picked_words[sensor, z][:, entries].bitcast(FP4X4),
+                    rhs_scale=x_scale_planes[z][:, entries],
                     start=(z == 0),
                     stop=(z == PASSES - 1),
                 )
-        first_head = keep.tile([P, V // 2], F32, name="first_head", align_bytes=64)
-        for n in range(2):
-            nc.scalar.activation(first_head[:, P * n : P * (n + 1)], first_sums[n][:], RELU)
-        nc.vector.tensor_copy(near_map(0)[:].indirect(near_sb[:, : LIST_COLUMNS // 2]), first_head[:])
-        quantize_low(NEAR, 1)
+
+        def rectify(engine, sensor, t, parts=1):
+            tag = "first_results" if (sensor, t) == (NEAR, 1) else f"result{sensor}{t}"
+            results[sensor, t] = keep.tile([P, V], F32, name=f"result{sensor}{t}", tag=tag, align_bytes=64)
+            for n in range(parts):
+                cols = slice(V // parts * n, V // parts * (n + 1))
+                if engine is nc.scalar:
+                    nc.scalar.activation(results[sensor, t][:, cols], sums[sensor, t][:, cols], RELU)
+                else:
+                    nc.vector.tensor_scalar_max(results[sensor, t][:, cols], sums[sensor, t][:, cols], 0.0)
+
+        def scatter(engine, sensor, t, lo, hi):
+            cells = maps[sensor, t][:].indirect(lists[sensor][:, lo // 16 : hi // 16])
+            if engine is nc.scalar:
+                nc.scalar.activation(cells, results[sensor, t][:, lo:hi], COPY)
+            else:
+                nc.vector.tensor_copy(cells, results[sensor, t][:, lo:hi])
+
+        def scalar_slab(sensor, t, parts=1):
+            rectify(nc.scalar, sensor, t, parts)
+            scatter(nc.scalar, sensor, t, 0, V // 2)
+            scatter(nc.scalar, sensor, t, V // 2, V)
+
+        def zero_by_dma(key, offset):
+            maps[key] = after_staging.tile([P, S], F32, name=f"map{key[0]}{key[1]}", align_bytes=64, offset=offset)
+            nc.sync.dma_start(maps[key][:], maps[FAR, 3][:])
+
+        halves = [slice(0, S // 2), slice(S // 2, S)]
+        planes = [keep.tile([P, PACK, S // 2], BF16, name=f"planes{h}") for h in range(2)]
+        second = [keep.tile([P, S // 2], BF16, name=f"second{h}") for h in range(2)]
+
+        def join(t, target, cols):
+            nc.vector.tensor_tensor(target, maps[NEAR, t][:, cols], maps[FAR, t][:, cols], MAX)
+
+        low = PASSES * PASS_ROWS
+        staging_first = keep.tile([P, low], BF16, name="staging_first", align_bytes=64)
+        staging_right = after_staging.tile([P, low], BF16, name="staging_right", align_bytes=64, offset=0)
+        staging_high_near = after_staging.tile([P, 2 * low], BF16, name="staging_high_near", align_bytes=64, offset=4 * S)
+        staging_far_left = after_staging.tile([P, low], BF16, name="staging_far_left", align_bytes=64, offset=8 * S)
+        staging_far_right = keep.tile([P, low], BF16, name="staging_far_right", align_bytes=64)
+        staging_high_far = keep.tile([P, 2 * low], BF16, name="staging_high_far", align_bytes=64)
+
         for z in range(PASSES):
-            round_high(NEAR, z, 1, staging_high[NEAR])
-        quantize_high(NEAR, staging_high[NEAR])
-        multiply(NEAR, 1)
-        first_rest = after_scales.tile([P, V // 2], F32, name="first_rest", align_bytes=64, offset=4096)
-        for n in range(2):
-            nc.scalar.activation(first_rest[:, P * n : P * (n + 1)], first_sums[2 + n][:], RELU)
-        nc.vector.tensor_copy(near_map(0)[:].indirect(near_sb[:, LIST_COLUMNS // 2 :]), first_rest[:])
-        quantize_low(FAR, 0)
-        round_high(FAR, 0, 0, staging_high[FAR])
-        rectify(NEAR, 1)
-        scatter_near(1)
-        multiply(FAR, 0)
-        quantize_low(FAR, 1)
-        for z, c in ((1, 0), (0, 1), (1, 1)):
-            round_high(FAR, z, c, staging_high[FAR])
-        quantize_high(FAR, staging_high[FAR])
-        rectify(FAR, 0)
-        scatter_far(0)
-        multiply(FAR, 1)
-        rectify(FAR, 1)
-        scatter_far(1)
+            pick(NEAR, z, keep.tile([P, V], U16, name=f"words_near{z}", align_bytes=64))
+            round_low(nc.scalar, NEAR, z, 0, staging_first)
+            round_high(nc.scalar, NEAR, z, 0, staging_high_near)
+        quantize_low(NEAR, 0, staging_first)
+        round_low(nc.scalar, NEAR, 0, 1, staging_right)
+        round_high(nc.scalar, NEAR, 0, 1, staging_high_near)
+        results[NEAR, 0] = keep.tile([P, V], F32, name="result00", tag="first_results", align_bytes=64)
+        for n, bank in enumerate((0, 2 * PACK - 1)):
+            entries = slice(V // 2 * n, V // 2 * (n + 1))
+            acc = psum.tile([P, V // 2], F32, name="first_sums", tag=f"bank{bank}")
+            accumulate(acc, NEAR, 0, entries)
+            nc.scalar.activation(results[NEAR, 0][:, entries], acc[:], RELU)
+        scatter(nc.scalar, NEAR, 0, 0, V // 2)
+        scatter(nc.scalar, NEAR, 0, V // 2, V)
+        for z in range(PASSES):
+            pick(FAR, z, after_left.tile([P, V], U16, name=f"words_far{z}", align_bytes=64, offset=4 * PIECE + 2 * V * z))
+        round_low(nc.vector, NEAR, 1, 1, staging_right)
+        round_high(nc.vector, NEAR, 1, 1, staging_high_near)
+        quantize_low(NEAR, 1, staging_right)
+        quantize_high(NEAR, staging_high_near)
+        zero_by_dma((NEAR, 3), 4 * S)
+        zero_by_dma((FAR, 2), 0)
+        for t in (1, 2, 3):
+            multiply(NEAR, t)
+            scalar_slab(NEAR, t)
+
+        for c, staging in enumerate((staging_far_left, staging_far_right)):
+            for z in range(PASSES):
+                round_low(nc.vector, FAR, z, c, staging)
+            for z in range(PASSES):
+                round_high(nc.vector, FAR, z, c, staging_high_far)
+            quantize_low(FAR, c, staging)
+            multiply(FAR, c)
+        quantize_high(FAR, staging_high_far)
+        for t in (2, 3):
+            multiply(FAR, t)
         staging_w3 = keep.tile([P, PASS_ROWS], BF16, name="staging_w3", align_bytes=64)
-        nc.scalar.copy(
-            staging_w3[:].rearrange("p (g h i t) -> p g h t i", h=2, i=PACK, t=PACK),
-            raw_w3[:].rearrange("p t (g h i) -> p g h t i", h=2, i=PACK),
+        nc.vector.tensor_copy(
+            staging_w3[:].rearrange("p (g i t) -> p g t i", i=RUN, t=PACK),
+            raw_w3.rearrange("p t (g i) -> p g t i", i=RUN),
         )
 
-        excess, lifted = join_tiles(0)
-        lift(0, excess, lifted, halves[0])
-        multiply(NEAR, 2)
-        rectify(NEAR, 2)
-        lift(0, excess, lifted, halves[1])
-        settle(0, lifted)
-        scatter_near(2)
-        for sensor, t in ((FAR, 2), (FAR, 3), (NEAR, 3)):
-            multiply(sensor, t)
-            rectify(sensor, t)
-        scatter_far(2)
-        for t in (1, 2):
-            excess, lifted = join_tiles(t)
-            for cols in halves[::-1] if t == 2 else halves:
-                lift(t, excess, lifted, cols)
-            settle(t, lifted)
+        rectify(nc.vector, FAR, 0)
+        w3_codes = keep.tile([P, P], U32, name="w3_codes", align_bytes=64)
+        w3_scales = keep.tile([P, P], U8, name="w3_scales", align_bytes=64)
+        nc.vector.quantize_mx(out=w3_codes[:].bitcast(FP8X4), scales=w3_scales[:], in_=staging_w3[:])
+        scatter(nc.vector, FAR, 0, 0, V)
+        rectify(nc.vector, FAR, 1)
+        for h, cols in enumerate(halves):
+            join(0, planes[h][:, 0, :], cols)
+            nc.sync.dma_start(planes[h][: P // 2, 1, :], planes[h][P // 2 :, 0, :])
+        scatter(nc.vector, FAR, 1, 0, V)
+        for h, cols in enumerate(halves):
+            join(1, second[h][:], cols)
+            nc.sync.dma_start(planes[h][P // 2 :, 0, :], second[h][: P // 2, :])
+            nc.sync.dma_start(planes[h][P // 2 :, 1, :], second[h][P // 2 :, :])
+
+        rectify(nc.scalar, FAR, 2)
+        scatter(nc.scalar, FAR, 2, 0, SHARED_ENTRIES)
+        scalar_slab(FAR, 3)
+        scatter(nc.vector, FAR, 2, SHARED_ENTRIES, V)
+        for h, cols in enumerate(halves):
+            join(2, planes[h][:, 2, :], cols)
 
         chunks = [slice(lo, hi) for lo, hi in zip(CHUNK_EDGES, CHUNK_EDGES[1:])]
-        woven = [
-            keep.tile([P, cols.stop - cols.start, PACK], BF16, name=f"woven{c}", align_bytes=64)
-            for c, cols in enumerate(chunks)
-        ]
-        for c, cols in enumerate(chunks):
+
+        def inside(cols):
             h, start = divmod(cols.start, S // 2)
-            inside = slice(start, start + cols.stop - cols.start)
-            nc.scalar.copy(woven[c][:, :, 0:2], lower[h][:, :, inside].rearrange("p t r -> p r t"))
-        scatter_near(3)
-        scatter_far(3)
-        w3_codes = after_joins.tile([P, P], U32, name="w3_codes", align_bytes=64, offset=8 * S)
-        w3_scales = after_joins.tile([P, P], U8, name="w3_scales", align_bytes=64, offset=8 * S + 512)
-        nc.vector.quantize_mx(out=w3_codes[:].bitcast(FP8X4), scales=w3_scales[:], in_=staging_w3[:])
+            return planes[h][:, :, start : start + cols.stop - cols.start]
 
         for first, last in MAX_RUNS:
             cols = slice(chunks[first].start, chunks[last].stop)
-            nc.vector.tensor_tensor(upper[:, 1, cols], near_map(3)[:, cols], far_map(3)[:, cols], MAX)
+            join(3, inside(cols)[:, 3, :], cols)
+        woven = []
         for c, cols in enumerate(chunks):
-            pairs = upper[:, :, cols].rearrange("p t r -> p r t")
-            if c in VECTOR_WEAVES:
-                nc.vector.tensor_copy(woven[c][:, :, 2:4], pairs)
-            else:
-                nc.scalar.copy(woven[c][:, :, 2:4], pairs)
+            woven.append(keep.tile([P, PACK * (cols.stop - cols.start)], BF16, name=f"woven{c}", align_bytes=64))
+            copy_on(
+                nc.vector if c in VECTOR_WEAVES else nc.scalar,
+                woven[c][:].rearrange("p (r i t) -> p r t i", i=RUN, t=PACK),
+                inside(cols).rearrange("p t (r i) -> p r t i", i=RUN),
+            )
         for c in FINISH_ORDER:
             width = chunks[c].stop - chunks[c].start
             z_codes = keep.tile([P, width], U32, name=f"z_codes{c}", align_bytes=64)
             z_scales = keep.tile([P, width], U8, name=f"z_scales{c}", align_bytes=64)
-            nc.vector.quantize_mx(
-                out=z_codes[:].bitcast(FP8X4), scales=z_scales[:], in_=woven[c][:].rearrange("p r t -> p (r t)")
-            )
-            total = psum.tile([P, width], F32, name="total", tag="total")
+            nc.vector.quantize_mx(out=z_codes[:].bitcast(FP8X4), scales=z_scales[:], in_=woven[c][:])
+            total = psum.tile([P, width], F32, name="total", tag=f"bank{c}")
             nc.tensor.matmul_mx(
                 out=total[:],
                 lhsT=w3_codes[:].bitcast(FP8X4),

@@ -27,7 +27,7 @@ LIST_COLUMNS = V // 16
 NEAR, FAR = 0, 1
 HALF = H // 2
 PIECE = PACK * HALF
-SHARED_ENTRIES = 128
+RING = 3
 CHUNK_EDGES = (0, 256, 512, 768, 896, 1024)
 MAX_RUNS = ((0, 0), (1, 1), (2, 4))
 VECTOR_WEAVES = (2, 3, 4)
@@ -44,6 +44,7 @@ def tile_picked_bev_max_p_kernel(
         after_first = ctx.enter_context(tc.tile_pool(name="after_first", bufs=1))
         after_left = ctx.enter_context(tc.tile_pool(name="after_left", bufs=1))
         after_staging = ctx.enter_context(tc.tile_pool(name="after_staging", bufs=1))
+        ring = ctx.enter_context(tc.tile_pool(name="ring", bufs=1))
         psum = ctx.enter_context(tc.psum_pool(name="psum", bufs=1))
 
         offs_sb = keep.tile([P, S // 16], U16, name="offs_sb")
@@ -73,9 +74,9 @@ def tile_picked_bev_max_p_kernel(
         scale_rows = x_scales.bitcast(I32).rearrange("z (q j) c -> j q z c", j=4)
         for j in range(4):
             nc.sync.dma_start(store_scales[j:P:SECOND_PASS_ROW, :].bitcast(I32), scale_rows[j])
-        for z in range(PASSES):
-            nc.sync.dma_start(store_words[z][:].bitcast(I32), x_words[z].bitcast(I32))
+        nc.sync.dma_start(store_words[0][:].bitcast(I32), x_words[0].bitcast(I32))
         nc.sync.dma_start(raw_left[1][:], w1_passes[1][:, :, :HALF])
+        nc.sync.dma_start(store_words[1][:].bitcast(I32), x_words[1].bitcast(I32))
         nc.sync.dma_start(raw_right[:], w1_passes[0][:, :, HALF:])
         nc.sync.dma_start(far_sb[:], far)
 
@@ -149,43 +150,31 @@ def tile_picked_bev_max_p_kernel(
 
         def multiply(sensor, t):
             sums[sensor, t] = psum.tile([P, V], F32, name="acc", tag=f"bank{PACK * sensor + t}")
-            accumulate(sums[sensor, t], sensor, t, slice(0, V))
-
-        def accumulate(acc, sensor, t, entries):
-            x_scale_planes = [plane[:, V * sensor : V * (sensor + 1)] for plane in (picked_scales, moved_scales)]
             for z in range(PASSES):
-                codes, scales = weights[sensor, z, t]
-                nc.tensor.matmul_mx(
-                    out=acc[:],
-                    lhsT=codes.bitcast(FP8X4),
-                    lhsT_scale=scales,
-                    rhs=picked_words[sensor, z][:, entries].bitcast(FP4X4),
-                    rhs_scale=x_scale_planes[z][:, entries],
-                    start=(z == 0),
-                    stop=(z == PASSES - 1),
-                )
+                accumulate(sums[sensor, t], sensor, t, slice(0, V), z)
 
-        def rectify(engine, sensor, t, parts=1):
-            tag = "first_results" if (sensor, t) == (NEAR, 1) else f"result{sensor}{t}"
+        def accumulate(acc, sensor, t, entries, z):
+            x_scale_plane = (picked_scales, moved_scales)[z][:, V * sensor : V * (sensor + 1)]
+            codes, scales = weights[sensor, z, t]
+            nc.tensor.matmul_mx(
+                out=acc[:],
+                lhsT=codes.bitcast(FP8X4),
+                lhsT_scale=scales,
+                rhs=picked_words[sensor, z][:, entries].bitcast(FP4X4),
+                rhs_scale=x_scale_plane[:, entries],
+                start=(z == 0),
+                stop=(z == PASSES - 1),
+            )
+
+        def rectify(sensor, t, lo, tag):
             results[sensor, t] = keep.tile([P, V], F32, name=f"result{sensor}{t}", tag=tag, align_bytes=64)
-            for n in range(parts):
-                cols = slice(V // parts * n, V // parts * (n + 1))
-                if engine is nc.scalar:
-                    nc.scalar.activation(results[sensor, t][:, cols], sums[sensor, t][:, cols], RELU)
-                else:
-                    nc.vector.tensor_scalar_max(results[sensor, t][:, cols], sums[sensor, t][:, cols], 0.0)
+            nc.vector.tensor_scalar_max(results[sensor, t][:, lo:], sums[sensor, t][:, lo:], 0.0)
 
-        def scatter(engine, sensor, t, lo, hi):
-            cells = maps[sensor, t][:].indirect(lists[sensor][:, lo // 16 : hi // 16])
-            if engine is nc.scalar:
-                nc.scalar.activation(cells, results[sensor, t][:, lo:hi], COPY)
-            else:
-                nc.vector.tensor_copy(cells, results[sensor, t][:, lo:hi])
+        def cells(sensor, t, lo, hi):
+            return maps[sensor, t][:].indirect(lists[sensor][:, lo // 16 : hi // 16])
 
-        def scalar_slab(sensor, t, parts=1):
-            rectify(nc.scalar, sensor, t, parts)
-            scatter(nc.scalar, sensor, t, 0, V // 2)
-            scatter(nc.scalar, sensor, t, V // 2, V)
+        def scatter(sensor, t, lo):
+            nc.vector.tensor_copy(cells(sensor, t, lo, V), results[sensor, t][:, lo:])
 
         def zero_by_dma(key, offset):
             maps[key] = after_staging.tile([P, S], F32, name=f"map{key[0]}{key[1]}", align_bytes=64, offset=offset)
@@ -203,24 +192,27 @@ def tile_picked_bev_max_p_kernel(
         staging_right = after_staging.tile([P, low], BF16, name="staging_right", align_bytes=64, offset=0)
         staging_high_near = after_staging.tile([P, 2 * low], BF16, name="staging_high_near", align_bytes=64, offset=4 * S)
         staging_far_left = after_staging.tile([P, low], BF16, name="staging_far_left", align_bytes=64, offset=8 * S)
-        staging_far_right = keep.tile([P, low], BF16, name="staging_far_right", align_bytes=64)
+        staging_far_right = keep.tile([P, low], BF16, name="staging_far_right", tag="result10", align_bytes=64)
         staging_high_far = keep.tile([P, 2 * low], BF16, name="staging_high_far", align_bytes=64)
 
         for z in range(PASSES):
-            pick(NEAR, z, keep.tile([P, V], U16, name=f"words_near{z}", align_bytes=64))
             round_low(nc.scalar, NEAR, z, 0, staging_first)
             round_high(nc.scalar, NEAR, z, 0, staging_high_near)
+        pick(NEAR, 0, keep.tile([P, V], U16, name="words_near0", align_bytes=64))
         quantize_low(NEAR, 0, staging_first)
+        pick(NEAR, 1, keep.tile([P, V], U16, name="words_near1", align_bytes=64))
         round_low(nc.scalar, NEAR, 0, 1, staging_right)
         round_high(nc.scalar, NEAR, 0, 1, staging_high_near)
-        results[NEAR, 0] = keep.tile([P, V], F32, name="result00", tag="first_results", align_bytes=64)
-        for n, bank in enumerate((0, 2 * PACK - 1)):
-            entries = slice(V // 2 * n, V // 2 * (n + 1))
-            acc = psum.tile([P, V // 2], F32, name="first_sums", tag=f"bank{bank}")
-            accumulate(acc, NEAR, 0, entries)
-            nc.scalar.activation(results[NEAR, 0][:, entries], acc[:], RELU)
-        scatter(nc.scalar, NEAR, 0, 0, V // 2)
-        scatter(nc.scalar, NEAR, 0, V // 2, V)
+        first_results = ring.tile([P, V], F32, name="first_results", align_bytes=64, offset=V)
+        first_sums = [psum.tile([P, V // 2], F32, name="first_sums", tag=f"bank{bank}") for bank in (0, 2 * PACK - 1)]
+        first_entries = [slice(0, V // 2), slice(V // 2, V)]
+        for z in range(PASSES):
+            for acc, entries in zip(first_sums, first_entries):
+                accumulate(acc, NEAR, 0, entries, z)
+        for acc, entries in zip(first_sums, first_entries):
+            nc.scalar.activation(first_results[:, entries], acc[:], RELU)
+        for entries in first_entries:
+            nc.scalar.activation(cells(NEAR, 0, entries.start, entries.stop), first_results[:, entries], COPY)
         for z in range(PASSES):
             pick(FAR, z, after_left.tile([P, V], U16, name=f"words_far{z}", align_bytes=64, offset=4 * PIECE + 2 * V * z))
         round_low(nc.vector, NEAR, 1, 1, staging_right)
@@ -231,7 +223,6 @@ def tile_picked_bev_max_p_kernel(
         zero_by_dma((FAR, 2), 0)
         for t in (1, 2, 3):
             multiply(NEAR, t)
-            scalar_slab(NEAR, t)
 
         for c, staging in enumerate((staging_far_left, staging_far_right)):
             for z in range(PASSES):
@@ -243,31 +234,43 @@ def tile_picked_bev_max_p_kernel(
         quantize_high(FAR, staging_high_far)
         for t in (2, 3):
             multiply(FAR, t)
+
+        results[FAR, 2] = keep.tile([P, V], F32, name="result12", align_bytes=64)
+        nc.scalar.activation(results[FAR, 2][:], sums[FAR, 2][:], RELU)
+        shares = [(NEAR, t, lo, lo + V // 2) for lo in (0, V // 2) for t in (1, 2)]
+        shares.extend((sensor, 3, lo, lo + V // 2) for lo in (0, V // 2) for sensor in (FAR, NEAR))
+        waiting = []
+        for n in range(len(shares) + RING - 1):
+            if n < len(shares):
+                sensor, t, lo, hi = shares[n]
+                values = ring.tile([P, hi - lo], F32, name=f"share{n}", align_bytes=64, offset=2 * V * (n % RING))
+                nc.scalar.activation(values[:], sums[sensor, t][:, lo:hi], RELU)
+                waiting.append(values)
+            if n >= RING - 1:
+                nc.scalar.activation(cells(*shares[n - RING + 1]), waiting[n - RING + 1][:], COPY)
+
         staging_w3 = keep.tile([P, PASS_ROWS], BF16, name="staging_w3", align_bytes=64)
         nc.vector.tensor_copy(
             staging_w3[:].rearrange("p (g i t) -> p g t i", i=RUN, t=PACK),
             raw_w3.rearrange("p t (g i) -> p g t i", i=RUN),
         )
 
-        rectify(nc.vector, FAR, 0)
+        rectify(FAR, 0, 0, "result10")
         w3_codes = keep.tile([P, P], U32, name="w3_codes", align_bytes=64)
         w3_scales = keep.tile([P, P], U8, name="w3_scales", align_bytes=64)
         nc.vector.quantize_mx(out=w3_codes[:].bitcast(FP8X4), scales=w3_scales[:], in_=staging_w3[:])
-        scatter(nc.vector, FAR, 0, 0, V)
-        rectify(nc.vector, FAR, 1)
+        scatter(FAR, 0, 0)
+        rectify(FAR, 1, 0, "result11")
         for h, cols in enumerate(halves):
             join(0, planes[h][:, 0, :], cols)
             nc.sync.dma_start(planes[h][: P // 2, 1, :], planes[h][P // 2 :, 0, :])
-        scatter(nc.vector, FAR, 1, 0, V)
+        scatter(FAR, 1, 0)
         for h, cols in enumerate(halves):
             join(1, second[h][:], cols)
             nc.sync.dma_start(planes[h][P // 2 :, 0, :], second[h][: P // 2, :])
             nc.sync.dma_start(planes[h][P // 2 :, 1, :], second[h][P // 2 :, :])
 
-        rectify(nc.scalar, FAR, 2)
-        scatter(nc.scalar, FAR, 2, 0, SHARED_ENTRIES)
-        scalar_slab(FAR, 3)
-        scatter(nc.vector, FAR, 2, SHARED_ENTRIES, V)
+        scatter(FAR, 2, 0)
         for h, cols in enumerate(halves):
             join(2, planes[h][:, 2, :], cols)
 

@@ -16,6 +16,8 @@ FP4X4 = mybir.dt.float4_e2m1fn_x4
 RELU = mybir.ActivationFunctionType.Relu
 COPY = mybir.ActivationFunctionType.Copy
 MAX = mybir.AluOpType.max
+MULT = mybir.AluOpType.mult
+ADD = mybir.AluOpType.add
 
 P = 128
 PACK = 4
@@ -26,13 +28,15 @@ SECOND_PASS_ROW = 16
 LIST_COLUMNS = V // 16
 NEAR, FAR = 0, 1
 HALF = H // 2
-PIECE = PACK * HALF
+SHARE = V // 2
 RING = 3
+KIB = 1024
 CHUNK_EDGES = (0, 256, 512, 768, 896, 1024)
 MAX_RUNS = ((0, 0), (1, 1), (2, 4))
 VECTOR_WEAVES = (2, 3, 4)
 FINISH_ORDER = (0, 2, 1, 3, 4)
 VECTOR_EMPTIES = (3, 4)
+FINAL_BANKS = (0, 1, 2, 3, 6)
 
 
 def tile_picked_bev_max_p_kernel(
@@ -41,9 +45,9 @@ def tile_picked_bev_max_p_kernel(
     nc = tc.nc
     with ExitStack() as ctx:
         keep = ctx.enter_context(tc.tile_pool(name="keep", bufs=1))
-        after_first = ctx.enter_context(tc.tile_pool(name="after_first", bufs=1))
-        after_left = ctx.enter_context(tc.tile_pool(name="after_left", bufs=1))
-        after_staging = ctx.enter_context(tc.tile_pool(name="after_staging", bufs=1))
+        late = ctx.enter_context(tc.tile_pool(name="late", bufs=1))
+        stage = ctx.enter_context(tc.tile_pool(name="stage", bufs=1))
+        picks = ctx.enter_context(tc.tile_pool(name="picks", bufs=1))
         ring = ctx.enter_context(tc.tile_pool(name="ring", bufs=1))
         psum = ctx.enter_context(tc.psum_pool(name="psum", bufs=1))
 
@@ -51,57 +55,68 @@ def tile_picked_bev_max_p_kernel(
         near_sb = keep.tile([P, LIST_COLUMNS], U16, name="near_sb")
         far_sb = keep.tile([P, LIST_COLUMNS], U16, name="far_sb")
         lists = [near_sb, far_sb]
-        store_scales = after_first.tile([P, T], U8, name="store_scales", align_bytes=64, offset=0)
-        picked_scales = keep.tile([P, S], U8, name="picked_scales", align_bytes=64)
-        raw_right = keep.tile([P, PACK, HALF], F32, name="raw_right", align_bytes=64)
-        moved_scales = keep.tile([P, S], U8, name="moved_scales", align_bytes=64)
+        store_scales = late.tile([P, T], U8, name="store_scales", align_bytes=64, offset=4 * KIB)
+        picked_scales = [keep.tile([P, V], U8, name=f"picked_scales{s}", align_bytes=64) for s in (NEAR, FAR)]
+        moved_scales = [keep.tile([P, V], U8, name=f"moved_scales{s}", align_bytes=64) for s in (NEAR, FAR)]
         store_words = [keep.tile([P, T], U16, name=f"store_words{z}", align_bytes=64) for z in range(PASSES)]
-        raw_left = [
-            after_left.tile([P, PACK, HALF], F32, name=f"raw_left{z}", align_bytes=64, offset=4 * PIECE * z)
-            for z in range(PASSES)
-        ]
+        raw_left = [keep.tile([P, PACK, HALF], F32, name=f"raw_left{z}", align_bytes=64) for z in range(PASSES)]
         maps = {}
-        for key in ((NEAR, 0), (NEAR, 1), (FAR, 3), (FAR, 0), (FAR, 1), (NEAR, 2)):
+        for key in ((NEAR, 0), (NEAR, 1), (NEAR, 2), (FAR, 0), (FAR, 1), (FAR, 3)):
             maps[key] = keep.tile([P, S], F32, name=f"map{key[0]}{key[1]}", align_bytes=64)
+        maps[FAR, 2] = maps[FAR, 1]
 
-        nc.vector.memset(store_scales[:, : T // 2].bitcast(I32), 0)
-        nc.gpsimd.memset(store_scales[:, T // 2 :].bitcast(I32), 0)
+        nc.gpsimd.memset(store_scales[:].bitcast(I32), 0)
         w1_passes = w1.rearrange("(z p j) c -> z p j c", z=PASSES, j=PACK)
         w2_passes = w2.rearrange("(z p j) c -> z p j c", z=PASSES, j=PACK)
         nc.sync.dma_start(offs_sb[:], offs)
         nc.sync.dma_start(near_sb[:], near)
-        nc.sync.dma_start(raw_left[0][:], w1_passes[0][:, :, :HALF])
+        nc.sync.dma_start(far_sb[:], far)
         scale_rows = x_scales.bitcast(I32).rearrange("z (q j) c -> j q z c", j=4)
         for j in range(4):
             nc.sync.dma_start(store_scales[j:P:SECOND_PASS_ROW, :].bitcast(I32), scale_rows[j])
-        nc.sync.dma_start(store_words[0][:].bitcast(I32), x_words[0].bitcast(I32))
-        nc.sync.dma_start(raw_left[1][:], w1_passes[1][:, :, :HALF])
-        nc.sync.dma_start(store_words[1][:].bitcast(I32), x_words[1].bitcast(I32))
-        nc.sync.dma_start(raw_right[:], w1_passes[0][:, :, HALF:])
-        nc.sync.dma_start(far_sb[:], far)
+        for z in range(PASSES):
+            nc.sync.dma_start(store_words[z][:].bitcast(I32), x_words[z].bitcast(I32))
+            nc.sync.dma_start(raw_left[z][:], w1_passes[z][:, :, :HALF])
 
         nc.vector.memset(maps[FAR, 3][:].bitcast(I32), 0)
-        nc.gpsimd.memset(moved_scales[:].bitcast(I32), 0)
+        for s in (NEAR, FAR):
+            nc.gpsimd.memset(moved_scales[s][:].bitcast(I32), 0)
         for key in ((NEAR, 0), (NEAR, 1), (NEAR, 2)):
             nc.vector.tensor_copy(maps[key][:], maps[FAR, 3][:])
         for key in ((FAR, 0), (FAR, 1)):
             nc.scalar.activation(maps[key][:], maps[FAR, 3][:], RELU)
 
-        nc.vector.tensor_copy(picked_scales[:], store_scales[:].indirect(offs_sb[:]))
-        for q in range(4):
-            nc.sync.dma_start(
-                moved_scales[32 * q : 32 * q + 4, :].bitcast(I32),
-                picked_scales[32 * q + SECOND_PASS_ROW : 32 * q + SECOND_PASS_ROW + 4, :].bitcast(I32),
-            )
-        raw_late = after_first.tile([P, 5 * PIECE + PACK * N], F32, name="raw_late", align_bytes=64, offset=0)
-        raw = {(NEAR, z, 0): raw_left[z][:] for z in range(PASSES)}
-        raw[NEAR, 0, 1] = raw_right[:]
-        late_keys = [(NEAR, 1, 1)] + [(FAR, z, c) for c in range(2) for z in range(PASSES)]
-        for n, (sensor, z, c) in enumerate(late_keys):
-            raw[sensor, z, c] = raw_late[:, PIECE * n : PIECE * (n + 1)].rearrange("p (j c) -> p j c", j=PACK)
-            source = (w1_passes, w2_passes)[sensor][z]
-            nc.sync.dma_start(raw[sensor, z, c], source[:, :, HALF * c : HALF * (c + 1)])
-        raw_w3 = raw_late[:, 5 * PIECE :].rearrange("p (t n) -> p t n", t=PACK)
+        def entries_of(sensor, lo, hi):
+            return offs_sb[:, (V * sensor + lo) // 16 : (V * sensor + hi) // 16]
+
+        def move_second_pass_scales(sensor):
+            for q in range(4):
+                nc.sync.dma_start(
+                    moved_scales[sensor][32 * q : 32 * q + 4, :].bitcast(I32),
+                    picked_scales[sensor][32 * q + SECOND_PASS_ROW : 32 * q + SECOND_PASS_ROW + 4, :].bitcast(I32),
+                )
+
+        for s in (NEAR, FAR):
+            nc.vector.tensor_copy(picked_scales[s][:], store_scales[:].indirect(entries_of(s, 0, V)))
+        move_second_pass_scales(NEAR)
+
+        piece = PACK * HALF
+        raw_late = late.tile([P, 6 * piece + PACK * N], F32, name="raw_late", align_bytes=64, offset=5 * KIB)
+        maps[NEAR, 3] = late.tile([P, S], F32, name="map03", align_bytes=64, offset=1 * KIB)
+        nc.gpsimd.memset(maps[NEAR, 3][:].bitcast(I32), 0)
+        raw_right = [
+            raw_late[:, piece * z : piece * (z + 1)].rearrange("p (j c) -> p j c", j=PACK) for z in range(PASSES)
+        ]
+        raw_far = [
+            raw_late[:, 2 * piece * (z + 1) : 2 * piece * (z + 2)].rearrange("p (j c) -> p j c", j=PACK)
+            for z in range(PASSES)
+        ]
+        raw_w3 = raw_late[:, 6 * piece :].rearrange("p (t n) -> p t n", t=PACK)
+        for z in range(PASSES):
+            nc.sync.dma_start(raw_right[z], w1_passes[z][:, :, HALF:])
+        move_second_pass_scales(FAR)
+        for z in range(PASSES):
+            nc.sync.dma_start(raw_far[z], w2_passes[z])
         w3_slabs = w3.rearrange("(g t i) n -> t g i n", t=PACK, i=RUN)
         for t in range(PACK):
             nc.sync.dma_start(raw_w3[:, t, :], w3_slabs[t])
@@ -109,30 +124,34 @@ def tile_picked_bev_max_p_kernel(
         picked_words = {}
         weights = {}
         sums = {}
-        results = {}
 
-        def copy_on(engine, target, source):
-            if engine is nc.scalar:
-                nc.scalar.copy(target, source)
+        def round_on(engine, rounded, values):
+            if engine is nc.gpsimd:
+                nc.gpsimd.tensor_scalar(
+                    rounded, values, 1.0, 0.0, MULT, ADD
+                )
+            elif engine is nc.scalar:
+                nc.scalar.copy(
+                    rounded.rearrange("p g u i j -> p u g j i"), values.rearrange("p g u i j -> p u g j i")
+                )
             else:
-                engine.tensor_copy(target, source)
+                nc.vector.tensor_copy(
+                    rounded.rearrange("p g u i j -> p u g j i"), values.rearrange("p g u i j -> p u g j i")
+                )
 
-        def pick(sensor, z, words):
-            picked_words[sensor, z] = words
-            entries = offs_sb[:, LIST_COLUMNS * sensor : LIST_COLUMNS * (sensor + 1)]
-            nc.vector.tensor_copy(words[:], store_words[z][:].indirect(entries))
+        def positions(raw, pair):
+            return raw.rearrange("p j (g t i) -> p g t i j", t=PACK, i=RUN)[:, :, 2 * pair : 2 * pair + 2]
 
-        def round_pair(engine, sensor, z, c, pair, rounded):
-            values = raw[sensor, z, c].rearrange("p j (g t i) -> p t g j i", t=PACK, i=RUN)
-            copy_on(engine, rounded, values[:, 2 * pair : 2 * pair + 2])
+        def round_low(engine, raw, rounded):
+            round_on(engine, rounded.rearrange("p (u g i j) -> p g u i j", u=2, i=RUN, j=PACK), positions(raw, 0))
 
-        def round_low(engine, sensor, z, c, staging):
-            rounded = staging[:, PASS_ROWS * z : PASS_ROWS * (z + 1)]
-            round_pair(engine, sensor, z, c, 0, rounded.rearrange("p (u g i j) -> p u g j i", u=2, i=RUN, j=PACK))
+        def round_high(engine, raw, staging, z, groups):
+            rounded = staging[:].rearrange("p (u z g i j) -> p z g u i j", z=PASSES, u=2, i=RUN, j=PACK)
+            round_on(engine, rounded[:, z, groups], positions(raw, 1))
 
-        def round_high(engine, sensor, z, c, staging):
-            rounded = staging[:].rearrange("p (z u c g i j) -> p z c u g j i", z=PASSES, u=2, c=2, i=RUN, j=PACK)
-            round_pair(engine, sensor, z, c, 1, rounded[:, z, c])
+        def pick(sensor, z, lo, hi, words):
+            picked_words[sensor, z, lo] = words
+            nc.vector.tensor_copy(words[:], store_words[z][:].indirect(entries_of(sensor, lo, hi)))
 
         def quantize(label, keys, staging):
             count = len(keys)
@@ -142,135 +161,159 @@ def tile_picked_bev_max_p_kernel(
             for n, key in enumerate(keys):
                 weights[key] = (codes[:, P * n : P * (n + 1)], scales[:, P * n : P * (n + 1)])
 
-        def quantize_low(sensor, c, staging):
-            quantize(f"low{sensor}{c}", [(sensor, z, c) for z in range(PASSES)], staging[:])
-
-        def quantize_high(sensor, staging):
-            quantize(f"high{sensor}", [(sensor, z, t) for z in range(PASSES) for t in (2, 3)], staging[:])
-
-        def multiply(sensor, t):
-            sums[sensor, t] = psum.tile([P, V], F32, name="acc", tag=f"bank{PACK * sensor + t}")
-            for z in range(PASSES):
-                accumulate(sums[sensor, t], sensor, t, slice(0, V), z)
-
-        def accumulate(acc, sensor, t, entries, z):
-            x_scale_plane = (picked_scales, moved_scales)[z][:, V * sensor : V * (sensor + 1)]
+        def accumulate(acc, sensor, t, z, lo, hi):
+            plane = (picked_scales, moved_scales)[z][sensor]
+            first = lo if (sensor, z, lo) in picked_words else 0
             codes, scales = weights[sensor, z, t]
             nc.tensor.matmul_mx(
-                out=acc[:],
+                out=acc,
                 lhsT=codes.bitcast(FP8X4),
                 lhsT_scale=scales,
-                rhs=picked_words[sensor, z][:, entries].bitcast(FP4X4),
-                rhs_scale=x_scale_plane[:, entries],
+                rhs=picked_words[sensor, z, first][:, lo - first : hi - first].bitcast(FP4X4),
+                rhs_scale=plane[:, lo:hi],
                 start=(z == 0),
                 stop=(z == PASSES - 1),
             )
 
-        def rectify(sensor, t, lo, tag):
-            results[sensor, t] = keep.tile([P, V], F32, name=f"result{sensor}{t}", tag=tag, align_bytes=64)
-            nc.vector.tensor_scalar_max(results[sensor, t][:, lo:], sums[sensor, t][:, lo:], 0.0)
+        def multiply(sensor, t, lo, bank):
+            sums[sensor, t, lo] = psum.tile([P, SHARE], F32, name="acc", tag=f"bank{bank}")[:]
+            for z in range(PASSES):
+                accumulate(sums[sensor, t, lo], sensor, t, z, lo, lo + SHARE)
+
+        def multiply_whole(sensor, t, bank):
+            acc = psum.tile([P, V], F32, name="acc", tag=f"bank{bank}")
+            for z in range(PASSES):
+                accumulate(acc[:], sensor, t, z, 0, V)
+            for lo in (0, SHARE):
+                sums[sensor, t, lo] = acc[:, lo : lo + SHARE]
+            sums[sensor, t] = acc[:]
 
         def cells(sensor, t, lo, hi):
             return maps[sensor, t][:].indirect(lists[sensor][:, lo // 16 : hi // 16])
 
-        def scatter(sensor, t, lo):
-            nc.vector.tensor_copy(cells(sensor, t, lo, V), results[sensor, t][:, lo:])
+        left_groups, right_groups, all_groups = slice(0, 16), slice(16, 32), slice(0, 32)
+        staging_left = [
+            keep.tile([P, PASS_ROWS], BF16, name="staging_left0", align_bytes=64),
+            picks.tile([P, PASS_ROWS], BF16, name="staging_left1", align_bytes=64, offset=768),
+        ]
+        staging_right = keep.tile([P, PASSES * PASS_ROWS], BF16, name="staging_right", align_bytes=64)
+        staging_high_near = stage.tile([P, 4 * PASS_ROWS], BF16, name="staging_high_near", align_bytes=64, offset=2 * KIB)
 
-        def zero_by_dma(key, offset):
-            maps[key] = after_staging.tile([P, S], F32, name=f"map{key[0]}{key[1]}", align_bytes=64, offset=offset)
-            nc.sync.dma_start(maps[key][:], maps[FAR, 3][:])
+        for z in range(PASSES):
+            round_low(nc.scalar, raw_left[z][:], staging_left[z][:])
+            round_high(nc.scalar, raw_left[z][:], staging_high_near, z, left_groups)
+        pick(NEAR, 0, 0, V, keep.tile([P, V], U16, name="words_near0", align_bytes=64))
+        quantize("left0", [(NEAR, 0, 0)], staging_left[0][:])
+        pick(NEAR, 1, 0, SHARE, keep.tile([P, SHARE], U16, name="words_near1a", align_bytes=64))
+        quantize("left1", [(NEAR, 1, 0)], staging_left[1][:])
+        pick(NEAR, 1, SHARE, V, picks.tile([P, SHARE], U16, name="words_near1b", align_bytes=64, offset=1024))
+        pick(FAR, 0, 0, V, picks.tile([P, V], U16, name="words_far0", align_bytes=64, offset=0))
+        for bank, lo in enumerate((0, SHARE)):
+            sums[NEAR, 0, lo] = psum.tile([P, SHARE], F32, name="first_sums", tag=f"bank{bank}")[:]
+        for z in range(PASSES):
+            for lo in (0, SHARE):
+                accumulate(sums[NEAR, 0, lo], NEAR, 0, z, lo, lo + SHARE)
+
+        round_high(nc.gpsimd, raw_right[0], staging_high_near, 0, right_groups)
+        round_low(nc.gpsimd, raw_right[0], staging_right[:, :PASS_ROWS])
+        round_high(nc.vector, raw_right[1], staging_high_near, 1, right_groups)
+        round_low(nc.vector, raw_right[1], staging_right[:, PASS_ROWS:])
+        both = PASSES * PASS_ROWS
+        quantize("near2", [(NEAR, z, 2) for z in range(PASSES)], staging_high_near[:, :both])
+        quantize("near1", [(NEAR, z, 1) for z in range(PASSES)], staging_right[:])
+        quantize("near3", [(NEAR, z, 3) for z in range(PASSES)], staging_high_near[:, both:])
+        pick(FAR, 1, 0, V, stage.tile([P, V], U16, name="words_far1", align_bytes=64, offset=1536))
+        for t, lo, bank in ((2, 0, 3), (2, SHARE, 4), (1, 0, 2), (3, 0, 6), (1, SHARE, 5), (3, SHARE, 7)):
+            multiply(NEAR, t, lo, bank)
+
+        emptied = []
+
+        def empty_share(sensor, t, lo):
+            n = len(emptied)
+            values = ring.tile([P, SHARE], F32, name=f"share{n}", align_bytes=64, offset=4 * SHARE * (n % RING))
+            nc.scalar.activation(values[:], sums[sensor, t, lo], RELU)
+            emptied.append(values)
+            return values
+
+        def scalar_shares(shares):
+            values = [empty_share(*share) for share in shares[: RING - 1]]
+            for n, (sensor, t, lo) in enumerate(shares):
+                if n + RING - 1 < len(shares):
+                    values.append(empty_share(*shares[n + RING - 1]))
+                nc.scalar.activation(cells(sensor, t, lo, lo + SHARE), values[n][:], COPY)
+
+        scalar_shares([(NEAR, 0, lo) for lo in (0, SHARE)])
+        scalar_shares([(NEAR, t, lo) for lo in (0, SHARE) for t in (1, 3)])
+        values_near2 = keep.tile([P, V], F32, name="values_near2", align_bytes=64)
+        for lo in (0, SHARE):
+            nc.vector.tensor_scalar_max(values_near2[:, lo : lo + SHARE], sums[NEAR, 2, lo], 0.0)
+        nc.vector.tensor_copy(cells(NEAR, 2, 0, V), values_near2[:])
+
+        staging_low_far = {
+            c: stage.tile([P, both], BF16, name=f"staging_low_far{c}", align_bytes=64, offset=4608 - 2 * KIB * c)
+            for c in (1, 0)
+        }
+        for z in range(PASSES):
+            for c in (1, 0):
+                round_low(
+                    nc.gpsimd,
+                    raw_far[z][:, :, HALF * c : HALF * (c + 1)],
+                    staging_low_far[c][:, PASS_ROWS * z : PASS_ROWS * (z + 1)],
+                )
+        for c in (1, 0):
+            quantize(f"low_far{c}", [(FAR, z, c) for z in range(PASSES)], staging_low_far[c][:])
+        for t, lo, bank in ((1, 0, 0), (0, 0, 2), (1, SHARE, 1), (0, SHARE, 3)):
+            multiply(FAR, t, lo, bank)
+        for lo in (0, SHARE):
+            values = keep.tile([P, SHARE], F32, name=f"values_far1{lo}", align_bytes=64)
+            nc.vector.tensor_scalar_max(values[:], sums[FAR, 1, lo], 0.0)
+            nc.vector.tensor_copy(cells(FAR, 1, lo, lo + SHARE), values[:])
+        scalar_shares([(FAR, 0, 0), (FAR, 0, SHARE)])
+
+        staging_w3 = stage.tile([P, PASS_ROWS], BF16, name="staging_w3", align_bytes=64, offset=5 * KIB)
+        staging_high_far = stage.tile([P, 4 * PASS_ROWS], BF16, name="staging_high_far", align_bytes=64, offset=6 * KIB)
+        for z in range(PASSES):
+            round_high(nc.gpsimd, raw_far[z], staging_high_far, z, all_groups)
+        nc.gpsimd.tensor_scalar(
+            staging_w3[:].rearrange("p (g i t) -> p g t i", i=RUN, t=PACK),
+            raw_w3.rearrange("p t (g i) -> p g t i", i=RUN),
+            1.0,
+            0.0,
+            MULT,
+            ADD,
+        )
+        quantize("high_far", [(FAR, z, t) for t in (2, 3) for z in range(PASSES)], staging_high_far[:])
+        quantize("w3", ["w3"], staging_w3[:])
+        multiply_whole(FAR, 2, 4)
+        multiply_whole(FAR, 3, 5)
+
+        values_far2 = keep.tile([P, V], F32, name="values_far2", align_bytes=64)
+        nc.scalar.activation(values_far2[:], sums[FAR, 2], RELU)
+        scalar_shares([(FAR, 3, 0), (FAR, 3, SHARE)])
 
         halves = [slice(0, S // 2), slice(S // 2, S)]
-        planes = [keep.tile([P, PACK, S // 2], BF16, name=f"planes{h}") for h in range(2)]
-        second = [keep.tile([P, S // 2], BF16, name=f"second{h}") for h in range(2)]
+        planes = [
+            late.tile([P, PACK, S // 2], BF16, name=f"planes{h}", align_bytes=64, offset=(8 + 4 * h) * KIB)
+            for h in range(2)
+        ]
+        joined = {}
+        for t in range(2):
+            for h in range(2):
+                offset = (16 + 2 * t + h) * KIB
+                joined[t, h] = late.tile([P, S // 2], BF16, name=f"joined{t}{h}", align_bytes=64, offset=offset)
 
         def join(t, target, cols):
             nc.vector.tensor_tensor(target, maps[NEAR, t][:, cols], maps[FAR, t][:, cols], MAX)
 
-        low = PASSES * PASS_ROWS
-        staging_first = keep.tile([P, low], BF16, name="staging_first", align_bytes=64)
-        staging_right = after_staging.tile([P, low], BF16, name="staging_right", align_bytes=64, offset=0)
-        staging_high_near = after_staging.tile([P, 2 * low], BF16, name="staging_high_near", align_bytes=64, offset=4 * S)
-        staging_far_left = after_staging.tile([P, low], BF16, name="staging_far_left", align_bytes=64, offset=8 * S)
-        staging_far_right = keep.tile([P, low], BF16, name="staging_far_right", tag="result10", align_bytes=64)
-        staging_high_far = keep.tile([P, 2 * low], BF16, name="staging_high_far", align_bytes=64)
+        for t in (1, 0):
+            for h, cols in enumerate(halves):
+                join(t, joined[t, h][:], cols)
+                for u in range(2):
+                    nc.sync.dma_start(
+                        planes[h][P // 2 * t : P // 2 * (t + 1), u, :], joined[t, h][P // 2 * u : P // 2 * (u + 1), :]
+                    )
 
-        for z in range(PASSES):
-            round_low(nc.scalar, NEAR, z, 0, staging_first)
-            round_high(nc.scalar, NEAR, z, 0, staging_high_near)
-        pick(NEAR, 0, keep.tile([P, V], U16, name="words_near0", align_bytes=64))
-        quantize_low(NEAR, 0, staging_first)
-        pick(NEAR, 1, keep.tile([P, V], U16, name="words_near1", align_bytes=64))
-        round_low(nc.scalar, NEAR, 0, 1, staging_right)
-        round_high(nc.scalar, NEAR, 0, 1, staging_high_near)
-        first_results = ring.tile([P, V], F32, name="first_results", align_bytes=64, offset=V)
-        first_sums = [psum.tile([P, V // 2], F32, name="first_sums", tag=f"bank{bank}") for bank in (0, 2 * PACK - 1)]
-        first_entries = [slice(0, V // 2), slice(V // 2, V)]
-        for z in range(PASSES):
-            for acc, entries in zip(first_sums, first_entries):
-                accumulate(acc, NEAR, 0, entries, z)
-        for acc, entries in zip(first_sums, first_entries):
-            nc.scalar.activation(first_results[:, entries], acc[:], RELU)
-        for entries in first_entries:
-            nc.scalar.activation(cells(NEAR, 0, entries.start, entries.stop), first_results[:, entries], COPY)
-        for z in range(PASSES):
-            pick(FAR, z, after_left.tile([P, V], U16, name=f"words_far{z}", align_bytes=64, offset=4 * PIECE + 2 * V * z))
-        round_low(nc.vector, NEAR, 1, 1, staging_right)
-        round_high(nc.vector, NEAR, 1, 1, staging_high_near)
-        quantize_low(NEAR, 1, staging_right)
-        quantize_high(NEAR, staging_high_near)
-        zero_by_dma((NEAR, 3), 4 * S)
-        zero_by_dma((FAR, 2), 0)
-        for t in (1, 2, 3):
-            multiply(NEAR, t)
-
-        for c, staging in enumerate((staging_far_left, staging_far_right)):
-            for z in range(PASSES):
-                round_low(nc.vector, FAR, z, c, staging)
-            for z in range(PASSES):
-                round_high(nc.vector, FAR, z, c, staging_high_far)
-            quantize_low(FAR, c, staging)
-            multiply(FAR, c)
-        quantize_high(FAR, staging_high_far)
-        for t in (2, 3):
-            multiply(FAR, t)
-
-        results[FAR, 2] = keep.tile([P, V], F32, name="result12", align_bytes=64)
-        nc.scalar.activation(results[FAR, 2][:], sums[FAR, 2][:], RELU)
-        shares = [(NEAR, t, lo, lo + V // 2) for lo in (0, V // 2) for t in (1, 2)]
-        shares.extend((sensor, 3, lo, lo + V // 2) for lo in (0, V // 2) for sensor in (FAR, NEAR))
-        waiting = []
-        for n in range(len(shares) + RING - 1):
-            if n < len(shares):
-                sensor, t, lo, hi = shares[n]
-                values = ring.tile([P, hi - lo], F32, name=f"share{n}", align_bytes=64, offset=2 * V * (n % RING))
-                nc.scalar.activation(values[:], sums[sensor, t][:, lo:hi], RELU)
-                waiting.append(values)
-            if n >= RING - 1:
-                nc.scalar.activation(cells(*shares[n - RING + 1]), waiting[n - RING + 1][:], COPY)
-
-        staging_w3 = keep.tile([P, PASS_ROWS], BF16, name="staging_w3", align_bytes=64)
-        nc.vector.tensor_copy(
-            staging_w3[:].rearrange("p (g i t) -> p g t i", i=RUN, t=PACK),
-            raw_w3.rearrange("p t (g i) -> p g t i", i=RUN),
-        )
-
-        rectify(FAR, 0, 0, "result10")
-        w3_codes = keep.tile([P, P], U32, name="w3_codes", align_bytes=64)
-        w3_scales = keep.tile([P, P], U8, name="w3_scales", align_bytes=64)
-        nc.vector.quantize_mx(out=w3_codes[:].bitcast(FP8X4), scales=w3_scales[:], in_=staging_w3[:])
-        scatter(FAR, 0, 0)
-        rectify(FAR, 1, 0, "result11")
-        for h, cols in enumerate(halves):
-            join(0, planes[h][:, 0, :], cols)
-            nc.sync.dma_start(planes[h][: P // 2, 1, :], planes[h][P // 2 :, 0, :])
-        scatter(FAR, 1, 0)
-        for h, cols in enumerate(halves):
-            join(1, second[h][:], cols)
-            nc.sync.dma_start(planes[h][P // 2 :, 0, :], second[h][: P // 2, :])
-            nc.sync.dma_start(planes[h][P // 2 :, 1, :], second[h][P // 2 :, :])
-
-        scatter(FAR, 2, 0)
+        nc.vector.tensor_copy(cells(FAR, 2, 0, V), values_far2[:])
         for h, cols in enumerate(halves):
             join(2, planes[h][:, 2, :], cols)
 
@@ -286,21 +329,23 @@ def tile_picked_bev_max_p_kernel(
         woven = []
         for c, cols in enumerate(chunks):
             woven.append(keep.tile([P, PACK * (cols.stop - cols.start)], BF16, name=f"woven{c}", align_bytes=64))
-            copy_on(
-                nc.vector if c in VECTOR_WEAVES else nc.scalar,
-                woven[c][:].rearrange("p (r i t) -> p r t i", i=RUN, t=PACK),
-                inside(cols).rearrange("p t (r i) -> p r t i", i=RUN),
-            )
+            target = woven[c][:].rearrange("p (r i t) -> p r t i", i=RUN, t=PACK)
+            source = inside(cols).rearrange("p t (r i) -> p r t i", i=RUN)
+            if c in VECTOR_WEAVES:
+                nc.vector.tensor_copy(target, source)
+            else:
+                nc.scalar.copy(target, source)
+        w3_codes, w3_scales = weights["w3"]
         for c in FINISH_ORDER:
             width = chunks[c].stop - chunks[c].start
             z_codes = keep.tile([P, width], U32, name=f"z_codes{c}", align_bytes=64)
             z_scales = keep.tile([P, width], U8, name=f"z_scales{c}", align_bytes=64)
             nc.vector.quantize_mx(out=z_codes[:].bitcast(FP8X4), scales=z_scales[:], in_=woven[c][:])
-            total = psum.tile([P, width], F32, name="total", tag=f"bank{c}")
+            total = psum.tile([P, width], F32, name="total", tag=f"bank{FINAL_BANKS[c]}")
             nc.tensor.matmul_mx(
                 out=total[:],
-                lhsT=w3_codes[:].bitcast(FP8X4),
-                lhsT_scale=w3_scales[:],
+                lhsT=w3_codes.bitcast(FP8X4),
+                lhsT_scale=w3_scales,
                 rhs=z_codes[:].bitcast(FP8X4),
                 rhs_scale=z_scales[:],
                 start=True,

@@ -29,14 +29,15 @@ LIST_COLUMNS = V // 16
 NEAR, FAR = 0, 1
 HALF = H // 2
 SHARE = V // 2
-RING = 3
+FIRST = 128
+HANDED = 128
 KIB = 1024
 CHUNK_EDGES = (0, 256, 512, 768, 896, 1024)
 MAX_RUNS = ((0, 0), (1, 1), (2, 4))
 VECTOR_WEAVES = (2, 3, 4)
 FINISH_ORDER = (0, 2, 1, 3, 4)
 VECTOR_EMPTIES = (3, 4)
-FINAL_BANKS = (0, 1, 2, 3, 6)
+FINAL_BANKS = (0, 1, 2, 5, 7)
 
 
 def tile_picked_bev_max_p_kernel(
@@ -59,10 +60,14 @@ def tile_picked_bev_max_p_kernel(
         picked_scales = [keep.tile([P, V], U8, name=f"picked_scales{s}", align_bytes=64) for s in (NEAR, FAR)]
         moved_scales = [keep.tile([P, V], U8, name=f"moved_scales{s}", align_bytes=64) for s in (NEAR, FAR)]
         store_words = [keep.tile([P, T], U16, name=f"store_words{z}", align_bytes=64) for z in range(PASSES)]
-        raw_left = [keep.tile([P, PACK, HALF], F32, name=f"raw_left{z}", align_bytes=64) for z in range(PASSES)]
+        raw_left = [
+            picks.tile([P, PACK, HALF], F32, name=f"raw_left{z}", align_bytes=64, offset=4 * KIB * z)
+            for z in range(PASSES)
+        ]
         maps = {}
-        for key in ((NEAR, 0), (NEAR, 1), (NEAR, 2), (FAR, 0), (FAR, 1), (FAR, 3)):
+        for key in ((NEAR, 0), (NEAR, 1), (NEAR, 2), (FAR, 1), (FAR, 3)):
             maps[key] = keep.tile([P, S], F32, name=f"map{key[0]}{key[1]}", align_bytes=64)
+        maps[FAR, 0] = ring.tile([P, S], F32, name="map10", align_bytes=64, offset=5 * KIB)
         maps[FAR, 2] = maps[FAR, 1]
 
         nc.gpsimd.memset(store_scales[:].bitcast(I32), 0)
@@ -74,9 +79,10 @@ def tile_picked_bev_max_p_kernel(
         scale_rows = x_scales.bitcast(I32).rearrange("z (q j) c -> j q z c", j=4)
         for j in range(4):
             nc.sync.dma_start(store_scales[j:P:SECOND_PASS_ROW, :].bitcast(I32), scale_rows[j])
+        nc.sync.dma_start(store_words[0][:].bitcast(I32), x_words[0].bitcast(I32))
         for z in range(PASSES):
-            nc.sync.dma_start(store_words[z][:].bitcast(I32), x_words[z].bitcast(I32))
             nc.sync.dma_start(raw_left[z][:], w1_passes[z][:, :, :HALF])
+        nc.sync.dma_start(store_words[1][:].bitcast(I32), x_words[1].bitcast(I32))
 
         nc.vector.memset(maps[FAR, 3][:].bitcast(I32), 0)
         for s in (NEAR, FAR):
@@ -85,6 +91,8 @@ def tile_picked_bev_max_p_kernel(
             nc.vector.tensor_copy(maps[key][:], maps[FAR, 3][:])
         for key in ((FAR, 0), (FAR, 1)):
             nc.scalar.activation(maps[key][:], maps[FAR, 3][:], RELU)
+        ones = keep.tile([P, 1], F32, name="ones")
+        nc.gpsimd.memset(ones[:], 1.0)
 
         def entries_of(sensor, lo, hi):
             return offs_sb[:, (V * sensor + lo) // 16 : (V * sensor + hi) // 16]
@@ -101,25 +109,18 @@ def tile_picked_bev_max_p_kernel(
         move_second_pass_scales(NEAR)
 
         piece = PACK * HALF
-        raw_late = late.tile([P, 6 * piece + PACK * N], F32, name="raw_late", align_bytes=64, offset=5 * KIB)
-        maps[NEAR, 3] = late.tile([P, S], F32, name="map03", align_bytes=64, offset=1 * KIB)
-        nc.gpsimd.memset(maps[NEAR, 3][:].bitcast(I32), 0)
-        raw_right = [
-            raw_late[:, piece * z : piece * (z + 1)].rearrange("p (j c) -> p j c", j=PACK) for z in range(PASSES)
-        ]
+        raw_late = late.tile([P, 5 * piece], F32, name="raw_late", align_bytes=64, offset=5 * KIB)
+        raw_last = late.tile([P, PACK, HALF], F32, name="raw_last", align_bytes=64, offset=1 * KIB)
+        raw_right = [raw_late[:, :piece].rearrange("p (j c) -> p j c", j=PACK), raw_last[:]]
         raw_far = [
-            raw_late[:, 2 * piece * (z + 1) : 2 * piece * (z + 2)].rearrange("p (j c) -> p j c", j=PACK)
+            raw_late[:, piece * (2 * z + 1) : piece * (2 * z + 3)].rearrange("p (j c) -> p j c", j=PACK)
             for z in range(PASSES)
         ]
-        raw_w3 = raw_late[:, 6 * piece :].rearrange("p (t n) -> p t n", t=PACK)
         for z in range(PASSES):
             nc.sync.dma_start(raw_right[z], w1_passes[z][:, :, HALF:])
         move_second_pass_scales(FAR)
         for z in range(PASSES):
             nc.sync.dma_start(raw_far[z], w2_passes[z])
-        w3_slabs = w3.rearrange("(g t i) n -> t g i n", t=PACK, i=RUN)
-        for t in range(PACK):
-            nc.sync.dma_start(raw_w3[:, t, :], w3_slabs[t])
 
         picked_words = {}
         weights = {}
@@ -163,7 +164,7 @@ def tile_picked_bev_max_p_kernel(
 
         def accumulate(acc, sensor, t, z, lo, hi):
             plane = (picked_scales, moved_scales)[z][sensor]
-            first = lo if (sensor, z, lo) in picked_words else 0
+            first = SHARE if lo >= SHARE and (sensor, z, SHARE) in picked_words else 0
             codes, scales = weights[sensor, z, t]
             nc.tensor.matmul_mx(
                 out=acc,
@@ -182,37 +183,39 @@ def tile_picked_bev_max_p_kernel(
 
         def multiply_whole(sensor, t, bank):
             acc = psum.tile([P, V], F32, name="acc", tag=f"bank{bank}")
-            for z in range(PASSES):
-                accumulate(acc[:], sensor, t, z, 0, V)
-            for lo in (0, SHARE):
-                sums[sensor, t, lo] = acc[:, lo : lo + SHARE]
+            for lo in (0, SHARE) if sensor == NEAR else (0,):
+                for z in range(PASSES):
+                    hi = lo + SHARE if sensor == NEAR else V
+                    accumulate(acc[:, lo:hi], sensor, t, z, lo, hi)
             sums[sensor, t] = acc[:]
 
         def cells(sensor, t, lo, hi):
             return maps[sensor, t][:].indirect(lists[sensor][:, lo // 16 : hi // 16])
 
         left_groups, right_groups, all_groups = slice(0, 16), slice(16, 32), slice(0, 32)
-        staging_left = [
-            keep.tile([P, PASS_ROWS], BF16, name="staging_left0", align_bytes=64),
-            picks.tile([P, PASS_ROWS], BF16, name="staging_left1", align_bytes=64, offset=768),
-        ]
+        staging_left = [keep.tile([P, PASS_ROWS], BF16, name=f"staging_left{z}", align_bytes=64) for z in range(PASSES)]
         staging_right = keep.tile([P, PASSES * PASS_ROWS], BF16, name="staging_right", align_bytes=64)
         staging_high_near = stage.tile([P, 4 * PASS_ROWS], BF16, name="staging_high_near", align_bytes=64, offset=2 * KIB)
 
         for z in range(PASSES):
             round_low(nc.scalar, raw_left[z][:], staging_left[z][:])
             round_high(nc.scalar, raw_left[z][:], staging_high_near, z, left_groups)
+        raw_w3 = picks.tile([P, PACK, N], F32, name="raw_w3", align_bytes=64, offset=5 * KIB)
+        w3_slabs = w3.rearrange("(g t i) n -> t g i n", t=PACK, i=RUN)
+        for t in range(PACK):
+            nc.sync.dma_start(raw_w3[:, t, :], w3_slabs[t])
         pick(NEAR, 0, 0, V, keep.tile([P, V], U16, name="words_near0", align_bytes=64))
-        quantize("left0", [(NEAR, 0, 0)], staging_left[0][:])
-        pick(NEAR, 1, 0, SHARE, keep.tile([P, SHARE], U16, name="words_near1a", align_bytes=64))
-        quantize("left1", [(NEAR, 1, 0)], staging_left[1][:])
-        pick(NEAR, 1, SHARE, V, picks.tile([P, SHARE], U16, name="words_near1b", align_bytes=64, offset=1024))
-        pick(FAR, 0, 0, V, picks.tile([P, V], U16, name="words_far0", align_bytes=64, offset=0))
-        for bank, lo in enumerate((0, SHARE)):
-            sums[NEAR, 0, lo] = psum.tile([P, SHARE], F32, name="first_sums", tag=f"bank{bank}")[:]
         for z in range(PASSES):
-            for lo in (0, SHARE):
-                accumulate(sums[NEAR, 0, lo], NEAR, 0, z, lo, lo + SHARE)
+            quantize(f"left{z}", [(NEAR, z, 0)], staging_left[z][:])
+        for lo in (0, SHARE):
+            pick(NEAR, 1, lo, lo + SHARE, keep.tile([P, SHARE], U16, name=f"words_near1{lo}", align_bytes=64))
+        pick(FAR, 0, 0, V, picks.tile([P, V], U16, name="words_far0", align_bytes=64, offset=4 * KIB))
+        first_groups = ((0, FIRST, 0), (FIRST, SHARE, 7), (SHARE, V, 1))
+        for lo, hi, bank in first_groups:
+            sums[NEAR, 0, lo] = psum.tile([P, hi - lo], F32, name="first_sums", tag=f"bank{bank}")[:]
+        for z in range(PASSES):
+            for lo, hi, bank in first_groups:
+                accumulate(sums[NEAR, 0, lo], NEAR, 0, z, lo, hi)
 
         round_high(nc.gpsimd, raw_right[0], staging_high_near, 0, right_groups)
         round_low(nc.gpsimd, raw_right[0], staging_right[:, :PASS_ROWS])
@@ -222,32 +225,36 @@ def tile_picked_bev_max_p_kernel(
         quantize("near2", [(NEAR, z, 2) for z in range(PASSES)], staging_high_near[:, :both])
         quantize("near1", [(NEAR, z, 1) for z in range(PASSES)], staging_right[:])
         quantize("near3", [(NEAR, z, 3) for z in range(PASSES)], staging_high_near[:, both:])
-        pick(FAR, 1, 0, V, stage.tile([P, V], U16, name="words_far1", align_bytes=64, offset=1536))
-        for t, lo, bank in ((2, 0, 3), (2, SHARE, 4), (1, 0, 2), (3, 0, 6), (1, SHARE, 5), (3, SHARE, 7)):
-            multiply(NEAR, t, lo, bank)
+        pick(FAR, 1, 0, V, late.tile([P, V], U16, name="words_far1", align_bytes=64, offset=1 * KIB))
+        for lo, bank in ((0, 3), (SHARE, 4)):
+            multiply(NEAR, 2, lo, bank)
+        multiply_whole(NEAR, 1, 2)
+        multiply_whole(NEAR, 3, 5)
 
-        emptied = []
-
-        def empty_share(sensor, t, lo):
-            n = len(emptied)
-            values = ring.tile([P, SHARE], F32, name=f"share{n}", align_bytes=64, offset=4 * SHARE * (n % RING))
-            nc.scalar.activation(values[:], sums[sensor, t, lo], RELU)
-            emptied.append(values)
+        def empty(name, source, offset):
+            values = ring.tile([P, source.shape[1]], F32, name=name, align_bytes=64, offset=offset)
+            nc.scalar.activation(values[:], source, RELU)
             return values
 
-        def scalar_shares(shares):
-            values = [empty_share(*share) for share in shares[: RING - 1]]
-            for n, (sensor, t, lo) in enumerate(shares):
-                if n + RING - 1 < len(shares):
-                    values.append(empty_share(*shares[n + RING - 1]))
-                nc.scalar.activation(cells(sensor, t, lo, lo + SHARE), values[n][:], COPY)
+        def scatter_slab(sensor, t, values):
+            nc.scalar.activation(cells(sensor, t, 0, V), values[:], COPY, scale=ones[:])
 
-        scalar_shares([(NEAR, 0, lo) for lo in (0, SHARE)])
-        scalar_shares([(NEAR, t, lo) for lo in (0, SHARE) for t in (1, 3)])
-        values_near2 = keep.tile([P, V], F32, name="values_near2", align_bytes=64)
-        for lo in (0, SHARE):
-            nc.vector.tensor_scalar_max(values_near2[:, lo : lo + SHARE], sums[NEAR, 2, lo], 0.0)
-        nc.vector.tensor_copy(cells(NEAR, 2, 0, V), values_near2[:])
+        values_near0 = ring.tile([P, V], F32, name="values_near0", align_bytes=64, offset=0)
+        for lo, hi, bank in first_groups[:2]:
+            nc.scalar.activation(values_near0[:, lo:hi], sums[NEAR, 0, lo], RELU)
+        nc.scalar.activation(cells(NEAR, 0, 0, FIRST), values_near0[:, :FIRST], COPY)
+        nc.scalar.activation(values_near0[:, SHARE:], sums[NEAR, 0, SHARE], RELU)
+        nc.scalar.activation(cells(NEAR, 0, FIRST, V), values_near0[:, FIRST:], COPY)
+        scatter_slab(NEAR, 1, empty("values_near1", sums[NEAR, 1], 2 * KIB))
+        kept = V - HANDED
+        values_near2 = keep.tile([P, kept], F32, name="values_near2", align_bytes=64)
+        nc.vector.tensor_scalar_max(values_near2[:, :SHARE], sums[NEAR, 2, 0], 0.0)
+        nc.vector.tensor_scalar_max(values_near2[:, SHARE:], sums[NEAR, 2, SHARE][:, : kept - SHARE], 0.0)
+        nc.vector.tensor_copy(cells(NEAR, 2, 0, kept), values_near2[:])
+
+        values_handed = empty("values_handed", sums[NEAR, 2, SHARE][:, kept - SHARE :], 1536 + 256)
+        values_near3 = empty("values_near3", sums[NEAR, 3], 2 * KIB + 256)
+        nc.scalar.activation(cells(NEAR, 2, kept, V), values_handed[:], COPY)
 
         staging_low_far = {
             c: stage.tile([P, both], BF16, name=f"staging_low_far{c}", align_bytes=64, offset=4608 - 2 * KIB * c)
@@ -262,34 +269,35 @@ def tile_picked_bev_max_p_kernel(
                 )
         for c in (1, 0):
             quantize(f"low_far{c}", [(FAR, z, c) for z in range(PASSES)], staging_low_far[c][:])
-        for t, lo, bank in ((1, 0, 0), (0, 0, 2), (1, SHARE, 1), (0, SHARE, 3)):
-            multiply(FAR, t, lo, bank)
+        multiply(FAR, 1, 0, 0)
+        multiply_whole(FAR, 0, 6)
+        multiply(FAR, 1, SHARE, 1)
         for lo in (0, SHARE):
-            values = keep.tile([P, SHARE], F32, name=f"values_far1{lo}", align_bytes=64)
-            nc.vector.tensor_scalar_max(values[:], sums[FAR, 1, lo], 0.0)
-            nc.vector.tensor_copy(cells(FAR, 1, lo, lo + SHARE), values[:])
-        scalar_shares([(FAR, 0, 0), (FAR, 0, SHARE)])
+            values_far1 = keep.tile([P, SHARE], F32, name=f"values_far1{lo}", align_bytes=64)
+            nc.vector.tensor_scalar_max(values_far1[:], sums[FAR, 1, lo], 0.0)
+            nc.vector.tensor_copy(cells(FAR, 1, lo, lo + SHARE), values_far1[:])
+        values_far0 = empty("values_far0", sums[FAR, 0], 9 * KIB)
+        scatter_slab(FAR, 0, values_far0)
+        maps[NEAR, 3] = stage.tile([P, S], F32, name="map03", align_bytes=64, offset=1 * KIB)
+        nc.sync.dma_start(maps[NEAR, 3][:], maps[FAR, 3][:])
+        scatter_slab(NEAR, 3, values_near3)
 
-        staging_w3 = stage.tile([P, PASS_ROWS], BF16, name="staging_w3", align_bytes=64, offset=5 * KIB)
         staging_high_far = stage.tile([P, 4 * PASS_ROWS], BF16, name="staging_high_far", align_bytes=64, offset=6 * KIB)
         for z in range(PASSES):
             round_high(nc.gpsimd, raw_far[z], staging_high_far, z, all_groups)
+        staging_w3 = stage.tile([P, PASS_ROWS], BF16, name="staging_w3", align_bytes=64, offset=5 * KIB)
         nc.gpsimd.tensor_scalar(
             staging_w3[:].rearrange("p (g i t) -> p g t i", i=RUN, t=PACK),
-            raw_w3.rearrange("p t (g i) -> p g t i", i=RUN),
+            raw_w3[:].rearrange("p t (g i) -> p g t i", i=RUN),
             1.0,
             0.0,
             MULT,
             ADD,
         )
-        quantize("high_far", [(FAR, z, t) for t in (2, 3) for z in range(PASSES)], staging_high_far[:])
-        quantize("w3", ["w3"], staging_w3[:])
+        quantize("far2", [(FAR, z, 2) for z in range(PASSES)], staging_high_far[:, :both])
+        quantize("far3", [(FAR, z, 3) for z in range(PASSES)], staging_high_far[:, both:])
         multiply_whole(FAR, 2, 4)
-        multiply_whole(FAR, 3, 5)
-
-        values_far2 = keep.tile([P, V], F32, name="values_far2", align_bytes=64)
-        nc.scalar.activation(values_far2[:], sums[FAR, 2], RELU)
-        scalar_shares([(FAR, 3, 0), (FAR, 3, SHARE)])
+        multiply_whole(FAR, 3, 3)
 
         halves = [slice(0, S // 2), slice(S // 2, S)]
         planes = [
@@ -305,15 +313,26 @@ def tile_picked_bev_max_p_kernel(
         def join(t, target, cols):
             nc.vector.tensor_tensor(target, maps[NEAR, t][:, cols], maps[FAR, t][:, cols], MAX)
 
-        for t in (1, 0):
-            for h, cols in enumerate(halves):
-                join(t, joined[t, h][:], cols)
-                for u in range(2):
-                    nc.sync.dma_start(
-                        planes[h][P // 2 * t : P // 2 * (t + 1), u, :], joined[t, h][P // 2 * u : P // 2 * (u + 1), :]
-                    )
+        def join_and_move(t, h):
+            join(t, joined[t, h][:], halves[h])
+            for u in range(2):
+                nc.sync.dma_start(
+                    planes[h][P // 2 * t : P // 2 * (t + 1), u, :], joined[t, h][P // 2 * u : P // 2 * (u + 1), :]
+                )
 
+        for h in range(2):
+            join_and_move(1, h)
+        values_far2 = keep.tile([P, V], F32, name="values_far2", align_bytes=64)
+        nc.vector.tensor_scalar_max(values_far2[:], sums[FAR, 2], 0.0)
+        join_and_move(0, 0)
+        values_far3 = keep.tile([P, V], F32, name="values_far3", align_bytes=64)
+        nc.vector.tensor_scalar_max(values_far3[:], sums[FAR, 3], 0.0)
+        join_and_move(0, 1)
+        scatter_slab(FAR, 3, values_far3)
         nc.vector.tensor_copy(cells(FAR, 2, 0, V), values_far2[:])
+        w3_codes = ring.tile([P, P], U32, name="w3_codes", align_bytes=64, offset=6 * KIB)
+        w3_scales = keep.tile([P, P], U8, name="w3_scales", align_bytes=64)
+        nc.vector.quantize_mx(out=w3_codes[:].bitcast(FP8X4), scales=w3_scales[:], in_=staging_w3[:])
         for h, cols in enumerate(halves):
             join(2, planes[h][:, 2, :], cols)
 
@@ -335,7 +354,6 @@ def tile_picked_bev_max_p_kernel(
                 nc.vector.tensor_copy(target, source)
             else:
                 nc.scalar.copy(target, source)
-        w3_codes, w3_scales = weights["w3"]
         for c in FINISH_ORDER:
             width = chunks[c].stop - chunks[c].start
             z_codes = keep.tile([P, width], U32, name=f"z_codes{c}", align_bytes=64)
@@ -344,8 +362,8 @@ def tile_picked_bev_max_p_kernel(
             total = psum.tile([P, width], F32, name="total", tag=f"bank{FINAL_BANKS[c]}")
             nc.tensor.matmul_mx(
                 out=total[:],
-                lhsT=w3_codes.bitcast(FP8X4),
-                lhsT_scale=w3_scales,
+                lhsT=w3_codes[:].bitcast(FP8X4),
+                lhsT_scale=w3_scales[:],
                 rhs=z_codes[:].bitcast(FP8X4),
                 rhs_scale=z_scales[:],
                 start=True,

@@ -37,7 +37,7 @@ MAX_RUNS = ((0, 0), (1, 1), (2, 4))
 VECTOR_WEAVES = (2, 3, 4)
 FINISH_ORDER = (0, 2, 1, 3, 4)
 VECTOR_EMPTIES = (3, 4)
-FINAL_BANKS = (0, 1, 2, 5, 7)
+FINAL_BANKS = (0, 1, 2, 5, 4)
 
 
 def tile_picked_bev_max_p_kernel(
@@ -154,9 +154,12 @@ def tile_picked_bev_max_p_kernel(
             picked_words[sensor, z, lo] = words
             nc.vector.tensor_copy(words[:], store_words[z][:].indirect(entries_of(sensor, lo, hi)))
 
-        def quantize(label, keys, staging):
+        def quantize(label, keys, staging, offset=None):
             count = len(keys)
-            codes = keep.tile([P, P * count], U32, name=f"codes_{label}", align_bytes=64)
+            if offset is None:
+                codes = keep.tile([P, P * count], U32, name=f"codes_{label}", align_bytes=64)
+            else:
+                codes = stage.tile([P, P * count], U32, name=f"codes_{label}", align_bytes=64, offset=offset)
             scales = keep.tile([P, P * count], U8, name=f"scales_{label}", align_bytes=64)
             nc.vector.quantize_mx(out=codes[:].bitcast(FP8X4), scales=scales[:], in_=staging)
             for n, key in enumerate(keys):
@@ -192,10 +195,10 @@ def tile_picked_bev_max_p_kernel(
         def cells(sensor, t, lo, hi):
             return maps[sensor, t][:].indirect(lists[sensor][:, lo // 16 : hi // 16])
 
-        left_groups, right_groups, all_groups = slice(0, 16), slice(16, 32), slice(0, 32)
+        left_groups, right_groups = slice(0, 16), slice(16, 32)
         staging_left = [keep.tile([P, PASS_ROWS], BF16, name=f"staging_left{z}", align_bytes=64) for z in range(PASSES)]
         staging_right = keep.tile([P, PASSES * PASS_ROWS], BF16, name="staging_right", align_bytes=64)
-        staging_high_near = stage.tile([P, 4 * PASS_ROWS], BF16, name="staging_high_near", align_bytes=64, offset=2 * KIB)
+        staging_high_near = stage.tile([P, 4 * PASS_ROWS], BF16, name="staging_high_near", align_bytes=64, offset=6 * KIB)
 
         for z in range(PASSES):
             round_low(nc.scalar, raw_left[z][:], staging_left[z][:])
@@ -257,46 +260,48 @@ def tile_picked_bev_max_p_kernel(
         nc.scalar.activation(cells(NEAR, 2, kept, V), values_handed[:], COPY)
 
         staging_low_far = {
-            c: stage.tile([P, both], BF16, name=f"staging_low_far{c}", align_bytes=64, offset=4608 - 2 * KIB * c)
+            c: stage.tile([P, both], BF16, name=f"staging_low_far{c}", align_bytes=64, offset=(6 + 2 * c) * KIB)
             for c in (1, 0)
         }
-        for z in range(PASSES):
+
+        def round_high_far(z, offset):
+            staging = stage.tile([P, both], BF16, name=f"staging_high_far{z}", align_bytes=64, offset=offset)
+            rounded = staging[:].rearrange("p (u g i j) -> p g u i j", u=2, i=RUN, j=PACK)
+            round_on(nc.gpsimd, rounded, positions(raw_far[z], 1))
+            return staging
+
+        for z, engine in enumerate((nc.gpsimd, nc.vector)):
             for c in (1, 0):
                 round_low(
-                    nc.gpsimd,
+                    engine,
                     raw_far[z][:, :, HALF * c : HALF * (c + 1)],
                     staging_low_far[c][:, PASS_ROWS * z : PASS_ROWS * (z + 1)],
                 )
+        staging_high_far = round_high_far(0, 10 * KIB)
         for c in (1, 0):
             quantize(f"low_far{c}", [(FAR, z, c) for z in range(PASSES)], staging_low_far[c][:])
+        quantize("high_far0", [(FAR, 0, t) for t in (2, 3)], staging_high_far[:], 9 * KIB)
         multiply(FAR, 1, 0, 0)
         multiply_whole(FAR, 0, 6)
         multiply(FAR, 1, SHARE, 1)
         for lo in (0, SHARE):
-            values_far1 = keep.tile([P, SHARE], F32, name=f"values_far1{lo}", align_bytes=64)
+            offset = 32 * KIB + 512 + 8 * lo
+            values_far1 = late.tile([P, SHARE], F32, name=f"values_far1{lo}", align_bytes=64, offset=offset)
             nc.vector.tensor_scalar_max(values_far1[:], sums[FAR, 1, lo], 0.0)
             nc.vector.tensor_copy(cells(FAR, 1, lo, lo + SHARE), values_far1[:])
         values_far0 = empty("values_far0", sums[FAR, 0], 9 * KIB)
         scatter_slab(FAR, 0, values_far0)
-        maps[NEAR, 3] = stage.tile([P, S], F32, name="map03", align_bytes=64, offset=1 * KIB)
+        maps[NEAR, 3] = stage.tile([P, S], F32, name="map03", align_bytes=64, offset=2560)
         nc.sync.dma_start(maps[NEAR, 3][:], maps[FAR, 3][:])
         scatter_slab(NEAR, 3, values_near3)
 
-        staging_high_far = stage.tile([P, 4 * PASS_ROWS], BF16, name="staging_high_far", align_bytes=64, offset=6 * KIB)
-        for z in range(PASSES):
-            round_high(nc.gpsimd, raw_far[z], staging_high_far, z, all_groups)
-        staging_w3 = stage.tile([P, PASS_ROWS], BF16, name="staging_w3", align_bytes=64, offset=5 * KIB)
-        nc.gpsimd.tensor_scalar(
-            staging_w3[:].rearrange("p (g i t) -> p g t i", i=RUN, t=PACK),
-            raw_w3[:].rearrange("p t (g i) -> p g t i", i=RUN),
-            1.0,
-            0.0,
-            MULT,
-            ADD,
+        staging_high_far = round_high_far(1, 7 * KIB)
+        quantize("high_far1", [(FAR, 1, t) for t in (2, 3)], staging_high_far[:])
+        staging_w3 = stage.tile([P, PASS_ROWS], BF16, name="staging_w3", align_bytes=64, offset=7680)
+        round_on(
+            nc.gpsimd, staging_w3[:].rearrange("p (n t) -> p n t", t=PACK), raw_w3[:].rearrange("p t n -> p n t")
         )
-        quantize("far2", [(FAR, z, 2) for z in range(PASSES)], staging_high_far[:, :both])
-        quantize("far3", [(FAR, z, 3) for z in range(PASSES)], staging_high_far[:, both:])
-        multiply_whole(FAR, 2, 4)
+        multiply_whole(FAR, 2, 7)
         multiply_whole(FAR, 3, 3)
 
         halves = [slice(0, S // 2), slice(S // 2, S)]
@@ -307,7 +312,7 @@ def tile_picked_bev_max_p_kernel(
         joined = {}
         for t in range(2):
             for h in range(2):
-                offset = (16 + 2 * t + h) * KIB
+                offset = (34 - 18 * t + h) * KIB
                 joined[t, h] = late.tile([P, S // 2], BF16, name=f"joined{t}{h}", align_bytes=64, offset=offset)
 
         def join(t, target, cols):
@@ -320,10 +325,10 @@ def tile_picked_bev_max_p_kernel(
                     planes[h][P // 2 * t : P // 2 * (t + 1), u, :], joined[t, h][P // 2 * u : P // 2 * (u + 1), :]
                 )
 
-        for h in range(2):
-            join_and_move(1, h)
         values_far2 = keep.tile([P, V], F32, name="values_far2", align_bytes=64)
         nc.vector.tensor_scalar_max(values_far2[:], sums[FAR, 2], 0.0)
+        for h in range(2):
+            join_and_move(1, h)
         join_and_move(0, 0)
         values_far3 = keep.tile([P, V], F32, name="values_far3", align_bytes=64)
         nc.vector.tensor_scalar_max(values_far3[:], sums[FAR, 3], 0.0)

@@ -70,19 +70,22 @@ def tile_picked_bev_max_p_kernel(
         maps[FAR, 0] = ring.tile([P, S], F32, name="map10", align_bytes=64, offset=5 * KIB)
         maps[FAR, 2] = maps[FAR, 1]
 
-        nc.gpsimd.memset(store_scales[:].bitcast(I32), 0)
+        nc.vector.memset(store_scales[:, : T // 2].bitcast(I32), 0)
+        nc.gpsimd.memset(store_scales[:, T // 2 :].bitcast(I32), 0)
         w1_passes = w1.rearrange("(z p j) c -> z p j c", z=PASSES, j=PACK)
         w2_passes = w2.rearrange("(z p j) c -> z p j c", z=PASSES, j=PACK)
         nc.sync.dma_start(offs_sb[:], offs)
         nc.sync.dma_start(near_sb[:], near)
-        nc.sync.dma_start(far_sb[:], far)
+        nc.sync.dma_start(raw_left[0][:], w1_passes[0][:, :, :HALF])
         scale_rows = x_scales.bitcast(I32).rearrange("z (q j) c -> j q z c", j=4)
         for j in range(4):
             nc.sync.dma_start(store_scales[j:P:SECOND_PASS_ROW, :].bitcast(I32), scale_rows[j])
         nc.sync.dma_start(store_words[0][:].bitcast(I32), x_words[0].bitcast(I32))
-        for z in range(PASSES):
-            nc.sync.dma_start(raw_left[z][:], w1_passes[z][:, :, :HALF])
+        nc.sync.dma_start(raw_left[1][:], w1_passes[1][:, :, :HALF])
         nc.sync.dma_start(store_words[1][:].bitcast(I32), x_words[1].bitcast(I32))
+        raw_third = keep.tile([P, PACK, HALF], F32, name="raw_third", align_bytes=64)
+        nc.sync.dma_start(raw_third[:], w1_passes[0][:, :, HALF:])
+        nc.sync.dma_start(far_sb[:], far)
 
         nc.vector.memset(maps[FAR, 3][:].bitcast(I32), 0)
         for s in (NEAR, FAR):
@@ -109,15 +112,13 @@ def tile_picked_bev_max_p_kernel(
         move_second_pass_scales(NEAR)
 
         piece = PACK * HALF
-        raw_late = late.tile([P, 5 * piece], F32, name="raw_late", align_bytes=64, offset=5 * KIB)
+        raw_late = late.tile([P, 4 * piece], F32, name="raw_late", align_bytes=64, offset=5 * KIB)
         raw_last = late.tile([P, PACK, HALF], F32, name="raw_last", align_bytes=64, offset=1 * KIB)
-        raw_right = [raw_late[:, :piece].rearrange("p (j c) -> p j c", j=PACK), raw_last[:]]
+        raw_right = [raw_third[:], raw_last[:]]
         raw_far = [
-            raw_late[:, piece * (2 * z + 1) : piece * (2 * z + 3)].rearrange("p (j c) -> p j c", j=PACK)
-            for z in range(PASSES)
+            raw_late[:, 2 * piece * z : 2 * piece * (z + 1)].rearrange("p (j c) -> p j c", j=PACK) for z in range(PASSES)
         ]
-        for z in range(PASSES):
-            nc.sync.dma_start(raw_right[z], w1_passes[z][:, :, HALF:])
+        nc.sync.dma_start(raw_last[:], w1_passes[1][:, :, HALF:])
         move_second_pass_scales(FAR)
         for z in range(PASSES):
             nc.sync.dma_start(raw_far[z], w2_passes[z])
@@ -196,23 +197,22 @@ def tile_picked_bev_max_p_kernel(
             return maps[sensor, t][:].indirect(lists[sensor][:, lo // 16 : hi // 16])
 
         left_groups, right_groups = slice(0, 16), slice(16, 32)
-        staging_left = [keep.tile([P, PASS_ROWS], BF16, name=f"staging_left{z}", align_bytes=64) for z in range(PASSES)]
+        staging_left = keep.tile([P, PASSES * PASS_ROWS], BF16, name="staging_left", align_bytes=64)
         staging_right = keep.tile([P, PASSES * PASS_ROWS], BF16, name="staging_right", align_bytes=64)
         staging_high_near = stage.tile([P, 4 * PASS_ROWS], BF16, name="staging_high_near", align_bytes=64, offset=6 * KIB)
 
         for z in range(PASSES):
-            round_low(nc.scalar, raw_left[z][:], staging_left[z][:])
+            round_low(nc.scalar, raw_left[z][:], staging_left[:, PASS_ROWS * z : PASS_ROWS * (z + 1)])
             round_high(nc.scalar, raw_left[z][:], staging_high_near, z, left_groups)
         raw_w3 = picks.tile([P, PACK, N], F32, name="raw_w3", align_bytes=64, offset=5 * KIB)
         w3_slabs = w3.rearrange("(g t i) n -> t g i n", t=PACK, i=RUN)
         for t in range(PACK):
             nc.sync.dma_start(raw_w3[:, t, :], w3_slabs[t])
         pick(NEAR, 0, 0, V, keep.tile([P, V], U16, name="words_near0", align_bytes=64))
-        for z in range(PASSES):
-            quantize(f"left{z}", [(NEAR, z, 0)], staging_left[z][:])
+        quantize("near0", [(NEAR, z, 0) for z in range(PASSES)], staging_left[:])
         for lo in (0, SHARE):
             pick(NEAR, 1, lo, lo + SHARE, keep.tile([P, SHARE], U16, name=f"words_near1{lo}", align_bytes=64))
-        pick(FAR, 0, 0, V, picks.tile([P, V], U16, name="words_far0", align_bytes=64, offset=4 * KIB))
+        pick(FAR, 1, 0, V, keep.tile([P, V], U16, name="words_far1", align_bytes=64))
         first_groups = ((0, FIRST, 0), (FIRST, SHARE, 7), (SHARE, V, 1))
         for lo, hi, bank in first_groups:
             sums[NEAR, 0, lo] = psum.tile([P, hi - lo], F32, name="first_sums", tag=f"bank{bank}")[:]
@@ -228,7 +228,7 @@ def tile_picked_bev_max_p_kernel(
         quantize("near2", [(NEAR, z, 2) for z in range(PASSES)], staging_high_near[:, :both])
         quantize("near1", [(NEAR, z, 1) for z in range(PASSES)], staging_right[:])
         quantize("near3", [(NEAR, z, 3) for z in range(PASSES)], staging_high_near[:, both:])
-        pick(FAR, 1, 0, V, late.tile([P, V], U16, name="words_far1", align_bytes=64, offset=1 * KIB))
+        pick(FAR, 0, 0, V, late.tile([P, V], U16, name="words_far0", align_bytes=64, offset=1 * KIB))
         for lo, bank in ((0, 3), (SHARE, 4)):
             multiply(NEAR, 2, lo, bank)
         multiply_whole(NEAR, 1, 2)

@@ -57,8 +57,8 @@ def tile_picked_bev_max_p_kernel(
         far_sb = keep.tile([P, LIST_COLUMNS], U16, name="far_sb")
         lists = [near_sb, far_sb]
         store_scales = late.tile([P, T], U8, name="store_scales", align_bytes=64, offset=4 * KIB)
-        picked_scales = [keep.tile([P, V], U8, name=f"picked_scales{s}", align_bytes=64) for s in (NEAR, FAR)]
-        moved_scales = [keep.tile([P, V], U8, name=f"moved_scales{s}", align_bytes=64) for s in (NEAR, FAR)]
+        picked_scales = keep.tile([P, S], U8, name="picked_scales", align_bytes=64)
+        moved_scales = keep.tile([P, S], U8, name="moved_scales", align_bytes=64)
         store_words = [keep.tile([P, T], U16, name=f"store_words{z}", align_bytes=64) for z in range(PASSES)]
         raw_left = [
             picks.tile([P, PACK, HALF], F32, name=f"raw_left{z}", align_bytes=64, offset=4 * KIB * z)
@@ -88,8 +88,7 @@ def tile_picked_bev_max_p_kernel(
         nc.sync.dma_start(far_sb[:], far)
 
         nc.vector.memset(maps[FAR, 3][:].bitcast(I32), 0)
-        for s in (NEAR, FAR):
-            nc.gpsimd.memset(moved_scales[s][:].bitcast(I32), 0)
+        nc.gpsimd.memset(moved_scales[:].bitcast(I32), 0)
         for key in ((NEAR, 0), (NEAR, 1), (NEAR, 2)):
             nc.vector.tensor_copy(maps[key][:], maps[FAR, 3][:])
         for key in ((FAR, 0), (FAR, 1)):
@@ -100,16 +99,12 @@ def tile_picked_bev_max_p_kernel(
         def entries_of(sensor, lo, hi):
             return offs_sb[:, (V * sensor + lo) // 16 : (V * sensor + hi) // 16]
 
-        def move_second_pass_scales(sensor):
-            for q in range(4):
-                nc.sync.dma_start(
-                    moved_scales[sensor][32 * q : 32 * q + 4, :].bitcast(I32),
-                    picked_scales[sensor][32 * q + SECOND_PASS_ROW : 32 * q + SECOND_PASS_ROW + 4, :].bitcast(I32),
-                )
-
-        for s in (NEAR, FAR):
-            nc.vector.tensor_copy(picked_scales[s][:], store_scales[:].indirect(entries_of(s, 0, V)))
-        move_second_pass_scales(NEAR)
+        nc.vector.tensor_copy(picked_scales[:], store_scales[:].indirect(offs_sb[:]))
+        for q in range(4):
+            nc.sync.dma_start(
+                moved_scales[32 * q : 32 * q + 4, :].bitcast(I32),
+                picked_scales[32 * q + SECOND_PASS_ROW : 32 * q + SECOND_PASS_ROW + 4, :].bitcast(I32),
+            )
 
         piece = PACK * HALF
         raw_late = late.tile([P, 4 * piece], F32, name="raw_late", align_bytes=64, offset=5 * KIB)
@@ -119,7 +114,6 @@ def tile_picked_bev_max_p_kernel(
             raw_late[:, 2 * piece * z : 2 * piece * (z + 1)].rearrange("p (j c) -> p j c", j=PACK) for z in range(PASSES)
         ]
         nc.sync.dma_start(raw_last[:], w1_passes[1][:, :, HALF:])
-        move_second_pass_scales(FAR)
         for z in range(PASSES):
             nc.sync.dma_start(raw_far[z], w2_passes[z])
 
@@ -167,7 +161,7 @@ def tile_picked_bev_max_p_kernel(
                 weights[key] = (codes[:, P * n : P * (n + 1)], scales[:, P * n : P * (n + 1)])
 
         def accumulate(acc, sensor, t, z, lo, hi):
-            plane = (picked_scales, moved_scales)[z][sensor]
+            plane = (picked_scales, moved_scales)[z][:, V * sensor : V * (sensor + 1)]
             first = SHARE if lo >= SHARE and (sensor, z, SHARE) in picked_words else 0
             codes, scales = weights[sensor, z, t]
             nc.tensor.matmul_mx(
@@ -220,7 +214,7 @@ def tile_picked_bev_max_p_kernel(
             for lo, hi, bank in first_groups:
                 accumulate(sums[NEAR, 0, lo], NEAR, 0, z, lo, hi)
 
-        round_high(nc.gpsimd, raw_right[0], staging_high_near, 0, right_groups)
+        round_high(nc.scalar, raw_right[0], staging_high_near, 0, right_groups)
         round_low(nc.gpsimd, raw_right[0], staging_right[:, :PASS_ROWS])
         round_high(nc.vector, raw_right[1], staging_high_near, 1, right_groups)
         round_low(nc.vector, raw_right[1], staging_right[:, PASS_ROWS:])
@@ -229,9 +223,8 @@ def tile_picked_bev_max_p_kernel(
         quantize("near1", [(NEAR, z, 1) for z in range(PASSES)], staging_right[:])
         quantize("near3", [(NEAR, z, 3) for z in range(PASSES)], staging_high_near[:, both:])
         pick(FAR, 0, 0, V, late.tile([P, V], U16, name="words_far0", align_bytes=64, offset=1 * KIB))
-        for lo, bank in ((0, 3), (SHARE, 4)):
-            multiply(NEAR, 2, lo, bank)
-        multiply_whole(NEAR, 1, 2)
+        for t, lo, bank in ((2, 0, 3), (1, 0, 2), (2, SHARE, 4), (1, SHARE, 0)):
+            multiply(NEAR, t, lo, bank)
         multiply_whole(NEAR, 3, 5)
 
         def empty(name, source, offset):
@@ -248,7 +241,10 @@ def tile_picked_bev_max_p_kernel(
         nc.scalar.activation(cells(NEAR, 0, 0, FIRST), values_near0[:, :FIRST], COPY)
         nc.scalar.activation(values_near0[:, SHARE:], sums[NEAR, 0, SHARE], RELU)
         nc.scalar.activation(cells(NEAR, 0, FIRST, V), values_near0[:, FIRST:], COPY)
-        scatter_slab(NEAR, 1, empty("values_near1", sums[NEAR, 1], 2 * KIB))
+        values_near1 = ring.tile([P, V], F32, name="values_near1", align_bytes=64, offset=2 * KIB)
+        for lo in (0, SHARE):
+            nc.scalar.activation(values_near1[:, lo : lo + SHARE], sums[NEAR, 1, lo], RELU)
+            nc.scalar.activation(cells(NEAR, 1, lo, lo + SHARE), values_near1[:, lo : lo + SHARE], COPY)
         kept = V - HANDED
         values_near2 = keep.tile([P, kept], F32, name="values_near2", align_bytes=64)
         nc.vector.tensor_scalar_max(values_near2[:, :SHARE], sums[NEAR, 2, 0], 0.0)
@@ -264,10 +260,13 @@ def tile_picked_bev_max_p_kernel(
             for c in (1, 0)
         }
 
-        def round_high_far(z, offset):
-            staging = stage.tile([P, both], BF16, name=f"staging_high_far{z}", align_bytes=64, offset=offset)
-            rounded = staging[:].rearrange("p (u g i j) -> p g u i j", u=2, i=RUN, j=PACK)
-            round_on(nc.gpsimd, rounded, positions(raw_far[z], 1))
+        def round_far_position(t, offset):
+            staging = stage.tile([P, PASS_ROWS], BF16, name=f"staging_far{t}", align_bytes=64, offset=offset)
+            round_on(
+                nc.gpsimd,
+                staging[:].rearrange("p (g i j) -> p g i j", i=RUN, j=PACK),
+                raw_far[0].rearrange("p j (g t i) -> p t g i j", t=PACK, i=RUN)[:, t],
+            )
             return staging
 
         for z, engine in enumerate((nc.gpsimd, nc.vector)):
@@ -277,10 +276,10 @@ def tile_picked_bev_max_p_kernel(
                     raw_far[z][:, :, HALF * c : HALF * (c + 1)],
                     staging_low_far[c][:, PASS_ROWS * z : PASS_ROWS * (z + 1)],
                 )
-        staging_high_far = round_high_far(0, 10 * KIB)
+        staging_far2 = round_far_position(2, 10 * KIB)
         for c in (1, 0):
             quantize(f"low_far{c}", [(FAR, z, c) for z in range(PASSES)], staging_low_far[c][:])
-        quantize("high_far0", [(FAR, 0, t) for t in (2, 3)], staging_high_far[:], 9 * KIB)
+        quantize("far2", [(FAR, 0, 2)], staging_far2[:], 9 * KIB + 512)
         multiply(FAR, 1, 0, 0)
         multiply_whole(FAR, 0, 6)
         multiply(FAR, 1, SHARE, 1)
@@ -291,15 +290,26 @@ def tile_picked_bev_max_p_kernel(
             nc.vector.tensor_copy(cells(FAR, 1, lo, lo + SHARE), values_far1[:])
         values_far0 = empty("values_far0", sums[FAR, 0], 9 * KIB)
         scatter_slab(FAR, 0, values_far0)
-        maps[NEAR, 3] = stage.tile([P, S], F32, name="map03", align_bytes=64, offset=2560)
+        maps[NEAR, 3] = stage.tile([P, S], F32, name="map03", align_bytes=64, offset=11 * KIB - 512)
         nc.sync.dma_start(maps[NEAR, 3][:], maps[FAR, 3][:])
         scatter_slab(NEAR, 3, values_near3)
 
-        staging_high_far = round_high_far(1, 7 * KIB)
-        quantize("high_far1", [(FAR, 1, t) for t in (2, 3)], staging_high_far[:])
-        staging_w3 = stage.tile([P, PASS_ROWS], BF16, name="staging_w3", align_bytes=64, offset=7680)
+        staging_second = stage.tile([P, both], BF16, name="staging_second", align_bytes=64, offset=5 * KIB + 512)
         round_on(
-            nc.gpsimd, staging_w3[:].rearrange("p (n t) -> p n t", t=PACK), raw_w3[:].rearrange("p t n -> p n t")
+            nc.gpsimd,
+            staging_second[:].rearrange("p (u g i j) -> p g u i j", u=2, i=RUN, j=PACK),
+            positions(raw_far[1], 1),
+        )
+        quantize("second", [(FAR, 1, t) for t in (2, 3)], staging_second[:])
+        staging_far3 = round_far_position(3, 7 * KIB)
+        codes = keep.tile([P, P], U32, name="codes_far3", align_bytes=64)
+        scales = late.tile([P, P], U8, name="scales_far3", align_bytes=64, offset=34 * KIB + 768)
+        nc.vector.quantize_mx(out=codes[:].bitcast(FP8X4), scales=scales[:], in_=staging_far3[:])
+        weights[FAR, 0, 3] = (codes[:], scales[:])
+        staging_w3 = stage.tile([P, PASS_ROWS], BF16, name="staging_w3", align_bytes=64, offset=7 * KIB + 512)
+        nc.vector.tensor_copy(
+            staging_w3[:].rearrange("p (g i t) -> p g t i", i=RUN, t=PACK),
+            raw_w3[:].rearrange("p t (g i) -> p g t i", i=RUN),
         )
         multiply_whole(FAR, 2, 7)
         multiply_whole(FAR, 3, 3)
@@ -312,7 +322,7 @@ def tile_picked_bev_max_p_kernel(
         joined = {}
         for t in range(2):
             for h in range(2):
-                offset = (34 - 18 * t + h) * KIB
+                offset = (16 + h) * KIB if t else 33 * KIB + 768 + 1536 * h
                 joined[t, h] = late.tile([P, S // 2], BF16, name=f"joined{t}{h}", align_bytes=64, offset=offset)
 
         def join(t, target, cols):
@@ -325,10 +335,10 @@ def tile_picked_bev_max_p_kernel(
                     planes[h][P // 2 * t : P // 2 * (t + 1), u, :], joined[t, h][P // 2 * u : P // 2 * (u + 1), :]
                 )
 
-        values_far2 = keep.tile([P, V], F32, name="values_far2", align_bytes=64)
-        nc.vector.tensor_scalar_max(values_far2[:], sums[FAR, 2], 0.0)
         for h in range(2):
             join_and_move(1, h)
+        values_far2 = keep.tile([P, V], F32, name="values_far2", align_bytes=64)
+        nc.vector.tensor_scalar_max(values_far2[:], sums[FAR, 2], 0.0)
         join_and_move(0, 0)
         values_far3 = keep.tile([P, V], F32, name="values_far3", align_bytes=64)
         nc.vector.tensor_scalar_max(values_far3[:], sums[FAR, 3], 0.0)

@@ -225,7 +225,6 @@ def tile_picked_bev_max_p_kernel(
         pick(FAR, 0, 0, V, late.tile([P, V], U16, name="words_far0", align_bytes=64, offset=1 * KIB))
         for t, lo, bank in ((2, 0, 3), (1, 0, 2), (2, SHARE, 4), (1, SHARE, 0)):
             multiply(NEAR, t, lo, bank)
-        multiply_whole(NEAR, 3, 5)
 
         def empty(name, source, offset):
             values = ring.tile([P, source.shape[1]], F32, name=name, align_bytes=64, offset=offset)
@@ -245,6 +244,7 @@ def tile_picked_bev_max_p_kernel(
         for lo in (0, SHARE):
             nc.scalar.activation(values_near1[:, lo : lo + SHARE], sums[NEAR, 1, lo], RELU)
             nc.scalar.activation(cells(NEAR, 1, lo, lo + SHARE), values_near1[:, lo : lo + SHARE], COPY)
+        multiply_whole(NEAR, 3, 0)
         kept = V - HANDED
         values_near2 = keep.tile([P, kept], F32, name="values_near2", align_bytes=64)
         nc.vector.tensor_scalar_max(values_near2[:, :SHARE], sums[NEAR, 2, 0], 0.0)
@@ -280,7 +280,7 @@ def tile_picked_bev_max_p_kernel(
         for c in (1, 0):
             quantize(f"low_far{c}", [(FAR, z, c) for z in range(PASSES)], staging_low_far[c][:])
         quantize("far2", [(FAR, 0, 2)], staging_far2[:], 9 * KIB + 512)
-        multiply(FAR, 1, 0, 0)
+        multiply(FAR, 1, 0, 5)
         multiply_whole(FAR, 0, 6)
         multiply(FAR, 1, SHARE, 1)
         for lo in (0, SHARE):

from contextlib import ExitStack

import concourse.mybir as mybir

K, T, S, H, N, V = 1024, 2048, 1024, 512, 128, 512
FLOPS = 2 * (2 * K * H * V) + 2 * H * N * S

F32 = mybir.dt.float32
BF16 = mybir.dt.bfloat16
I32 = mybir.dt.int32
U32 = mybir.dt.uint32
U16 = mybir.dt.uint16
U8 = mybir.dt.uint8
FP8X4 = mybir.dt.float8_e4m3fn_x4
FP4X4 = mybir.dt.float4_e2m1fn_x4
RELU = mybir.ActivationFunctionType.Relu
COPY = mybir.ActivationFunctionType.Copy
MAX = mybir.AluOpType.max
MULT = mybir.AluOpType.mult
ADD = mybir.AluOpType.add

P = 128
PACK = 4
PASS_ROWS = P * PACK
PASSES = K // PASS_ROWS
RUN = 4
SECOND_PASS_ROW = 16
LIST_COLUMNS = V // 16
NEAR, FAR = 0, 1
HALF = H // 2
SHARE = V // 2
FIRST = 128
HANDED = 128
KIB = 1024
CHUNK_EDGES = (0, 256, 512, 768, 896, 1024)
MAX_RUNS = ((0, 0), (1, 1), (2, 4))
VECTOR_WEAVES = (2, 3, 4)
FINISH_ORDER = (0, 2, 1, 3, 4)
VECTOR_EMPTIES = (3, 4)
FINAL_BANKS = (0, 1, 2, 5, 4)


def tile_picked_bev_max_p_kernel(
    tc, x_words, x_scales, w1, w2, w3, offs, near, far, out
):
    nc = tc.nc
    with ExitStack() as ctx:
        keep = ctx.enter_context(tc.tile_pool(name="keep", bufs=1))
        late = ctx.enter_context(tc.tile_pool(name="late", bufs=1))
        stage = ctx.enter_context(tc.tile_pool(name="stage", bufs=1))
        picks = ctx.enter_context(tc.tile_pool(name="picks", bufs=1))
        ring = ctx.enter_context(tc.tile_pool(name="ring", bufs=1))
        psum = ctx.enter_context(tc.psum_pool(name="psum", bufs=1))

        offs_sb = keep.tile([P, S // 16], U16, name="offs_sb")
        near_sb = keep.tile([P, LIST_COLUMNS], U16, name="near_sb")
        far_sb = keep.tile([P, LIST_COLUMNS], U16, name="far_sb")
        lists = [near_sb, far_sb]
        store_scales = late.tile([P, T], U8, name="store_scales", align_bytes=64, offset=4 * KIB)
        picked_scales = keep.tile([P, S], U8, name="picked_scales", align_bytes=64)
        moved_scales = keep.tile([P, S], U8, name="moved_scales", align_bytes=64)
        store_words = [keep.tile([P, T], U16, name=f"store_words{z}", align_bytes=64) for z in range(PASSES)]
        raw_left = [
            picks.tile([P, PACK, HALF], F32, name=f"raw_left{z}", align_bytes=64, offset=4 * KIB * z)
            for z in range(PASSES)
        ]
        maps = {}
        for key in ((NEAR, 0), (NEAR, 1), (NEAR, 2), (FAR, 1), (FAR, 3)):
            maps[key] = keep.tile([P, S], F32, name=f"map{key[0]}{key[1]}", align_bytes=64)
        maps[FAR, 0] = ring.tile([P, S], F32, name="map10", align_bytes=64, offset=5 * KIB)
        maps[FAR, 2] = maps[FAR, 1]

        nc.vector.memset(store_scales[:, : T // 2].bitcast(I32), 0)
        nc.gpsimd.memset(store_scales[:, T // 2 :].bitcast(I32), 0)
        w1_passes = w1.rearrange("(z p j) c -> z p j c", z=PASSES, j=PACK)
        w2_passes = w2.rearrange("(z p j) c -> z p j c", z=PASSES, j=PACK)
        nc.sync.dma_start(offs_sb[:], offs)
        nc.sync.dma_start(near_sb[:], near)
        nc.sync.dma_start(raw_left[0][:], w1_passes[0][:, :, :HALF])
        scale_rows = x_scales.bitcast(I32).rearrange("z (q j) c -> j q z c", j=4)
        for j in range(4):
            nc.sync.dma_start(store_scales[j:P:SECOND_PASS_ROW, :].bitcast(I32), scale_rows[j])
        nc.sync.dma_start(store_words[0][:].bitcast(I32), x_words[0].bitcast(I32))
        nc.sync.dma_start(raw_left[1][:], w1_passes[1][:, :, :HALF])
        nc.sync.dma_start(store_words[1][:].bitcast(I32), x_words[1].bitcast(I32))
        raw_third = keep.tile([P, PACK, HALF], F32, name="raw_third", align_bytes=64)
        nc.sync.dma_start(raw_third[:], w1_passes[0][:, :, HALF:])
        nc.sync.dma_start(far_sb[:], far)

        nc.vector.memset(maps[FAR, 3][:].bitcast(I32), 0)
        nc.gpsimd.memset(moved_scales[:].bitcast(I32), 0)
        for key in ((NEAR, 0), (NEAR, 1), (NEAR, 2)):
            nc.vector.tensor_copy(maps[key][:], maps[FAR, 3][:])
        for key in ((FAR, 0), (FAR, 1)):
            nc.scalar.activation(maps[key][:], maps[FAR, 3][:], RELU)
        ones = keep.tile([P, 1], F32, name="ones")
        nc.gpsimd.memset(ones[:], 1.0)

        def entries_of(sensor, lo, hi):
            return offs_sb[:, (V * sensor + lo) // 16 : (V * sensor + hi) // 16]

        nc.vector.tensor_copy(picked_scales[:], store_scales[:].indirect(offs_sb[:]))
        for q in range(4):
            nc.sync.dma_start(
                moved_scales[32 * q : 32 * q + 4, :].bitcast(I32),
                picked_scales[32 * q + SECOND_PASS_ROW : 32 * q + SECOND_PASS_ROW + 4, :].bitcast(I32),
            )

        piece = PACK * HALF
        raw_late = late.tile([P, 4 * piece], F32, name="raw_late", align_bytes=64, offset=5 * KIB)
        raw_last = late.tile([P, PACK, HALF], F32, name="raw_last", align_bytes=64, offset=1 * KIB)
        raw_right = [raw_third[:], raw_last[:]]
        raw_far = [
            raw_late[:, 2 * piece * z : 2 * piece * (z + 1)].rearrange("p (j c) -> p j c", j=PACK) for z in range(PASSES)
        ]
        nc.sync.dma_start(raw_last[:], w1_passes[1][:, :, HALF:])
        for z in range(PASSES):
            nc.sync.dma_start(raw_far[z], w2_passes[z])

        picked_words = {}
        weights = {}
        sums = {}

        def round_on(engine, rounded, values):
            if engine is nc.gpsimd:
                nc.gpsimd.tensor_scalar(
                    rounded, values, 1.0, 0.0, MULT, ADD
                )
            elif engine is nc.scalar:
                nc.scalar.copy(
                    rounded.rearrange("p g u i j -> p u g j i"), values.rearrange("p g u i j -> p u g j i")
                )
            else:
                nc.vector.tensor_copy(
                    rounded.rearrange("p g u i j -> p u g j i"), values.rearrange("p g u i j -> p u g j i")
                )

        def positions(raw, pair):
            return raw.rearrange("p j (g t i) -> p g t i j", t=PACK, i=RUN)[:, :, 2 * pair : 2 * pair + 2]

        def round_low(engine, raw, rounded):
            round_on(engine, rounded.rearrange("p (u g i j) -> p g u i j", u=2, i=RUN, j=PACK), positions(raw, 0))

        def round_high(engine, raw, staging, z, groups):
            rounded = staging[:].rearrange("p (u z g i j) -> p z g u i j", z=PASSES, u=2, i=RUN, j=PACK)
            round_on(engine, rounded[:, z, groups], positions(raw, 1))

        def pick(sensor, z, lo, hi, words):
            picked_words[sensor, z, lo] = words
            nc.vector.tensor_copy(words[:], store_words[z][:].indirect(entries_of(sensor, lo, hi)))

        def quantize(label, keys, staging, offset=None):
            count = len(keys)
            if offset is None:
                codes = keep.tile([P, P * count], U32, name=f"codes_{label}", align_bytes=64)
            else:
                codes = stage.tile([P, P * count], U32, name=f"codes_{label}", align_bytes=64, offset=offset)
            scales = keep.tile([P, P * count], U8, name=f"scales_{label}", align_bytes=64)
            nc.vector.quantize_mx(out=codes[:].bitcast(FP8X4), scales=scales[:], in_=staging)
            for n, key in enumerate(keys):
                weights[key] = (codes[:, P * n : P * (n + 1)], scales[:, P * n : P * (n + 1)])

        def accumulate(acc, sensor, t, z, lo, hi):
            plane = (picked_scales, moved_scales)[z][:, V * sensor : V * (sensor + 1)]
            first = SHARE if lo >= SHARE and (sensor, z, SHARE) in picked_words else 0
            codes, scales = weights[sensor, z, t]
            nc.tensor.matmul_mx(
                out=acc,
                lhsT=codes.bitcast(FP8X4),
                lhsT_scale=scales,
                rhs=picked_words[sensor, z, first][:, lo - first : hi - first].bitcast(FP4X4),
                rhs_scale=plane[:, lo:hi],
                start=(z == 0),
                stop=(z == PASSES - 1),
            )

        def multiply(sensor, t, lo, bank):
            sums[sensor, t, lo] = psum.tile([P, SHARE], F32, name="acc", tag=f"bank{bank}")[:]
            for z in range(PASSES):
                accumulate(sums[sensor, t, lo], sensor, t, z, lo, lo + SHARE)

        def multiply_whole(sensor, t, bank):
            acc = psum.tile([P, V], F32, name="acc", tag=f"bank{bank}")
            for lo in (0, SHARE) if sensor == NEAR else (0,):
                for z in range(PASSES):
                    hi = lo + SHARE if sensor == NEAR else V
                    accumulate(acc[:, lo:hi], sensor, t, z, lo, hi)
            sums[sensor, t] = acc[:]

        def cells(sensor, t, lo, hi):
            return maps[sensor, t][:].indirect(lists[sensor][:, lo // 16 : hi // 16])

        left_groups, right_groups = slice(0, 16), slice(16, 32)
        staging_left = keep.tile([P, PASSES * PASS_ROWS], BF16, name="staging_left", align_bytes=64)
        staging_right = keep.tile([P, PASSES * PASS_ROWS], BF16, name="staging_right", align_bytes=64)
        staging_high_near = stage.tile([P, 4 * PASS_ROWS], BF16, name="staging_high_near", align_bytes=64, offset=6 * KIB)

        for z in range(PASSES):
            round_low(nc.scalar, raw_left[z][:], staging_left[:, PASS_ROWS * z : PASS_ROWS * (z + 1)])
            round_high(nc.scalar, raw_left[z][:], staging_high_near, z, left_groups)
        raw_w3 = picks.tile([P, PACK, N], F32, name="raw_w3", align_bytes=64, offset=5 * KIB)
        w3_slabs = w3.rearrange("(g t i) n -> t g i n", t=PACK, i=RUN)
        for t in range(PACK):
            nc.sync.dma_start(raw_w3[:, t, :], w3_slabs[t])
        pick(NEAR, 0, 0, V, keep.tile([P, V], U16, name="words_near0", align_bytes=64))
        quantize("near0", [(NEAR, z, 0) for z in range(PASSES)], staging_left[:])
        for lo in (0, SHARE):
            pick(NEAR, 1, lo, lo + SHARE, keep.tile([P, SHARE], U16, name=f"words_near1{lo}", align_bytes=64))
        pick(FAR, 1, 0, V, keep.tile([P, V], U16, name="words_far1", align_bytes=64))
        first_groups = ((0, FIRST, 0), (FIRST, SHARE, 7), (SHARE, V, 1))
        for lo, hi, bank in first_groups:
            sums[NEAR, 0, lo] = psum.tile([P, hi - lo], F32, name="first_sums", tag=f"bank{bank}")[:]
        for z in range(PASSES):
            for lo, hi, bank in first_groups:
                accumulate(sums[NEAR, 0, lo], NEAR, 0, z, lo, hi)

        round_high(nc.scalar, raw_right[0], staging_high_near, 0, right_groups)
        round_low(nc.gpsimd, raw_right[0], staging_right[:, :PASS_ROWS])
        round_high(nc.vector, raw_right[1], staging_high_near, 1, right_groups)
        round_low(nc.vector, raw_right[1], staging_right[:, PASS_ROWS:])
        both = PASSES * PASS_ROWS
        quantize("near2", [(NEAR, z, 2) for z in range(PASSES)], staging_high_near[:, :both])
        quantize("near1", [(NEAR, z, 1) for z in range(PASSES)], staging_right[:])
        quantize("near3", [(NEAR, z, 3) for z in range(PASSES)], staging_high_near[:, both:])
        pick(FAR, 0, 0, V, late.tile([P, V], U16, name="words_far0", align_bytes=64, offset=1 * KIB))
        for t, lo, bank in ((2, 0, 3), (1, 0, 2), (2, SHARE, 4), (1, SHARE, 0)):
            multiply(NEAR, t, lo, bank)

        def empty(name, source, offset):
            values = ring.tile([P, source.shape[1]], F32, name=name, align_bytes=64, offset=offset)
            nc.scalar.activation(values[:], source, RELU)
            return values

        def scatter_slab(sensor, t, values):
            nc.scalar.activation(cells(sensor, t, 0, V), values[:], COPY, scale=ones[:])

        values_near0 = ring.tile([P, V], F32, name="values_near0", align_bytes=64, offset=0)
        for lo, hi, bank in first_groups[:2]:
            nc.scalar.activation(values_near0[:, lo:hi], sums[NEAR, 0, lo], RELU)
        nc.scalar.activation(cells(NEAR, 0, 0, FIRST), values_near0[:, :FIRST], COPY)
        nc.scalar.activation(values_near0[:, SHARE:], sums[NEAR, 0, SHARE], RELU)
        nc.scalar.activation(cells(NEAR, 0, FIRST, V), values_near0[:, FIRST:], COPY)
        values_near1 = ring.tile([P, V], F32, name="values_near1", align_bytes=64, offset=2 * KIB)
        for lo in (0, SHARE):
            nc.scalar.activation(values_near1[:, lo : lo + SHARE], sums[NEAR, 1, lo], RELU)
            nc.scalar.activation(cells(NEAR, 1, lo, lo + SHARE), values_near1[:, lo : lo + SHARE], COPY)
        multiply_whole(NEAR, 3, 0)
        kept = V - HANDED
        values_near2 = keep.tile([P, kept], F32, name="values_near2", align_bytes=64)
        nc.vector.tensor_scalar_max(values_near2[:, :SHARE], sums[NEAR, 2, 0], 0.0)
        nc.vector.tensor_scalar_max(values_near2[:, SHARE:], sums[NEAR, 2, SHARE][:, : kept - SHARE], 0.0)
        nc.vector.tensor_copy(cells(NEAR, 2, 0, kept), values_near2[:])

        values_handed = empty("values_handed", sums[NEAR, 2, SHARE][:, kept - SHARE :], 1536 + 256)
        values_near3 = empty("values_near3", sums[NEAR, 3], 2 * KIB + 256)
        nc.scalar.activation(cells(NEAR, 2, kept, V), values_handed[:], COPY)

        staging_low_far = {
            c: stage.tile([P, both], BF16, name=f"staging_low_far{c}", align_bytes=64, offset=(6 + 2 * c) * KIB)
            for c in (1, 0)
        }

        def round_far_position(t, offset):
            staging = stage.tile([P, PASS_ROWS], BF16, name=f"staging_far{t}", align_bytes=64, offset=offset)
            round_on(
                nc.gpsimd,
                staging[:].rearrange("p (g i j) -> p g i j", i=RUN, j=PACK),
                raw_far[0].rearrange("p j (g t i) -> p t g i j", t=PACK, i=RUN)[:, t],
            )
            return staging

        for z, engine in enumerate((nc.gpsimd, nc.vector)):
            for c in (1, 0):
                round_low(
                    engine,
                    raw_far[z][:, :, HALF * c : HALF * (c + 1)],
                    staging_low_far[c][:, PASS_ROWS * z : PASS_ROWS * (z + 1)],
                )
        staging_far2 = round_far_position(2, 10 * KIB)
        for c in (1, 0):
            quantize(f"low_far{c}", [(FAR, z, c) for z in range(PASSES)], staging_low_far[c][:])
        quantize("far2", [(FAR, 0, 2)], staging_far2[:], 9 * KIB + 512)
        multiply(FAR, 1, 0, 5)
        multiply_whole(FAR, 0, 6)
        multiply(FAR, 1, SHARE, 1)
        for lo in (0, SHARE):
            offset = 32 * KIB + 512 + 8 * lo
            values_far1 = late.tile([P, SHARE], F32, name=f"values_far1{lo}", align_bytes=64, offset=offset)
            nc.vector.tensor_scalar_max(values_far1[:], sums[FAR, 1, lo], 0.0)
            nc.vector.tensor_copy(cells(FAR, 1, lo, lo + SHARE), values_far1[:])
        values_far0 = empty("values_far0", sums[FAR, 0], 9 * KIB)
        scatter_slab(FAR, 0, values_far0)
        maps[NEAR, 3] = stage.tile([P, S], F32, name="map03", align_bytes=64, offset=11 * KIB - 512)
        nc.sync.dma_start(maps[NEAR, 3][:], maps[FAR, 3][:])
        scatter_slab(NEAR, 3, values_near3)

        staging_second = stage.tile([P, both], BF16, name="staging_second", align_bytes=64, offset=5 * KIB + 512)
        round_on(
            nc.gpsimd,
            staging_second[:].rearrange("p (u g i j) -> p g u i j", u=2, i=RUN, j=PACK),
            positions(raw_far[1], 1),
        )
        quantize("second", [(FAR, 1, t) for t in (2, 3)], staging_second[:])
        staging_far3 = round_far_position(3, 7 * KIB)
        codes = keep.tile([P, P], U32, name="codes_far3", align_bytes=64)
        scales = late.tile([P, P], U8, name="scales_far3", align_bytes=64, offset=34 * KIB + 768)
        nc.vector.quantize_mx(out=codes[:].bitcast(FP8X4), scales=scales[:], in_=staging_far3[:])
        weights[FAR, 0, 3] = (codes[:], scales[:])
        staging_w3 = stage.tile([P, PASS_ROWS], BF16, name="staging_w3", align_bytes=64, offset=7 * KIB + 512)
        nc.vector.tensor_copy(
            staging_w3[:].rearrange("p (g i t) -> p g t i", i=RUN, t=PACK),
            raw_w3[:].rearrange("p t (g i) -> p g t i", i=RUN),
        )
        multiply_whole(FAR, 2, 7)
        multiply_whole(FAR, 3, 3)

        halves = [slice(0, S // 2), slice(S // 2, S)]
        planes = [
            late.tile([P, PACK, S // 2], BF16, name=f"planes{h}", align_bytes=64, offset=(8 + 4 * h) * KIB)
            for h in range(2)
        ]
        joined = {}
        for t in range(2):
            for h in range(2):
                offset = (16 + h) * KIB if t else 33 * KIB + 768 + 1536 * h
                joined[t, h] = late.tile([P, S // 2], BF16, name=f"joined{t}{h}", align_bytes=64, offset=offset)

        def join(t, target, cols):
            nc.vector.tensor_tensor(target, maps[NEAR, t][:, cols], maps[FAR, t][:, cols], MAX)

        def join_and_move(t, h):
            join(t, joined[t, h][:], halves[h])
            for u in range(2):
                nc.sync.dma_start(
                    planes[h][P // 2 * t : P // 2 * (t + 1), u, :], joined[t, h][P // 2 * u : P // 2 * (u + 1), :]
                )

        for h in range(2):
            join_and_move(1, h)
        values_far2 = keep.tile([P, V], F32, name="values_far2", align_bytes=64)
        nc.vector.tensor_scalar_max(values_far2[:], sums[FAR, 2], 0.0)
        join_and_move(0, 0)
        values_far3 = keep.tile([P, V], F32, name="values_far3", align_bytes=64)
        nc.vector.tensor_scalar_max(values_far3[:], sums[FAR, 3], 0.0)
        join_and_move(0, 1)
        scatter_slab(FAR, 3, values_far3)
        nc.vector.tensor_copy(cells(FAR, 2, 0, V), values_far2[:])
        w3_codes = ring.tile([P, P], U32, name="w3_codes", align_bytes=64, offset=6 * KIB)
        w3_scales = keep.tile([P, P], U8, name="w3_scales", align_bytes=64)
        nc.vector.quantize_mx(out=w3_codes[:].bitcast(FP8X4), scales=w3_scales[:], in_=staging_w3[:])
        for h, cols in enumerate(halves):
            join(2, planes[h][:, 2, :], cols)

        chunks = [slice(lo, hi) for lo, hi in zip(CHUNK_EDGES, CHUNK_EDGES[1:])]

        def inside(cols):
            h, start = divmod(cols.start, S // 2)
            return planes[h][:, :, start : start + cols.stop - cols.start]

        for first, last in MAX_RUNS:
            cols = slice(chunks[first].start, chunks[last].stop)
            join(3, inside(cols)[:, 3, :], cols)
        woven = []
        for c, cols in enumerate(chunks):
            woven.append(keep.tile([P, PACK * (cols.stop - cols.start)], BF16, name=f"woven{c}", align_bytes=64))
            target = woven[c][:].rearrange("p (r i t) -> p r t i", i=RUN, t=PACK)
            source = inside(cols).rearrange("p t (r i) -> p r t i", i=RUN)
            if c in VECTOR_WEAVES:
                nc.vector.tensor_copy(target, source)
            else:
                nc.scalar.copy(target, source)
        for c in FINISH_ORDER:
            width = chunks[c].stop - chunks[c].start
            z_codes = keep.tile([P, width], U32, name=f"z_codes{c}", align_bytes=64)
            z_scales = keep.tile([P, width], U8, name=f"z_scales{c}", align_bytes=64)
            nc.vector.quantize_mx(out=z_codes[:].bitcast(FP8X4), scales=z_scales[:], in_=woven[c][:])
            total = psum.tile([P, width], F32, name="total", tag=f"bank{FINAL_BANKS[c]}")
            nc.tensor.matmul_mx(
                out=total[:],
                lhsT=w3_codes[:].bitcast(FP8X4),
                lhsT_scale=w3_scales[:],
                rhs=z_codes[:].bitcast(FP8X4),
                rhs_scale=z_scales[:],
                start=True,
                stop=True,
            )
            leaving = keep.tile([P, width], F32, name=f"leaving{c}")
            if c in VECTOR_EMPTIES:
                nc.vector.tensor_copy(leaving[:], total[:])
            else:
                nc.scalar.copy(leaving[:], total[:])
            nc.sync.dma_start(out[:, chunks[c]], leaving[:])
